import numpy as np
import ml_dtypes


def mxq(x, axis, fmt="e4m3"):
    dtype, down = {"e4m3": (ml_dtypes.float8_e4m3fn, 7), "e5m2": (ml_dtypes.float8_e5m2, 14)}[fmt]
    v = np.moveaxis(np.asarray(x, np.float32).astype(ml_dtypes.bfloat16).astype(np.float64), axis, -1)
    blocks = v.reshape(v.shape[:-1] + (-1, 32))
    amax = np.abs(blocks).max(-1, keepdims=True)
    byte = np.maximum(np.where(amax > 0, np.frexp(amax)[1] - 1 + 127, 0) - down, 1)
    scale = np.exp2(byte - 127.0)
    codes = (blocks / scale).astype(np.float32).astype(dtype).astype(np.float64)
    return np.moveaxis((codes * scale).reshape(v.shape), -1, axis)


WIDE = False


def mx_kscale(k, group=512):
    if not WIDE:
        return np.ones(k)
    levels = np.array([10, -10, 5, -5, 0])
    if group != 512:
        return np.exp2(np.random.permutation(np.resize(levels, k // group))).repeat(group)
    if k % 512:
        return np.exp2(np.random.permutation(np.resize(levels, k // 32))).repeat(32)
    a = np.empty((k // 512, 16))
    for p in range(k // 512):
        a[p, :8] = np.random.permutation(np.resize(levels, 8))
        for g in range(8):
            far = levels[np.abs(levels - a[p, g]) >= 10]
            a[p, g + 8] = far[np.random.randint(len(far))]
    return np.exp2(a.ravel()).repeat(32)


def f64(x):
    return np.asarray(x).astype(np.float64)


def striped(idx):
    return np.tile(np.asarray(idx).reshape(-1, 16).T, (8, 1)).astype(np.uint16)


def unstriped(offs):
    return offs[:16].T.reshape(-1).astype(np.int64)


H, KV, D, NQ, N = 2, 2, 256, 512, 512


def setup_inputs():
    n = np.random.standard_normal
    s = mx_kscale(D, 0)[:, None]
    u = mx_kscale(N)
    t = np.random.uniform(0.5, 2.0, N) * u
    v = n((KV, N, 128))
    v[:, :, 127] = 1.0
    return {
        "qT": (n((H, D, NQ)) * s * (0.70 / np.sqrt(D))).astype(np.float32),
        "kT": (n((KV, D, N)) / s).astype(np.float32),
        "t": t.reshape(N, 1).astype(np.float32),
        "v": (v / t[:, None]).astype(np.float32),
        "sink": (N * np.random.uniform(0.1, 1.0, (H, NQ, 1))).astype(np.float32),
        "og": n((H, NQ, 128)).astype(np.float32),
    }


def reference(qT, kT, t, v, sink, og):
    a = mxq(f64(kT), 1, "e4m3").transpose(0, 2, 1) @ mxq(f64(qT), 1, "e4m3")
    p = np.exp(a)
    w = p * f64(t)
    y = mxq(w, 1, "e4m3").transpose(0, 2, 1) @ mxq(f64(v), 1, "e4m3")
    y = y / (y[:, :, 127:128] + f64(sink))
    y = y / (1.0 + np.exp(-f64(og)))
    return y

@@ -1,0 +1,237 @@
+import math
+from contextlib import ExitStack
+
+import concourse.mybir as mybir
+
+F32 = mybir.dt.float32
+BF16 = mybir.dt.bfloat16
+I32 = mybir.dt.int32
+U32 = mybir.dt.uint32
+U8 = mybir.dt.uint8
+FP8X4 = mybir.dt.float8_e4m3fn_x4
+ALU = mybir.AluOpType
+ACT = mybir.ActivationFunctionType
+
+H, D, NQ, N, E = 2, 256, 512, 512, 128
+P = 128
+ROWS = 64
+PACK = 4
+HALF = 256
+FLOPS = 2 * H * N * NQ * (D + E)
+
+
+def tile_rows_sink_gate_kernel(tc, qT, kT, t, v, sink, og, out):
+    nc = tc.nc
+    units = [(h, u) for u in range(2) for h in range(H)]
+
+    with ExitStack() as ctx:
+        sb = ctx.enter_context(tc.tile_pool(name="sb", bufs=1))
+        ps = ctx.enter_context(tc.psum_pool(name="ps", bufs=1))
+        ctx.enter_context(tc.manual_schedule())
+
+        def sbuf(name, shape, dtype):
+            return sb.tile(shape, dtype, name=name, align_bytes=64)
+
+        t_sb = sbuf("t_sb", [P, PACK], F32)
+        sink_sb = sbuf("sink_sb", [P, H * 2, 2], F32)
+        q_raw = [sbuf("q_raw%d" % u, [P, PACK, HALF], F32) for u in range(2)]
+        k_raw = [sbuf("k_raw%d" % u, [P, PACK, HALF], F32) for u in range(2)]
+        v_raw = sbuf("v_raw", [P, H, PACK, E], F32)
+        og_sb = [sbuf("og_sb%d" % h, [P, 2, 2 * E], F32) for h in range(H)]
+        q_g = [sbuf("q_g%d" % u, [P, HALF, PACK], BF16) for u in range(2)]
+        k_g = sbuf("k_g", [P, PACK, P, PACK], BF16)
+        v_g = sbuf("v_g", [P, H * E, PACK], BF16)
+        q_c = [sbuf("q_c%d" % u, [P, HALF], U32) for u in range(2)]
+        q_s = [sbuf("q_s%d" % u, [P, HALF], U8) for u in range(2)]
+        k_c = sbuf("k_c", [P, N], U32)
+        k_s = sbuf("k_s", [P, N], U8)
+        v_c = sbuf("v_c", [P, H * E], U32)
+        v_s = sbuf("v_s", [P, H * E], U8)
+        w_r = [sbuf("w_r%d" % i, [P, PACK, HALF], BF16) for i in range(4)]
+        w_g = [sbuf("w_g%d" % i, [P, HALF, PACK], BF16) for i in range(4)]
+        w_c = [sbuf("w_c%d" % i, [P, HALF], U32) for i in range(4)]
+        w_s = [sbuf("w_s%d" % i, [P, HALF], U8) for i in range(4)]
+        th = [sbuf("th%d" % i, [P, 2 * E], F32) for i in range(4)]
+        gate = [sbuf("gate%d" % i, [P, 2 * E], F32) for i in range(4)]
+        den = [sbuf("den%d" % i, [P, 2], F32) for i in range(4)]
+        rec = [sbuf("rec%d" % i, [P, 2], F32) for i in range(4)]
+        res = [sbuf("res%d" % i, [P, 2, E], F32) for i in range(4)]
+        expo = sbuf("expo", [P, PACK], I32)
+        mant = sbuf("mant", [P, PACK], I32)
+        sgn = sbuf("sgn", [P, PACK], I32)
+        ln_e = sbuf("ln_e", [P, PACK], F32)
+        ln_m = sbuf("ln_m", [P, PACK], F32)
+        ln_t = sbuf("ln_t", [P, PACK], F32)
+        one = sbuf("one", [P, 1], F32)
+        warm = sbuf("warm", [P, 1], F32)
+        warm2 = sbuf("warm2", [P, 1], F32)
+
+        score = [[ps.tile([P, HALF], F32, name="score%d_%d" % (h, b)) for b in range(3)] for h in range(H)]
+        ybank = [ps.tile([P, 2, E], F32, name="y%d" % b) for b in range(2)]
+
+        q_hbm = qT.rearrange("h (p j) n -> (h p) j n", j=PACK)
+        k_hbm = kT.rearrange("h (p j) n -> (h p) j n", j=PACK)
+
+        nc.sync.dma_start(out=t_sb[:], in_=t.rearrange("(p r) o -> p (r o)", r=PACK))
+        nc.sync.dma_start(out=q_raw[0][:], in_=q_hbm[:, :, 0:HALF])
+        nc.sync.dma_start(out=k_raw[0][:], in_=k_hbm[:, :, 0:HALF])
+        nc.sync.dma_start(out=k_raw[1][:], in_=k_hbm[:, :, HALF:N])
+        nc.sync.dma_start(out=v_raw[:].rearrange("p h r e -> p h (r e)"), in_=v.rearrange("h (p r) e -> p h (r e)", r=PACK))
+        nc.sync.dma_start(out=q_raw[1][:], in_=q_hbm[:, :, HALF:NQ])
+        nc.sync.dma_start(out=og_sb[0][:], in_=og[0].rearrange("(u p c) e -> p u (c e)", u=2, c=2))
+        nc.sync.dma_start(out=sink_sb[:], in_=sink.rearrange("h (u p c) o -> p (h u) (c o)", u=2, c=2))
+        nc.sync.dma_start(out=og_sb[1][:], in_=og[1].rearrange("(u p c) e -> p u (c e)", u=2, c=2))
+
+        nc.vector.memset(one[:], 1.0)
+        nc.scalar.activation(out=warm[:], in_=one[:], func=ACT.Ln)
+
+        t_bits = t_sb[:].bitcast(I32)
+        nc.vector.tensor_scalar(out=mant[:], in0=t_bits, scalar1=0x007FFFFF, scalar2=0x3F800000, op0=ALU.bitwise_and, op1=ALU.bitwise_or)
+        nc.vector.tensor_scalar(out=expo[:], in0=t_bits, scalar1=23, scalar2=255, op0=ALU.logical_shift_right, op1=ALU.bitwise_and)
+        nc.vector.tensor_scalar(out=sgn[:], in0=t_bits, scalar1=-0x80000000, scalar2=0x3F800000, op0=ALU.bitwise_and, op1=ALU.bitwise_or)
+        nc.scalar.activation(out=ln_m[:], in_=mant[:].bitcast(F32), func=ACT.Ln)
+        nc.scalar.activation(out=warm2[:], in_=one[:], func=ACT.Exp)
+        nc.vector.tensor_scalar(out=ln_e[:], in0=expo[:], scalar1=-127.0, scalar2=math.log(2.0), op0=ALU.add, op1=ALU.mult)
+        nc.vector.tensor_tensor(out=ln_t[:], in0=ln_e[:], in1=ln_m[:], op=ALU.add)
+
+        def quant(codes, scales, src):
+            nc.vector.quantize_mx(out=codes.bitcast(FP8X4), scales=scales, in_=src)
+
+        def q_copy(u):
+            nc.vector.tensor_copy(
+                out=q_g[u][:].rearrange("p (c a b) j -> p a j b c", c=2, b=2),
+                in_=q_raw[u][:].rearrange("p j (a b c) -> p a j b c", b=2, c=2))
+
+        def q_quant(u):
+            quant(q_c[u][:], q_s[u][:], q_g[u][:].rearrange("p n j -> p (n j)"))
+
+        def k_copy(u, s0, s1, copy):
+            copy(out=k_g[:, :, 64 * u + s0:64 * u + s1, :].rearrange("p r s j -> p s j r"),
+                 in_=k_raw[u][:, :, PACK * s0:PACK * s1].rearrange("p j (s r) -> p s j r", r=PACK))
+
+        def k_quant(r0, r1):
+            quant(k_c[:, P * r0:P * r1], k_s[:, P * r0:P * r1], k_g[:, r0:r1].rearrange("p r s j -> p (r s j)"))
+
+        def v_copy():
+            nc.vector.tensor_tensor(
+                out=v_g[:].rearrange("p (h e) r -> p h e r", h=H),
+                in0=v_raw[:].rearrange("p h r e -> p h e r"),
+                in1=sgn[:].bitcast(F32).unsqueeze(1).unsqueeze(1).to_broadcast([P, H, E, PACK]),
+                op=ALU.mult)
+
+        def scores(i, r):
+            h, u = units[i]
+            rows = slice(ROWS * h, ROWS * (h + 1))
+            bank = score[h][(PACK * u + r) % 3]
+            for c in range(2):
+                cols = slice(P * c, P * (c + 1))
+                keys = slice(P * r, P * (r + 1))
+                nc.tensor.matmul_mx(out=bank[:, cols], lhsT=k_c[rows, keys].bitcast(FP8X4), lhsT_scale=k_s[rows, keys],
+                                    rhs=q_c[u][rows, cols].bitcast(FP8X4), rhs_scale=q_s[u][rows, cols], start=True, stop=True)
+
+        def weights(i, r):
+            h, u = units[i]
+            bank = score[h][(PACK * u + r) % 3]
+            nc.scalar.activation(out=w_r[i][:, r, :], in_=bank[:], func=ACT.Exp, bias=ln_t[:, r:r + 1])
+
+        def w_copy(i):
+            nc.vector.tensor_copy(out=w_g[i][:].rearrange("p (a b) r -> p a r b", b=4),
+                                  in_=w_r[i][:].rearrange("p r (a b) -> p a r b", b=4))
+
+        def w_quant(i):
+            quant(w_c[i][:], w_s[i][:], w_g[i][:].rearrange("p n r -> p (n r)"))
+
+        def values(i):
+            h, u = units[i]
+            feats = slice(E * h, E * (h + 1))
+            for c in range(2):
+                cols = slice(P * c, P * (c + 1))
+                nc.tensor.matmul_mx(out=ybank[i % 2][:, c, :], lhsT=w_c[i][:, cols].bitcast(FP8X4), lhsT_scale=w_s[i][:, cols],
+                                    rhs=v_c[:, feats].bitcast(FP8X4), rhs_scale=v_s[:, feats], start=True, stop=True)
+
+        def tanh(i):
+            h, u = units[i]
+            nc.scalar.activation(out=th[i][:], in_=og_sb[h][:, u, :], func=ACT.Tanh, scale=0.5)
+
+        def gate_v(i):
+            nc.vector.tensor_scalar(out=gate[i][:], in0=th[i][:], scalar1=0.5, scalar2=0.5, op0=ALU.mult, op1=ALU.add)
+
+        def gate_s(i):
+            nc.scalar.activation(out=gate[i][:], in_=th[i][:], func=ACT.Copy, scale=0.5, bias=0.5)
+
+        def denom(i):
+            h, u = units[i]
+            nc.vector.tensor_tensor(out=den[i][:], in0=ybank[i % 2][:, :, E - 1], in1=sink_sb[:, 2 * h + u, :], op=ALU.add)
+
+        def recip(i):
+            nc.vector.reciprocal(out=rec[i][:], in_=den[i][:])
+
+        def finish(i):
+            h, u = units[i]
+            for c in range(2):
+                nc.vector.scalar_tensor_tensor(out=res[i][:, c, :], in0=ybank[i % 2][:, c, :], scalar=rec[i][:, c:c + 1],
+                                               in1=gate[i][:, E * c:E * (c + 1)], op0=ALU.mult, op1=ALU.mult)
+            nc.sync.dma_start(out=out[h, HALF * u:HALF * (u + 1), :].rearrange("(p c) e -> p c e", c=2), in_=res[i][:])
+
+        def ahead(i):
+            for r in range(3):
+                scores(i, r)
+
+        def unit(i):
+            weights(i, 0)
+            scores(i, 3)
+            for r in range(1, PACK):
+                weights(i, r)
+
+        q_copy(0)
+        q_quant(0)
+        k_copy(0, 0, 64, nc.vector.tensor_copy)
+        k_copy(1, 44, 64, nc.scalar.copy)
+        k_copy(1, 0, 44, nc.vector.tensor_copy)
+        k_quant(0, 1)
+        k_quant(1, 2)
+        k_quant(2, 4)
+        ahead(0)
+        ahead(1)
+        unit(0)
+        v_copy()
+        unit(1)
+        q_copy(1)
+        quant(v_c[:], v_s[:], v_g[:].rearrange("p n r -> p (n r)"))
+        q_quant(1)
+        w_copy(0)
+        ahead(2)
+        ahead(3)
+        tanh(0)
+        w_quant(0)
+        values(0)
+        unit(2)
+        w_copy(1)
+        gate_v(0)
+        denom(0)
+        w_quant(1)
+        values(1)
+        recip(0)
+        tanh(1)
+        unit(3)
+        denom(1)
+        finish(0)
+        w_copy(2)
+        recip(1)
+        w_quant(2)
+        values(2)
+        gate_v(1)
+        tanh(2)
+        gate_s(2)
+        tanh(3)
+        gate_s(3)
+        w_copy(3)
+        finish(1)
+        w_quant(3)
+        values(3)
+        denom(2)
+        recip(2)
+        denom(3)
+        finish(2)
+        recip(3)
+        finish(3)

@@ -16,13 +16,20 @@ H, D, NQ, N, E = 2, 256, 512, 512, 128
 P = 128
 ROWS = 64
 PACK = 4
-HALF = 256
 FLOPS = 2 * H * N * NQ * (D + E)
+QW = [128,128,256]
+Q0 = [0,128,256]
+KW = [128,384]
+K0 = [0,128]
+YB = [[0,1,0],[0,1,1]]
+YO = [[0,0,256],[128,128,256]]
+SB = [[[[0,0],[1,0],[2,0],[0,0]],[[1,0],[1,128],[2,0],[2,128]],[[0,0],[0,256],[1,0],[1,256]]],[[[0,0],[1,0],[2,0],[0,0]],[[1,0],[1,128],[2,0],[2,128]],[[0,0],[0,256],[1,0],[1,256]]]]
+WP = [1,1,0]
 
 
 def tile_rows_sink_gate_kernel(tc, qT, kT, t, v, sink, og, out):
     nc = tc.nc
-    units = [(h, u) for u in range(2) for h in range(H)]
+    nu = len(QW)
 
     with ExitStack() as ctx:
         sb = ctx.enter_context(tc.tile_pool(name="sb", bufs=1))
@@ -32,30 +39,46 @@ def tile_rows_sink_gate_kernel(tc, qT, kT, t, v, sink, og, out):
         def sbuf(name, shape, dtype):
             return sb.tile(shape, dtype, name=name, align_bytes=64)
 
+        def per_u(name, shape, dtype):
+            return [sbuf("%s%d" % (name, u), shape(QW[u]), dtype) for u in range(nu)]
+
+        def per_hu(name, shape, dtype):
+            tiles = [[], []]
+            for u in range(nu):
+                if WP[u]:
+                    both = sbuf("%s%d" % (name, u), shape(2 * QW[u]), dtype)
+                    tiles[0].append(both)
+                    tiles[1].append(both)
+                else:
+                    for h in range(H):
+                        tiles[h].append(sbuf("%s%d_%d" % (name, u, h), shape(QW[u]), dtype))
+            return tiles
+
         t_sb = sbuf("t_sb", [P, PACK], F32)
-        sink_sb = sbuf("sink_sb", [P, H * 2, 2], F32)
-        q_raw = [sbuf("q_raw%d" % u, [P, PACK, HALF], F32) for u in range(2)]
-        k_raw = [sbuf("k_raw%d" % u, [P, PACK, HALF], F32) for u in range(2)]
+        sink_sb = per_u("sink_sb", lambda w: [P, H, w // P], F32)
+        q_raw = per_u("q_raw", lambda w: [P, PACK, w], F32)
+        k_raw = [sbuf("k_raw%d" % u, [P, PACK, w], F32) for u, w in enumerate(KW)]
         v_raw = sbuf("v_raw", [P, H, PACK, E], F32)
-        og_sb = [sbuf("og_sb%d" % h, [P, 2, 2 * E], F32) for h in range(H)]
-        q_g = [sbuf("q_g%d" % u, [P, HALF, PACK], BF16) for u in range(2)]
+        v_r = sbuf("v_r", [P, H, PACK, E], BF16)
+        og_sb = per_u("og_sb", lambda w: [P, H, w], F32)
+        q_g = per_u("q_g", lambda w: [P, w, PACK], BF16)
         k_g = sbuf("k_g", [P, PACK, P, PACK], BF16)
-        v_g = sbuf("v_g", [P, H * E, PACK], BF16)
-        q_c = [sbuf("q_c%d" % u, [P, HALF], U32) for u in range(2)]
-        q_s = [sbuf("q_s%d" % u, [P, HALF], U8) for u in range(2)]
+        v_g = sbuf("v_g", [P, H, E, PACK], BF16)
+        q_c = per_u("q_c", lambda w: [P, w], U32)
+        q_s = per_u("q_s", lambda w: [P, w], U8)
         k_c = sbuf("k_c", [P, N], U32)
         k_s = sbuf("k_s", [P, N], U8)
         v_c = sbuf("v_c", [P, H * E], U32)
         v_s = sbuf("v_s", [P, H * E], U8)
-        w_r = [sbuf("w_r%d" % i, [P, PACK, HALF], BF16) for i in range(4)]
-        w_g = [sbuf("w_g%d" % i, [P, HALF, PACK], BF16) for i in range(4)]
-        w_c = [sbuf("w_c%d" % i, [P, HALF], U32) for i in range(4)]
-        w_s = [sbuf("w_s%d" % i, [P, HALF], U8) for i in range(4)]
-        th = [sbuf("th%d" % i, [P, 2 * E], F32) for i in range(4)]
-        gate = [sbuf("gate%d" % i, [P, 2 * E], F32) for i in range(4)]
-        den = [sbuf("den%d" % i, [P, 2], F32) for i in range(4)]
-        rec = [sbuf("rec%d" % i, [P, 2], F32) for i in range(4)]
-        res = [sbuf("res%d" % i, [P, 2, E], F32) for i in range(4)]
+        w_r = per_hu("w_r", lambda w: [P, PACK, w], BF16)
+        w_g = per_hu("w_g", lambda w: [P, w, PACK], BF16)
+        w_c = per_hu("w_c", lambda w: [P, w], U32)
+        w_s = per_hu("w_s", lambda w: [P, w], U8)
+        th = per_u("th", lambda w: [P, H * w], F32)
+        gate = per_u("gate", lambda w: [P, H * w], F32)
+        den = [per_u("den%d" % h, lambda w: [P, H * w // P], F32) for h in range(H)]
+        rec = [per_u("rec%d" % h, lambda w: [P, H * w // P], F32) for h in range(H)]
+        res = per_u("res", lambda w: [P, H * w], F32)
         expo = sbuf("expo", [P, PACK], I32)
         mant = sbuf("mant", [P, PACK], I32)
         sgn = sbuf("sgn", [P, PACK], I32)
@@ -66,172 +89,261 @@ def tile_rows_sink_gate_kernel(tc, qT, kT, t, v, sink, og, out):
         warm = sbuf("warm", [P, 1], F32)
         warm2 = sbuf("warm2", [P, 1], F32)
 
-        score = [[ps.tile([P, HALF], F32, name="score%d_%d" % (h, b)) for b in range(3)] for h in range(H)]
-        ybank = [ps.tile([P, 2, E], F32, name="y%d" % b) for b in range(2)]
+        score = [[ps.tile([P, 512], F32, name="score%d_%d" % (h, b)) for b in range(3)] for h in range(H)]
+        ybank = [ps.tile([P, 512], F32, name="y%d" % b) for b in range(2)]
 
         q_hbm = qT.rearrange("h (p j) n -> (h p) j n", j=PACK)
         k_hbm = kT.rearrange("h (p j) n -> (h p) j n", j=PACK)
-
-        nc.sync.dma_start(out=t_sb[:], in_=t.rearrange("(p r) o -> p (r o)", r=PACK))
-        nc.sync.dma_start(out=q_raw[0][:], in_=q_hbm[:, :, 0:HALF])
-        nc.sync.dma_start(out=k_raw[0][:], in_=k_hbm[:, :, 0:HALF])
-        nc.sync.dma_start(out=k_raw[1][:], in_=k_hbm[:, :, HALF:N])
-        nc.sync.dma_start(out=v_raw[:].rearrange("p h r e -> p h (r e)"), in_=v.rearrange("h (p r) e -> p h (r e)", r=PACK))
-        nc.sync.dma_start(out=q_raw[1][:], in_=q_hbm[:, :, HALF:NQ])
-        nc.sync.dma_start(out=og_sb[0][:], in_=og[0].rearrange("(u p c) e -> p u (c e)", u=2, c=2))
-        nc.sync.dma_start(out=sink_sb[:], in_=sink.rearrange("h (u p c) o -> p (h u) (c o)", u=2, c=2))
-        nc.sync.dma_start(out=og_sb[1][:], in_=og[1].rearrange("(u p c) e -> p u (c e)", u=2, c=2))
-
-        nc.vector.memset(one[:], 1.0)
-        nc.scalar.activation(out=warm[:], in_=one[:], func=ACT.Ln)
-
         t_bits = t_sb[:].bitcast(I32)
-        nc.vector.tensor_scalar(out=mant[:], in0=t_bits, scalar1=0x007FFFFF, scalar2=0x3F800000, op0=ALU.bitwise_and, op1=ALU.bitwise_or)
-        nc.vector.tensor_scalar(out=expo[:], in0=t_bits, scalar1=23, scalar2=255, op0=ALU.logical_shift_right, op1=ALU.bitwise_and)
-        nc.vector.tensor_scalar(out=sgn[:], in0=t_bits, scalar1=-0x80000000, scalar2=0x3F800000, op0=ALU.bitwise_and, op1=ALU.bitwise_or)
-        nc.scalar.activation(out=ln_m[:], in_=mant[:].bitcast(F32), func=ACT.Ln)
-        nc.scalar.activation(out=warm2[:], in_=one[:], func=ACT.Exp)
-        nc.vector.tensor_scalar(out=ln_e[:], in0=expo[:], scalar1=-127.0, scalar2=math.log(2.0), op0=ALU.add, op1=ALU.mult)
-        nc.vector.tensor_tensor(out=ln_t[:], in0=ln_e[:], in1=ln_m[:], op=ALU.add)
 
         def quant(codes, scales, src):
             nc.vector.quantize_mx(out=codes.bitcast(FP8X4), scales=scales, in_=src)
 
-        def q_copy(u):
-            nc.vector.tensor_copy(
-                out=q_g[u][:].rearrange("p (c a b) j -> p a j b c", c=2, b=2),
-                in_=q_raw[u][:].rearrange("p j (a b c) -> p a j b c", b=2, c=2))
+        def ld_q(u):
+            nc.sync.dma_start(out=q_raw[u][:], in_=q_hbm[:, :, Q0[u]:Q0[u] + QW[u]])
+
+        def ld_k(u):
+            nc.sync.dma_start(out=k_raw[u][:], in_=k_hbm[:, :, K0[u]:K0[u] + KW[u]])
+
+        def ld_og(u):
+            nc.sync.dma_start(out=og_sb[u][:], in_=og[:, Q0[u]:Q0[u] + QW[u], :].rearrange("h (p c) e -> p h (c e)", p=P))
+
+        def ld_sink(u):
+            with nc.allow_non_contiguous_dma(reason="one sink a query row"):
+                nc.sync.dma_start(out=sink_sb[u][:], in_=sink[:, Q0[u]:Q0[u] + QW[u], :].rearrange("h (p c) o -> p h (c o)", p=P))
+
+        def q_copy(u, copy):
+            if QW[u] == P:
+                copy(out=q_g[u][:].rearrange("p (a b) j -> p a j b", b=4), in_=q_raw[u][:].rearrange("p j (a b) -> p a j b", b=4))
+            else:
+                copy(out=q_g[u][:].rearrange("p (c a b) j -> p a j b c", c=2, b=2),
+                     in_=q_raw[u][:].rearrange("p j (a b c) -> p a j b c", b=2, c=2))
 
         def q_quant(u):
             quant(q_c[u][:], q_s[u][:], q_g[u][:].rearrange("p n j -> p (n j)"))
 
-        def k_copy(u, s0, s1, copy):
-            copy(out=k_g[:, :, 64 * u + s0:64 * u + s1, :].rearrange("p r s j -> p s j r"),
-                 in_=k_raw[u][:, :, PACK * s0:PACK * s1].rearrange("p j (s r) -> p s j r", r=PACK))
+        def k_copy(u, n0, n1, copy):
+            copy(out=k_g[:, :, (K0[u] + n0) // PACK:(K0[u] + n1) // PACK, :].rearrange("p r s j -> p s j r"),
+                 in_=k_raw[u][:, :, n0:n1].rearrange("p j (s r) -> p s j r", r=PACK))
 
         def k_quant(r0, r1):
             quant(k_c[:, P * r0:P * r1], k_s[:, P * r0:P * r1], k_g[:, r0:r1].rearrange("p r s j -> p (r s j)"))
 
-        def v_copy():
+        def v_sign(r):
+            nc.scalar.activation(out=v_r[:, :, r, :], in_=v_raw[:, :, r, :], func=ACT.Copy, scale=sgn[:, r:r + 1].bitcast(F32))
+
+        def v_move(h):
+            nc.vector.tensor_copy(out=v_g[:, h].rearrange("p (a b) r -> p a r b", b=4), in_=v_r[:, h].rearrange("p r (a b) -> p a r b", b=4))
+
+        def v_copy(h):
             nc.vector.tensor_tensor(
-                out=v_g[:].rearrange("p (h e) r -> p h e r", h=H),
-                in0=v_raw[:].rearrange("p h r e -> p h e r"),
-                in1=sgn[:].bitcast(F32).unsqueeze(1).unsqueeze(1).to_broadcast([P, H, E, PACK]),
+                out=v_g[:, h].rearrange("p (a b) r -> p a r b", b=4),
+                in0=v_raw[:, h].rearrange("p r (a b) -> p a r b", b=4),
+                in1=sgn[:].bitcast(F32).unsqueeze(1).unsqueeze(3).to_broadcast([P, E // 4, PACK, 4]),
                 op=ALU.mult)
 
-        def scores(i, r):
-            h, u = units[i]
+        def v_quant(h0, h1):
+            quant(v_c[:, E * h0:E * h1], v_s[:, E * h0:E * h1], v_g[:, h0:h1].rearrange("p h e r -> p (h e r)"))
+
+        def wcol(h, u):
+            return h * QW[u] if WP[u] else 0
+
+        def scores(h, u, r):
             rows = slice(ROWS * h, ROWS * (h + 1))
-            bank = score[h][(PACK * u + r) % 3]
-            for c in range(2):
+            b, c0 = SB[h][u][r]
+            keys = slice(P * r, P * (r + 1))
+            for c in range(QW[u] // P):
                 cols = slice(P * c, P * (c + 1))
-                keys = slice(P * r, P * (r + 1))
-                nc.tensor.matmul_mx(out=bank[:, cols], lhsT=k_c[rows, keys].bitcast(FP8X4), lhsT_scale=k_s[rows, keys],
+                nc.tensor.matmul_mx(out=score[h][b][:, c0 + P * c:c0 + P * (c + 1)], lhsT=k_c[rows, keys].bitcast(FP8X4), lhsT_scale=k_s[rows, keys],
                                     rhs=q_c[u][rows, cols].bitcast(FP8X4), rhs_scale=q_s[u][rows, cols], start=True, stop=True)
 
-        def weights(i, r):
-            h, u = units[i]
-            bank = score[h][(PACK * u + r) % 3]
-            nc.scalar.activation(out=w_r[i][:, r, :], in_=bank[:], func=ACT.Exp, bias=ln_t[:, r:r + 1])
+        def weights(h, u, r):
+            b, c0 = SB[h][u][r]
+            w0 = wcol(h, u)
+            nc.scalar.activation(out=w_r[h][u][:, r, w0:w0 + QW[u]], in_=score[h][b][:, c0:c0 + QW[u]], func=ACT.Exp, bias=ln_t[:, r:r + 1])
 
-        def w_copy(i):
-            nc.vector.tensor_copy(out=w_g[i][:].rearrange("p (a b) r -> p a r b", b=4),
-                                  in_=w_r[i][:].rearrange("p r (a b) -> p a r b", b=4))
+        def w_copy(h, u, n0, n1, copy):
+            copy(out=w_g[h][u][:, n0:n1].rearrange("p (a b) r -> p a r b", b=4),
+                 in_=w_r[h][u][:, :, n0:n1].rearrange("p r (a b) -> p a r b", b=4))
 
-        def w_quant(i):
-            quant(w_c[i][:], w_s[i][:], w_g[i][:].rearrange("p n r -> p (n r)"))
+        def w_quant(h, u):
+            quant(w_c[h][u][:], w_s[h][u][:], w_g[h][u][:].rearrange("p n r -> p (n r)"))
 
-        def values(i):
-            h, u = units[i]
+        def values(h, u):
             feats = slice(E * h, E * (h + 1))
-            for c in range(2):
-                cols = slice(P * c, P * (c + 1))
-                nc.tensor.matmul_mx(out=ybank[i % 2][:, c, :], lhsT=w_c[i][:, cols].bitcast(FP8X4), lhsT_scale=w_s[i][:, cols],
+            for c in range(QW[u] // P):
+                cols = slice(wcol(h, u) + P * c, wcol(h, u) + P * (c + 1))
+                y0 = YO[h][u] + E * c
+                nc.tensor.matmul_mx(out=ybank[YB[h][u]][:, y0:y0 + E], lhsT=w_c[h][u][:, cols].bitcast(FP8X4), lhsT_scale=w_s[h][u][:, cols],
                                     rhs=v_c[:, feats].bitcast(FP8X4), rhs_scale=v_s[:, feats], start=True, stop=True)
 
-        def tanh(i):
-            h, u = units[i]
-            nc.scalar.activation(out=th[i][:], in_=og_sb[h][:, u, :], func=ACT.Tanh, scale=0.5)
+        def span(h0, h1, u):
+            return slice(h0 * QW[u], h1 * QW[u])
 
-        def gate_v(i):
-            nc.vector.tensor_scalar(out=gate[i][:], in0=th[i][:], scalar1=0.5, scalar2=0.5, op0=ALU.mult, op1=ALU.add)
+        def y_of(h0, h1, u):
+            return ybank[YB[h0][u]][:, YO[h0][u]:YO[h0][u] + (h1 - h0) * QW[u]]
 
-        def gate_s(i):
-            nc.scalar.activation(out=gate[i][:], in_=th[i][:], func=ACT.Copy, scale=0.5, bias=0.5)
+        def tanh(h0, h1, u):
+            nc.scalar.activation(out=th[u][:, span(h0, h1, u)], in_=og_sb[u][:, h0:h1].rearrange("p h n -> p (h n)"), func=ACT.Tanh, scale=0.5)
 
-        def denom(i):
-            h, u = units[i]
-            nc.vector.tensor_tensor(out=den[i][:], in0=ybank[i % 2][:, :, E - 1], in1=sink_sb[:, 2 * h + u, :], op=ALU.add)
+        def gate_v(h0, h1, u):
+            nc.vector.tensor_scalar(out=gate[u][:, span(h0, h1, u)], in0=th[u][:, span(h0, h1, u)], scalar1=1.0, scalar2=None, op0=ALU.add)
 
-        def recip(i):
-            nc.vector.reciprocal(out=rec[i][:], in_=den[i][:])
+        def gate_s(h0, h1, u):
+            nc.scalar.activation(out=gate[u][:, span(h0, h1, u)], in_=th[u][:, span(h0, h1, u)], func=ACT.Copy, bias=1.0)
 
-        def finish(i):
-            h, u = units[i]
-            for c in range(2):
-                nc.vector.scalar_tensor_tensor(out=res[i][:, c, :], in0=ybank[i % 2][:, c, :], scalar=rec[i][:, c:c + 1],
-                                               in1=gate[i][:, E * c:E * (c + 1)], op0=ALU.mult, op1=ALU.mult)
-            nc.sync.dma_start(out=out[h, HALF * u:HALF * (u + 1), :].rearrange("(p c) e -> p c e", c=2), in_=res[i][:])
+        def denom(h0, h1, u):
+            nt = (h1 - h0) * QW[u] // P
+            nc.vector.scalar_tensor_tensor(out=den[h0][u][:, 0:nt], in0=y_of(h0, h1, u).rearrange("p (c e) -> p c e", e=E)[:, :, E - 1], scalar=2.0,
+                                           in1=sink_sb[u][:, h0:h1].rearrange("p h c -> p (h c)"), op0=ALU.mult, op1=ALU.add)
 
-        def ahead(i):
-            for r in range(3):
-                scores(i, r)
+        def recip(h0, h1, u):
+            nt = (h1 - h0) * QW[u] // P
+            nc.vector.reciprocal(out=rec[h0][u][:, 0:nt], in_=den[h0][u][:, 0:nt])
 
-        def unit(i):
-            weights(i, 0)
-            scores(i, 3)
-            for r in range(1, PACK):
-                weights(i, r)
+        def gated(h0, h1, u):
+            nc.vector.scalar_tensor_tensor(out=gate[u][:, span(h0, h1, u)], in0=th[u][:, span(h0, h1, u)], scalar=1.0,
+                                           in1=y_of(h0, h1, u), op0=ALU.add, op1=ALU.mult)
 
-        q_copy(0)
+        def fin_v(h0, h1, u, c):
+            g0 = h0 * QW[u] + E * c
+            nc.vector.scalar_tensor_tensor(out=res[u][:, g0:g0 + E], in0=y_of(h0, h1, u)[:, E * c:E * (c + 1)], scalar=rec[h0][u][:, c:c + 1],
+                                           in1=gate[u][:, g0:g0 + E], op0=ALU.mult, op1=ALU.mult)
+
+        def fin_s(h0, h1, u, c):
+            g0 = h0 * QW[u] + E * c
+            nc.scalar.activation(out=res[u][:, g0:g0 + E], in_=gate[u][:, g0:g0 + E], func=ACT.Copy, scale=rec[h0][u][:, c:c + 1])
+
+        def store(h0, h1, u, eng):
+            eng.dma_start(out=out[h0:h1, Q0[u]:Q0[u] + QW[u], :].rearrange("h (p c) e -> p h (c e)", p=P),
+                          in_=res[u][:, span(h0, h1, u)].rearrange("p (h n) -> p h n", h=h1 - h0))
+
+        nc.vector.memset(one[:], 1.0)
+        nc.scalar.dma_start(out=t_sb[:], in_=t.rearrange("(p r) o -> p (r o)", r=PACK))
+        nc.vector.tensor_scalar(out=mant[:], in0=t_bits, scalar1=0x007FFFFF, scalar2=0x3F800000, op0=ALU.bitwise_and, op1=ALU.bitwise_or)
+        nc.scalar.activation(out=warm[:], in_=one[:], func=ACT.Ln)
+        nc.vector.tensor_scalar(out=expo[:], in0=t_bits, scalar1=23, scalar2=255, op0=ALU.logical_shift_right, op1=ALU.bitwise_and)
+        nc.vector.tensor_scalar(out=sgn[:], in0=t_bits, scalar1=-0x80000000, scalar2=0x3F000000, op0=ALU.bitwise_and, op1=ALU.bitwise_or)
+        nc.scalar.activation(out=ln_m[:], in_=mant[:].bitcast(F32), func=ACT.Ln)
+        nc.scalar.activation(out=warm2[:], in_=one[:], func=ACT.Exp)
+        ld_k(1)
+        nc.vector.tensor_scalar(out=ln_e[:], in0=expo[:], scalar1=-127.0, scalar2=math.log(2.0), op0=ALU.add, op1=ALU.mult)
+        nc.vector.tensor_tensor(out=ln_t[:], in0=ln_e[:], in1=ln_m[:], op=ALU.add)
+        k_copy(1, 0, 288, nc.vector.tensor_copy)
+        ld_q(0)
+        q_copy(0, nc.vector.tensor_copy)
+        ld_k(0)
+        k_copy(0, 0, 96, nc.vector.tensor_copy)
         q_quant(0)
-        k_copy(0, 0, 64, nc.vector.tensor_copy)
-        k_copy(1, 44, 64, nc.scalar.copy)
-        k_copy(1, 0, 44, nc.vector.tensor_copy)
+        k_copy(1, 288, 384, nc.scalar.copy)
+        k_copy(0, 96, 128, nc.scalar.copy)
         k_quant(0, 1)
+        scores(1, 0, 0)
+        weights(1, 0, 0)
         k_quant(1, 2)
+        scores(1, 0, 1)
+        weights(1, 0, 1)
+        ld_q(1)
+        q_copy(1, nc.vector.tensor_copy)
         k_quant(2, 4)
-        ahead(0)
-        ahead(1)
-        unit(0)
-        v_copy()
-        unit(1)
-        q_copy(1)
-        quant(v_c[:], v_s[:], v_g[:].rearrange("p n r -> p (n r)"))
+        scores(0, 0, 0)
+        weights(0, 0, 0)
         q_quant(1)
-        w_copy(0)
-        ahead(2)
-        ahead(3)
-        tanh(0)
-        w_quant(0)
-        values(0)
-        unit(2)
-        w_copy(1)
-        gate_v(0)
-        denom(0)
-        w_quant(1)
-        values(1)
-        recip(0)
-        tanh(1)
-        unit(3)
-        denom(1)
-        finish(0)
-        w_copy(2)
-        recip(1)
-        w_quant(2)
-        values(2)
-        gate_v(1)
-        tanh(2)
-        gate_s(2)
-        tanh(3)
-        gate_s(3)
-        w_copy(3)
-        finish(1)
-        w_quant(3)
-        values(3)
-        denom(2)
-        recip(2)
-        denom(3)
-        finish(2)
-        recip(3)
-        finish(3)
+        scores(0, 0, 1)
+        ld_q(2)
+        scores(0, 0, 2)
+        scores(1, 0, 2)
+        scores(1, 1, 1)
+        scores(1, 1, 0)
+        nc.sync.dma_start(out=v_raw[:].rearrange("p h r e -> p h (r e)"), in_=v.rearrange("h (p r) e -> p h (r e)", r=PACK))
+        weights(0, 0, 1)
+        weights(0, 0, 2)
+        weights(1, 0, 2)
+        scores(1, 0, 3)
+        scores(0, 0, 3)
+        scores(0, 1, 0)
+        weights(1, 1, 1)
+        scores(0, 1, 1)
+        ld_sink(2)
+        scores(0, 1, 3)
+        ld_sink(0)
+        ld_sink(1)
+        ld_og(1)
+        q_copy(2, nc.vector.tensor_copy)
+        scores(1, 1, 2)
+        q_quant(2)
+        weights(1, 0, 3)
+        v_copy(1)
+        weights(0, 0, 3)
+        weights(0, 1, 0)
+        scores(0, 1, 2)
+        v_copy(0)
+        weights(1, 1, 0)
+        weights(0, 1, 3)
+        w_copy(1, 0, 0, 256, nc.vector.tensor_copy)
+        weights(0, 1, 1)
+        weights(0, 1, 2)
+        scores(1, 1, 3)
+        scores(1, 2, 0)
+        weights(1, 1, 3)
+        weights(1, 1, 2)
+        v_quant(0, 2)
+        w_quant(1, 0)
+        w_copy(1, 1, 0, 256, nc.vector.tensor_copy)
+        scores(1, 2, 1)
+        weights(1, 2, 1)
+        scores(1, 2, 3)
+        scores(1, 2, 2)
+        weights(1, 2, 3)
+        weights(1, 2, 2)
+        scores(0, 2, 3)
+        weights(1, 2, 0)
+        scores(0, 2, 1)
+        scores(0, 2, 0)
+        scores(0, 2, 2)
+        weights(0, 2, 0)
+        ld_og(0)
+        values(0, 0)
+        weights(0, 2, 1)
+        w_copy(1, 2, 0, 256, nc.vector.tensor_copy)
+        weights(0, 2, 3)
+        weights(0, 2, 2)
+        values(1, 0)
+        denom(0, 2, 0)
+        w_quant(1, 1)
+        values(1, 1)
+        tanh(0, 2, 0)
+        values(0, 1)
+        w_quant(1, 2)
+        w_copy(0, 2, 0, 160, nc.vector.tensor_copy)
+        gated(0, 2, 0)
+        w_copy(0, 2, 160, 256, nc.scalar.copy)
+        w_quant(0, 2)
+        values(1, 2)
+        ld_og(2)
+        tanh(1, 2, 2)
+        tanh(0, 2, 1)
+        tanh(0, 1, 2)
+        recip(0, 2, 0)
+        fin_s(0, 2, 0, 0)
+        denom(1, 2, 2)
+        gated(1, 2, 2)
+        recip(1, 2, 2)
+        denom(0, 2, 1)
+        gated(0, 2, 1)
+        recip(0, 2, 1)
+        fin_s(0, 2, 0, 1)
+        values(0, 2)
+        denom(0, 1, 2)
+        fin_s(1, 2, 2, 1)
+        fin_s(1, 2, 2, 0)
+        fin_s(0, 2, 1, 0)
+        store(0, 2, 0, nc.sync)
+        gate_v(0, 1, 2)
+        recip(0, 1, 2)
+        fin_v(0, 1, 2, 1)
+        store(1, 2, 2, nc.sync)
+        fin_v(0, 1, 2, 0)
+        fin_s(0, 2, 1, 1)
+        store(0, 2, 1, nc.scalar)
+        store(0, 1, 2, nc.sync)

@@ -17,14 +17,15 @@ P = 128
 ROWS = 64
 PACK = 4
 FLOPS = 2 * H * N * NQ * (D + E)
-QW = [128,128,256]
-Q0 = [0,128,256]
-KW = [128,384]
-K0 = [0,128]
-YB = [[0,1,0],[0,1,1]]
-YO = [[0,0,256],[128,128,256]]
-SB = [[[[0,0],[1,0],[2,0],[0,0]],[[1,0],[1,128],[2,0],[2,128]],[[0,0],[0,256],[1,0],[1,256]]],[[[0,0],[1,0],[2,0],[0,0]],[[1,0],[1,128],[2,0],[2,128]],[[0,0],[0,256],[1,0],[1,256]]]]
-WP = [1,1,0]
+QW = [128,256,128]
+Q0 = [0,128,384]
+KW = [512]
+K0 = [0]
+YB = [[0,0,1],[0,1,1]]
+YO = [[0,256,256],[128,0,384]]
+SB = [[[[0,0],[1,0],[1,128],[2,0]],[[0,0],[0,256],[1,0],[1,256]],[[2,0],[2,128],[2,256],[2,384]]],[[[0,0],[1,0],[1,128],[2,0]],[[0,0],[0,256],[1,0],[1,256]],[[2,0],[2,128],[2,256],[2,384]]]]
+WP = [1,0,1]
+QL = [[0],[1],[2]]
 
 
 def tile_rows_sink_gate_kernel(tc, qT, kT, t, v, sink, og, out):
@@ -55,12 +56,14 @@ def tile_rows_sink_gate_kernel(tc, qT, kT, t, v, sink, og, out):
             return tiles
 
         t_sb = sbuf("t_sb", [P, PACK], F32)
-        sink_sb = per_u("sink_sb", lambda w: [P, H, w // P], F32)
-        q_raw = per_u("q_raw", lambda w: [P, PACK, w], F32)
+        sink_in = sbuf("sink_in", [P, 32], F32)
+        sink_t = sbuf("sink_t", [P, 32], F32)
+        q_grp = {g[0]: sbuf("q_raw%d" % g[0], [P, PACK, sum(QW[u] for u in g)], F32) for g in QL}
+        q_raw = [q_grp[g[0]][:, :, Q0[u] - Q0[g[0]]:Q0[u] - Q0[g[0]] + QW[u]] for g in QL for u in g]
         k_raw = [sbuf("k_raw%d" % u, [P, PACK, w], F32) for u, w in enumerate(KW)]
         v_raw = sbuf("v_raw", [P, H, PACK, E], F32)
         v_r = sbuf("v_r", [P, H, PACK, E], BF16)
-        og_sb = per_u("og_sb", lambda w: [P, H, w], F32)
+        og_sb = sbuf("og_sb", [P, H, NQ], F32)
         q_g = per_u("q_g", lambda w: [P, w, PACK], BF16)
         k_g = sbuf("k_g", [P, PACK, P, PACK], BF16)
         v_g = sbuf("v_g", [P, H, E, PACK], BF16)
@@ -99,28 +102,28 @@ def tile_rows_sink_gate_kernel(tc, qT, kT, t, v, sink, og, out):
         def quant(codes, scales, src):
             nc.vector.quantize_mx(out=codes.bitcast(FP8X4), scales=scales, in_=src)
 
+        def quant_cols(codes, scales, src):
+            w = codes.shape[1]
+            for n0, n1 in ([(0, 256), (256, 384)] if w == 384 else [(0, w)]):
+                quant(codes[:, n0:n1], scales[:, n0:n1], src[:, n0:n1].rearrange("p n j -> p (n j)"))
+
         def ld_q(u):
-            nc.sync.dma_start(out=q_raw[u][:], in_=q_hbm[:, :, Q0[u]:Q0[u] + QW[u]])
+            nc.sync.dma_start(out=q_grp[u][:], in_=q_hbm[:, :, Q0[u]:Q0[u] + q_grp[u].shape[2]])
 
         def ld_k(u):
             nc.sync.dma_start(out=k_raw[u][:], in_=k_hbm[:, :, K0[u]:K0[u] + KW[u]])
 
-        def ld_og(u):
-            nc.sync.dma_start(out=og_sb[u][:], in_=og[:, Q0[u]:Q0[u] + QW[u], :].rearrange("h (p c) e -> p h (c e)", p=P))
+        def ld_og(h):
+            nc.sync.dma_start(out=og_sb[:, h].rearrange("p (c e) -> p c e", e=E), in_=og[h].rearrange("(c p) e -> p c e", p=P))
 
-        def ld_sink(u):
-            with nc.allow_non_contiguous_dma(reason="one sink a query row"):
-                nc.sync.dma_start(out=sink_sb[u][:], in_=sink[:, Q0[u]:Q0[u] + QW[u], :].rearrange("h (p c) o -> p h (c o)", p=P))
+        def ld_sk(a):
+            nc.sync.dma_start(out=sink_in[32 * a:32 * a + 8, :], in_=sink.rearrange("h (c a j) o -> a (h c) (j o)", a=4, j=32)[a])
 
         def q_copy(u, copy):
-            if QW[u] == P:
-                copy(out=q_g[u][:].rearrange("p (a b) j -> p a j b", b=4), in_=q_raw[u][:].rearrange("p j (a b) -> p a j b", b=4))
-            else:
-                copy(out=q_g[u][:].rearrange("p (c a b) j -> p a j b c", c=2, b=2),
-                     in_=q_raw[u][:].rearrange("p j (a b c) -> p a j b c", b=2, c=2))
+            copy(out=q_g[u][:].rearrange("p (a b) j -> p a j b", b=4), in_=q_raw[u].rearrange("p j (a b) -> p a j b", b=4))
 
         def q_quant(u):
-            quant(q_c[u][:], q_s[u][:], q_g[u][:].rearrange("p n j -> p (n j)"))
+            quant_cols(q_c[u], q_s[u], q_g[u])
 
         def k_copy(u, n0, n1, copy):
             copy(out=k_g[:, :, (K0[u] + n0) // PACK:(K0[u] + n1) // PACK, :].rearrange("p r s j -> p s j r"),
@@ -167,7 +170,7 @@ def tile_rows_sink_gate_kernel(tc, qT, kT, t, v, sink, og, out):
                  in_=w_r[h][u][:, :, n0:n1].rearrange("p r (a b) -> p a r b", b=4))
 
         def w_quant(h, u):
-            quant(w_c[h][u][:], w_s[h][u][:], w_g[h][u][:].rearrange("p n r -> p (n r)"))
+            quant_cols(w_c[h][u], w_s[h][u], w_g[h][u])
 
         def values(h, u):
             feats = slice(E * h, E * (h + 1))
@@ -184,7 +187,7 @@ def tile_rows_sink_gate_kernel(tc, qT, kT, t, v, sink, og, out):
             return ybank[YB[h0][u]][:, YO[h0][u]:YO[h0][u] + (h1 - h0) * QW[u]]
 
         def tanh(h0, h1, u):
-            nc.scalar.activation(out=th[u][:, span(h0, h1, u)], in_=og_sb[u][:, h0:h1].rearrange("p h n -> p (h n)"), func=ACT.Tanh, scale=0.5)
+            nc.scalar.activation(out=th[u][:, span(h0, h1, u)].rearrange("p (h n) -> p h n", h=h1 - h0), in_=og_sb[:, h0:h1, Q0[u]:Q0[u] + QW[u]], func=ACT.Tanh, scale=0.5)
 
         def gate_v(h0, h1, u):
             nc.vector.tensor_scalar(out=gate[u][:, span(h0, h1, u)], in0=th[u][:, span(h0, h1, u)], scalar1=1.0, scalar2=None, op0=ALU.add)
@@ -194,8 +197,10 @@ def tile_rows_sink_gate_kernel(tc, qT, kT, t, v, sink, og, out):
 
         def denom(h0, h1, u):
             nt = (h1 - h0) * QW[u] // P
-            nc.vector.scalar_tensor_tensor(out=den[h0][u][:, 0:nt], in0=y_of(h0, h1, u).rearrange("p (c e) -> p c e", e=E)[:, :, E - 1], scalar=2.0,
-                                           in1=sink_sb[u][:, h0:h1].rearrange("p h c -> p (h c)"), op0=ALU.mult, op1=ALU.add)
+            c0 = Q0[u] // P
+            nc.vector.scalar_tensor_tensor(out=den[h0][u][:, 0:nt].rearrange("p (h c) -> p h c", h=h1 - h0),
+                                           in0=y_of(h0, h1, u).rearrange("p (h c e) -> p h c e", h=h1 - h0, e=E)[:, :, :, E - 1], scalar=2.0,
+                                           in1=sink_t[:, 0:8].rearrange("p (h c) -> p h c", h=H)[:, h0:h1, c0:c0 + QW[u] // P], op0=ALU.mult, op1=ALU.add)
 
         def recip(h0, h1, u):
             nt = (h1 - h0) * QW[u] // P
@@ -215,135 +220,139 @@ def tile_rows_sink_gate_kernel(tc, qT, kT, t, v, sink, og, out):
             nc.scalar.activation(out=res[u][:, g0:g0 + E], in_=gate[u][:, g0:g0 + E], func=ACT.Copy, scale=rec[h0][u][:, c:c + 1])
 
         def store(h0, h1, u, eng):
-            eng.dma_start(out=out[h0:h1, Q0[u]:Q0[u] + QW[u], :].rearrange("h (p c) e -> p h (c e)", p=P),
-                          in_=res[u][:, span(h0, h1, u)].rearrange("p (h n) -> p h n", h=h1 - h0))
+            rows = slice(Q0[u], Q0[u] + QW[u])
+            if QW[u] == P:
+                eng.dma_start(out=out[h0:h1, rows, :].rearrange("h p e -> p h e"), in_=res[u][:, span(h0, h1, u)].rearrange("p (h e) -> p h e", e=E))
+            else:
+                for h in range(h0, h1):
+                    eng.dma_start(out=out[h, rows, :].rearrange("(c p) e -> p c e", p=P), in_=res[u][:, span(h, h + 1, u)].rearrange("p (c e) -> p c e", e=E))
 
         nc.vector.memset(one[:], 1.0)
+        nc.vector.memset(sink_in[:], 0.0)
         nc.scalar.dma_start(out=t_sb[:], in_=t.rearrange("(p r) o -> p (r o)", r=PACK))
-        nc.vector.tensor_scalar(out=mant[:], in0=t_bits, scalar1=0x007FFFFF, scalar2=0x3F800000, op0=ALU.bitwise_and, op1=ALU.bitwise_or)
+        ld_k(0)
+        ld_q(0)
+        ld_q(1)
+        nc.sync.dma_start(out=v_raw[:].rearrange("p h r e -> p h (r e)"), in_=v.rearrange("h (p r) e -> p h (r e)", r=PACK))
+        ld_q(2)
+        ld_og(0)
+        ld_og(1)
+        ld_sk(0)
+        ld_sk(1)
+        ld_sk(2)
+        ld_sk(3)
         nc.scalar.activation(out=warm[:], in_=one[:], func=ACT.Ln)
+        nc.vector.tensor_scalar(out=mant[:], in0=t_bits, scalar1=0x007FFFFF, scalar2=0x3F800000, op0=ALU.bitwise_and, op1=ALU.bitwise_or)
         nc.vector.tensor_scalar(out=expo[:], in0=t_bits, scalar1=23, scalar2=255, op0=ALU.logical_shift_right, op1=ALU.bitwise_and)
         nc.vector.tensor_scalar(out=sgn[:], in0=t_bits, scalar1=-0x80000000, scalar2=0x3F000000, op0=ALU.bitwise_and, op1=ALU.bitwise_or)
         nc.scalar.activation(out=ln_m[:], in_=mant[:].bitcast(F32), func=ACT.Ln)
         nc.scalar.activation(out=warm2[:], in_=one[:], func=ACT.Exp)
-        ld_k(1)
         nc.vector.tensor_scalar(out=ln_e[:], in0=expo[:], scalar1=-127.0, scalar2=math.log(2.0), op0=ALU.add, op1=ALU.mult)
         nc.vector.tensor_tensor(out=ln_t[:], in0=ln_e[:], in1=ln_m[:], op=ALU.add)
-        k_copy(1, 0, 288, nc.vector.tensor_copy)
-        ld_q(0)
+        k_copy(0, 384, 512, nc.scalar.copy)
+        k_copy(0, 0, 384, nc.vector.tensor_copy)
         q_copy(0, nc.vector.tensor_copy)
-        ld_k(0)
-        k_copy(0, 0, 96, nc.vector.tensor_copy)
-        q_quant(0)
-        k_copy(1, 288, 384, nc.scalar.copy)
-        k_copy(0, 96, 128, nc.scalar.copy)
         k_quant(0, 1)
-        scores(1, 0, 0)
-        weights(1, 0, 0)
+        q_quant(0)
         k_quant(1, 2)
-        scores(1, 0, 1)
-        weights(1, 0, 1)
-        ld_q(1)
+        k_quant(2, 3)
         q_copy(1, nc.vector.tensor_copy)
-        k_quant(2, 4)
-        scores(0, 0, 0)
-        weights(0, 0, 0)
+        k_quant(3, 4)
         q_quant(1)
+        scores(0, 0, 0)
+        scores(1, 0, 0)
         scores(0, 0, 1)
-        ld_q(2)
+        scores(1, 0, 1)
         scores(0, 0, 2)
         scores(1, 0, 2)
-        scores(1, 1, 1)
-        scores(1, 1, 0)
-        nc.sync.dma_start(out=v_raw[:].rearrange("p h r e -> p h (r e)"), in_=v.rearrange("h (p r) e -> p h (r e)", r=PACK))
+        weights(0, 0, 0)
+        weights(1, 0, 0)
         weights(0, 0, 1)
         weights(0, 0, 2)
+        weights(1, 0, 1)
         weights(1, 0, 2)
-        scores(1, 0, 3)
         scores(0, 0, 3)
-        scores(0, 1, 0)
-        weights(1, 1, 1)
-        scores(0, 1, 1)
-        ld_sink(2)
-        scores(0, 1, 3)
-        ld_sink(0)
-        ld_sink(1)
-        ld_og(1)
-        q_copy(2, nc.vector.tensor_copy)
+        scores(1, 0, 3)
+        scores(1, 1, 0)
+        scores(1, 1, 1)
         scores(1, 1, 2)
-        q_quant(2)
-        weights(1, 0, 3)
-        v_copy(1)
+        scores(1, 1, 3)
         weights(0, 0, 3)
-        weights(0, 1, 0)
+        weights(1, 0, 3)
+        scores(0, 1, 0)
+        scores(0, 1, 1)
         scores(0, 1, 2)
+        scores(0, 1, 3)
         v_copy(0)
-        weights(1, 1, 0)
-        weights(0, 1, 3)
+        v_copy(1)
+        q_copy(2, nc.vector.tensor_copy)
         w_copy(1, 0, 0, 256, nc.vector.tensor_copy)
+        q_quant(2)
+        v_quant(0, 1)
+        v_quant(1, 2)
+        w_quant(1, 0)
+        weights(1, 1, 0)
+        weights(1, 1, 1)
+        weights(1, 1, 2)
+        weights(1, 1, 3)
+        weights(0, 1, 0)
         weights(0, 1, 1)
         weights(0, 1, 2)
-        scores(1, 1, 3)
-        scores(1, 2, 0)
-        weights(1, 1, 3)
-        weights(1, 1, 2)
-        v_quant(0, 2)
-        w_quant(1, 0)
-        w_copy(1, 1, 0, 256, nc.vector.tensor_copy)
-        scores(1, 2, 1)
-        weights(1, 2, 1)
-        scores(1, 2, 3)
-        scores(1, 2, 2)
-        weights(1, 2, 3)
-        weights(1, 2, 2)
-        scores(0, 2, 3)
-        weights(1, 2, 0)
-        scores(0, 2, 1)
+        weights(0, 1, 3)
         scores(0, 2, 0)
+        scores(0, 2, 1)
         scores(0, 2, 2)
-        weights(0, 2, 0)
-        ld_og(0)
+        scores(0, 2, 3)
+        scores(1, 2, 0)
+        scores(1, 2, 1)
+        scores(1, 2, 2)
+        scores(1, 2, 3)
         values(0, 0)
-        weights(0, 2, 1)
-        w_copy(1, 2, 0, 256, nc.vector.tensor_copy)
-        weights(0, 2, 3)
-        weights(0, 2, 2)
         values(1, 0)
+        w_copy(1, 1, 0, 256, nc.vector.tensor_copy)
+        nc.vector.transpose(out=sink_t[:], in_=sink_in[:])
+        w_copy(0, 1, 0, 256, nc.vector.tensor_copy)
         denom(0, 2, 0)
         w_quant(1, 1)
         values(1, 1)
-        tanh(0, 2, 0)
+        w_quant(0, 1)
         values(0, 1)
-        w_quant(1, 2)
-        w_copy(0, 2, 0, 160, nc.vector.tensor_copy)
+        weights(0, 2, 0)
+        weights(0, 2, 1)
+        weights(0, 2, 2)
+        weights(0, 2, 3)
+        weights(1, 2, 0)
+        weights(1, 2, 1)
+        weights(1, 2, 2)
+        weights(1, 2, 3)
+        tanh(0, 2, 0)
+        tanh(0, 2, 2)
+        tanh(1, 2, 1)
+        tanh(0, 1, 1)
+        gate_s(1, 2, 1)
+        w_copy(1, 2, 0, 256, nc.vector.tensor_copy)
         gated(0, 2, 0)
-        w_copy(0, 2, 160, 256, nc.scalar.copy)
-        w_quant(0, 2)
-        values(1, 2)
-        ld_og(2)
-        tanh(1, 2, 2)
-        tanh(0, 2, 1)
-        tanh(0, 1, 2)
-        recip(0, 2, 0)
-        fin_s(0, 2, 0, 0)
-        denom(1, 2, 2)
-        gated(1, 2, 2)
-        recip(1, 2, 2)
-        denom(0, 2, 1)
-        gated(0, 2, 1)
-        recip(0, 2, 1)
-        fin_s(0, 2, 0, 1)
+        denom(1, 2, 1)
+        w_quant(1, 2)
         values(0, 2)
-        denom(0, 1, 2)
-        fin_s(1, 2, 2, 1)
-        fin_s(1, 2, 2, 0)
-        fin_s(0, 2, 1, 0)
+        values(1, 2)
+        recip(0, 2, 0)
+        denom(0, 1, 1)
+        recip(1, 2, 1)
+        gated(0, 1, 1)
+        recip(0, 1, 1)
+        fin_s(0, 2, 0, 0)
+        fin_s(0, 2, 0, 1)
         store(0, 2, 0, nc.sync)
-        gate_v(0, 1, 2)
-        recip(0, 1, 2)
-        fin_v(0, 1, 2, 1)
-        store(1, 2, 2, nc.sync)
-        fin_v(0, 1, 2, 0)
-        fin_s(0, 2, 1, 1)
-        store(0, 2, 1, nc.scalar)
-        store(0, 1, 2, nc.sync)
+        gate_s(0, 2, 2)
+        fin_v(1, 2, 1, 0)
+        denom(0, 2, 2)
+        fin_v(1, 2, 1, 1)
+        store(1, 2, 1, nc.sync)
+        recip(0, 2, 2)
+        fin_s(0, 1, 1, 0)
+        fin_s(0, 1, 1, 1)
+        store(0, 1, 1, nc.sync)
+        fin_v(0, 2, 2, 0)
+        fin_v(0, 2, 2, 1)
+        store(0, 2, 2, nc.sync)

@@ -13,24 +13,39 @@ ALU = mybir.AluOpType
 ACT = mybir.ActivationFunctionType
 
 H, D, NQ, N, E = 2, 256, 512, 512, 128
+FLOPS = 2 * H * N * NQ * (D + E)
+
 P = 128
 ROWS = 64
 PACK = 4
-FLOPS = 2 * H * N * NQ * (D + E)
-QW = [128,256,128]
-Q0 = [0,128,384]
-KW = [512]
-K0 = [0]
-YB = [[0,0,1],[0,1,1]]
-YO = [[0,256,256],[128,0,384]]
-SB = [[[[0,0],[1,0],[1,128],[2,0]],[[0,0],[0,256],[1,0],[1,256]],[[2,0],[2,128],[2,256],[2,384]]],[[[0,0],[1,0],[1,128],[2,0]],[[0,0],[0,256],[1,0],[1,256]],[[2,0],[2,128],[2,256],[2,384]]]]
-WP = [1,0,1]
-QL = [[0],[1],[2]]
+RUN = 4
+QUAD = 32
+TILES = NQ // P
+
+PIECES = [[0], [1, 2], [3]]
+GROUPS = [[(0, 0), (1, 0)], [(1, 1), (1, 2)], [(0, 1), (0, 2)], [(0, 3), (1, 3)]]
+WIDTH = 2 * P
+K_SCALAR = 144
+
+MANTISSA, SIGN, ONE, HALF = 0x007FFFFF, -0x80000000, 0x3F800000, 0x3F000000
+MANTISSA_BITS, EXPONENT, EXPONENT_BIAS = 23, 0xFF, 127
+
+
+def score_place(piece, r):
+    if piece == 0:
+        return [(0, 0), (1, 0), (1, P), (2, 0)][r]
+    if piece == 1:
+        return r // 2, WIDTH * (r % 2)
+    return 2, P * r
+
+
+def of_group(view, g):
+    (h0, c0), (h1, c1) = GROUPS[g]
+    return view[:, h0, c0:c1 + 1] if h0 == h1 else view[:, :, c0]
 
 
 def tile_rows_sink_gate_kernel(tc, qT, kT, t, v, sink, og, out):
     nc = tc.nc
-    nu = len(QW)
 
     with ExitStack() as ctx:
         sb = ctx.enter_context(tc.tile_pool(name="sb", bufs=1))
@@ -40,319 +55,229 @@ def tile_rows_sink_gate_kernel(tc, qT, kT, t, v, sink, og, out):
         def sbuf(name, shape, dtype):
             return sb.tile(shape, dtype, name=name, align_bytes=64)
 
-        def per_u(name, shape, dtype):
-            return [sbuf("%s%d" % (name, u), shape(QW[u]), dtype) for u in range(nu)]
+        def per_piece(name, shape, dtype):
+            return [sbuf("%s%d" % (name, u), shape(P * len(tiles)), dtype) for u, tiles in enumerate(PIECES)]
 
-        def per_hu(name, shape, dtype):
-            tiles = [[], []]
-            for u in range(nu):
-                if WP[u]:
-                    both = sbuf("%s%d" % (name, u), shape(2 * QW[u]), dtype)
-                    tiles[0].append(both)
-                    tiles[1].append(both)
-                else:
-                    for h in range(H):
-                        tiles[h].append(sbuf("%s%d_%d" % (name, u, h), shape(QW[u]), dtype))
-            return tiles
+        def per_group(name, shape, dtype):
+            return [sbuf("%s%d" % (name, g), shape, dtype) for g in range(len(GROUPS))]
+
+        k_raw = sbuf("k_raw", [P, PACK, N], F32)
+        k_words = sbuf("k_words", [P, PACK, P, PACK], BF16)
+        k_codes = sbuf("k_codes", [P, N], U32)
+        k_scales = sbuf("k_scales", [P, N], U8)
+        q_raw = per_piece("q_raw", lambda n: [P, PACK, n], F32)
+        q_words = per_piece("q_words", lambda n: [P, n, PACK], BF16)
+        q_codes = per_piece("q_codes", lambda n: [P, n], U32)
+        q_scales = per_piece("q_scales", lambda n: [P, n], U8)
+        v_raw = sbuf("v_raw", [P, H, PACK, E], F32)
+        v_words = sbuf("v_words", [P, H, E, PACK], BF16)
+        v_codes = sbuf("v_codes", [P, H, E], U32)
+        v_scales = sbuf("v_scales", [P, H, E], U8)
+        w_rows = per_group("w_rows", [P, PACK, WIDTH], BF16)
+        w_words = per_group("w_words", [P, WIDTH, PACK], BF16)
+        w_codes = per_group("w_codes", [P, WIDTH], U32)
+        w_scales = per_group("w_scales", [P, WIDTH], U8)
 
         t_sb = sbuf("t_sb", [P, PACK], F32)
-        sink_in = sbuf("sink_in", [P, 32], F32)
-        sink_t = sbuf("sink_t", [P, 32], F32)
-        q_grp = {g[0]: sbuf("q_raw%d" % g[0], [P, PACK, sum(QW[u] for u in g)], F32) for g in QL}
-        q_raw = [q_grp[g[0]][:, :, Q0[u] - Q0[g[0]]:Q0[u] - Q0[g[0]] + QW[u]] for g in QL for u in g]
-        k_raw = [sbuf("k_raw%d" % u, [P, PACK, w], F32) for u, w in enumerate(KW)]
-        v_raw = sbuf("v_raw", [P, H, PACK, E], F32)
-        v_r = sbuf("v_r", [P, H, PACK, E], BF16)
-        og_sb = sbuf("og_sb", [P, H, NQ], F32)
-        q_g = per_u("q_g", lambda w: [P, w, PACK], BF16)
-        k_g = sbuf("k_g", [P, PACK, P, PACK], BF16)
-        v_g = sbuf("v_g", [P, H, E, PACK], BF16)
-        q_c = per_u("q_c", lambda w: [P, w], U32)
-        q_s = per_u("q_s", lambda w: [P, w], U8)
-        k_c = sbuf("k_c", [P, N], U32)
-        k_s = sbuf("k_s", [P, N], U8)
-        v_c = sbuf("v_c", [P, H * E], U32)
-        v_s = sbuf("v_s", [P, H * E], U8)
-        w_r = per_hu("w_r", lambda w: [P, PACK, w], BF16)
-        w_g = per_hu("w_g", lambda w: [P, w, PACK], BF16)
-        w_c = per_hu("w_c", lambda w: [P, w], U32)
-        w_s = per_hu("w_s", lambda w: [P, w], U8)
-        th = per_u("th", lambda w: [P, H * w], F32)
-        gate = per_u("gate", lambda w: [P, H * w], F32)
-        den = [per_u("den%d" % h, lambda w: [P, H * w // P], F32) for h in range(H)]
-        rec = [per_u("rec%d" % h, lambda w: [P, H * w // P], F32) for h in range(H)]
-        res = per_u("res", lambda w: [P, H * w], F32)
-        expo = sbuf("expo", [P, PACK], I32)
-        mant = sbuf("mant", [P, PACK], I32)
-        sgn = sbuf("sgn", [P, PACK], I32)
-        ln_e = sbuf("ln_e", [P, PACK], F32)
-        ln_m = sbuf("ln_m", [P, PACK], F32)
+        t_mantissa = sbuf("t_mantissa", [P, PACK], I32)
+        t_exponent = sbuf("t_exponent", [P, PACK], I32)
+        half_sign = sbuf("half_sign", [P, PACK], I32)
+        ln_mantissa = sbuf("ln_mantissa", [P, PACK], F32)
+        ln_power = sbuf("ln_power", [P, PACK], F32)
         ln_t = sbuf("ln_t", [P, PACK], F32)
-        one = sbuf("one", [P, 1], F32)
-        warm = sbuf("warm", [P, 1], F32)
-        warm2 = sbuf("warm2", [P, 1], F32)
+        sink_rows = sbuf("sink_rows", [P, QUAD], F32)
+        sink_cols = sbuf("sink_cols", [P, QUAD], F32)
+        og_sb = sbuf("og_sb", [P, H, TILES, E], F32)
+        tanh_og = per_group("tanh_og", [P, 2, E], F32)
+        gate = {g: sbuf("gate%d" % g, [P, 2, E], F32) for g in (1, 3)}
+        gated_y = {g: sbuf("gated_y%d" % g, [P, 2, E], F32) for g in (0, 2)}
+        denom = per_group("denom", [P, 2], F32)
+        inverse = per_group("inverse", [P, 2], F32)
+        result = per_group("result", [P, 2, E], F32)
 
-        score = [[ps.tile([P, 512], F32, name="score%d_%d" % (h, b)) for b in range(3)] for h in range(H)]
-        ybank = [ps.tile([P, 512], F32, name="y%d" % b) for b in range(2)]
+        score_banks = [[ps.tile([P, N], F32, name="score%d_%d" % (h, b)) for b in range(3)] for h in range(H)]
+        y_banks = [ps.tile([P, 2, 2, E], F32, name="y%d" % b) for b in range(2)]
+        half_y = [y_banks[g % 2][:, g // 2] for g in range(len(GROUPS))]
 
-        q_hbm = qT.rearrange("h (p j) n -> (h p) j n", j=PACK)
-        k_hbm = kT.rearrange("h (p j) n -> (h p) j n", j=PACK)
-        t_bits = t_sb[:].bitcast(I32)
+        def quantise(codes, scales, words):
+            nc.vector.quantize_mx(out=codes.bitcast(FP8X4), scales=scales, in_=words.rearrange("p n j -> p (n j)"))
 
-        def quant(codes, scales, src):
-            nc.vector.quantize_mx(out=codes.bitcast(FP8X4), scales=scales, in_=src)
+        def interleave(words, rows):
+            nc.vector.tensor_copy(out=words.rearrange("p (a b) j -> p a j b", b=RUN),
+                                  in_=rows.rearrange("p j (a b) -> p a j b", b=RUN))
 
-        def quant_cols(codes, scales, src):
-            w = codes.shape[1]
-            for n0, n1 in ([(0, 256), (256, 384)] if w == 384 else [(0, w)]):
-                quant(codes[:, n0:n1], scales[:, n0:n1], src[:, n0:n1].rearrange("p n j -> p (n j)"))
+        def deal_keys(copy, n0, n1):
+            copy(out=k_words[:, :, n0 // PACK:n1 // PACK, :].rearrange("p r s j -> p s j r"),
+                 in_=k_raw[:, :, n0:n1].rearrange("p j (s r) -> p s j r", r=PACK))
 
-        def ld_q(u):
-            nc.sync.dma_start(out=q_grp[u][:], in_=q_hbm[:, :, Q0[u]:Q0[u] + q_grp[u].shape[2]])
+        def quantise_keys(r):
+            quantise(k_codes[:, P * r:P * (r + 1)], k_scales[:, P * r:P * (r + 1)], k_words[:, r])
 
-        def ld_k(u):
-            nc.sync.dma_start(out=k_raw[u][:], in_=k_hbm[:, :, K0[u]:K0[u] + KW[u]])
+        def quantise_queries(u):
+            quantise(q_codes[u][:], q_scales[u][:], q_words[u][:])
 
-        def ld_og(h):
-            nc.sync.dma_start(out=og_sb[:, h].rearrange("p (c e) -> p c e", e=E), in_=og[h].rearrange("(c p) e -> p c e", p=P))
-
-        def ld_sk(a):
-            nc.sync.dma_start(out=sink_in[32 * a:32 * a + 8, :], in_=sink.rearrange("h (c a j) o -> a (h c) (j o)", a=4, j=32)[a])
-
-        def q_copy(u, copy):
-            copy(out=q_g[u][:].rearrange("p (a b) j -> p a j b", b=4), in_=q_raw[u].rearrange("p j (a b) -> p a j b", b=4))
-
-        def q_quant(u):
-            quant_cols(q_c[u], q_s[u], q_g[u])
-
-        def k_copy(u, n0, n1, copy):
-            copy(out=k_g[:, :, (K0[u] + n0) // PACK:(K0[u] + n1) // PACK, :].rearrange("p r s j -> p s j r"),
-                 in_=k_raw[u][:, :, n0:n1].rearrange("p j (s r) -> p s j r", r=PACK))
-
-        def k_quant(r0, r1):
-            quant(k_c[:, P * r0:P * r1], k_s[:, P * r0:P * r1], k_g[:, r0:r1].rearrange("p r s j -> p (r s j)"))
-
-        def v_sign(r):
-            nc.scalar.activation(out=v_r[:, :, r, :], in_=v_raw[:, :, r, :], func=ACT.Copy, scale=sgn[:, r:r + 1].bitcast(F32))
-
-        def v_move(h):
-            nc.vector.tensor_copy(out=v_g[:, h].rearrange("p (a b) r -> p a r b", b=4), in_=v_r[:, h].rearrange("p r (a b) -> p a r b", b=4))
-
-        def v_copy(h):
-            nc.vector.tensor_tensor(
-                out=v_g[:, h].rearrange("p (a b) r -> p a r b", b=4),
-                in0=v_raw[:, h].rearrange("p r (a b) -> p a r b", b=4),
-                in1=sgn[:].bitcast(F32).unsqueeze(1).unsqueeze(3).to_broadcast([P, E // 4, PACK, 4]),
-                op=ALU.mult)
-
-        def v_quant(h0, h1):
-            quant(v_c[:, E * h0:E * h1], v_s[:, E * h0:E * h1], v_g[:, h0:h1].rearrange("p h e r -> p (h e r)"))
-
-        def wcol(h, u):
-            return h * QW[u] if WP[u] else 0
+        def sign_values(h):
+            factor = half_sign[:].bitcast(F32).unsqueeze(1).unsqueeze(3).to_broadcast([P, E // RUN, PACK, RUN])
+            nc.vector.tensor_tensor(out=v_words[:, h].rearrange("p (a b) r -> p a r b", b=RUN),
+                                    in0=v_raw[:, h].rearrange("p r (a b) -> p a r b", b=RUN), in1=factor, op=ALU.mult)
 
         def scores(h, u, r):
-            rows = slice(ROWS * h, ROWS * (h + 1))
-            b, c0 = SB[h][u][r]
-            keys = slice(P * r, P * (r + 1))
-            for c in range(QW[u] // P):
-                cols = slice(P * c, P * (c + 1))
-                nc.tensor.matmul_mx(out=score[h][b][:, c0 + P * c:c0 + P * (c + 1)], lhsT=k_c[rows, keys].bitcast(FP8X4), lhsT_scale=k_s[rows, keys],
-                                    rhs=q_c[u][rows, cols].bitcast(FP8X4), rhs_scale=q_s[u][rows, cols], start=True, stop=True)
+            rows, keys = slice(ROWS * h, ROWS * (h + 1)), slice(P * r, P * (r + 1))
+            bank, first = score_place(u, r)
+            for n0 in range(0, P * len(PIECES[u]), P):
+                nc.tensor.matmul_mx(out=score_banks[h][bank][:, first + n0:first + n0 + P],
+                                    lhsT=k_codes[rows, keys].bitcast(FP8X4), lhsT_scale=k_scales[rows, keys],
+                                    rhs=q_codes[u][rows, n0:n0 + P].bitcast(FP8X4),
+                                    rhs_scale=q_scales[u][rows, n0:n0 + P], start=True, stop=True)
 
         def weights(h, u, r):
-            b, c0 = SB[h][u][r]
-            w0 = wcol(h, u)
-            nc.scalar.activation(out=w_r[h][u][:, r, w0:w0 + QW[u]], in_=score[h][b][:, c0:c0 + QW[u]], func=ACT.Exp, bias=ln_t[:, r:r + 1])
+            g = [(h, PIECES[u][0]) in members for members in GROUPS].index(True)
+            n0, n = P * GROUPS[g].index((h, PIECES[u][0])), P * len(PIECES[u])
+            bank, first = score_place(u, r)
+            nc.scalar.activation(out=w_rows[g][:, r, n0:n0 + n], in_=score_banks[h][bank][:, first:first + n],
+                                 func=ACT.Exp, bias=ln_t[:, r:r + 1])
 
-        def w_copy(h, u, n0, n1, copy):
-            copy(out=w_g[h][u][:, n0:n1].rearrange("p (a b) r -> p a r b", b=4),
-                 in_=w_r[h][u][:, :, n0:n1].rearrange("p r (a b) -> p a r b", b=4))
+        def interleave_weights(g):
+            interleave(w_words[g][:], w_rows[g][:])
 
-        def w_quant(h, u):
-            quant_cols(w_c[h][u], w_s[h][u], w_g[h][u])
+        def values(g):
+            quantise(w_codes[g][:], w_scales[g][:], w_words[g][:])
+            for m, h in enumerate(member[0] for member in GROUPS[g]):
+                cols = slice(P * m, P * (m + 1))
+                nc.tensor.matmul_mx(out=half_y[g][:, m], lhsT=w_codes[g][:, cols].bitcast(FP8X4),
+                                    lhsT_scale=w_scales[g][:, cols], rhs=v_codes[:, h].bitcast(FP8X4),
+                                    rhs_scale=v_scales[:, h], start=True, stop=True)
 
-        def values(h, u):
-            feats = slice(E * h, E * (h + 1))
-            for c in range(QW[u] // P):
-                cols = slice(wcol(h, u) + P * c, wcol(h, u) + P * (c + 1))
-                y0 = YO[h][u] + E * c
-                nc.tensor.matmul_mx(out=ybank[YB[h][u]][:, y0:y0 + E], lhsT=w_c[h][u][:, cols].bitcast(FP8X4), lhsT_scale=w_s[h][u][:, cols],
-                                    rhs=v_c[:, feats].bitcast(FP8X4), rhs_scale=v_s[:, feats], start=True, stop=True)
+        def add_sink(g):
+            sinks = sink_cols[:, 0:H * TILES].rearrange("p (h c) -> p h c", h=H)
+            nc.vector.scalar_tensor_tensor(out=denom[g][:], in0=half_y[g][:, :, E - 1], scalar=2.0,
+                                           in1=of_group(sinks, g), op0=ALU.mult, op1=ALU.add)
 
-        def span(h0, h1, u):
-            return slice(h0 * QW[u], h1 * QW[u])
+        def invert(g):
+            nc.vector.reciprocal(out=inverse[g][:], in_=denom[g][:])
 
-        def y_of(h0, h1, u):
-            return ybank[YB[h0][u]][:, YO[h0][u]:YO[h0][u] + (h1 - h0) * QW[u]]
+        def store(g):
+            nc.sync.dma_start(out=of_group(out.rearrange("h (c p) e -> p h c e", p=P), g), in_=result[g][:])
 
-        def tanh(h0, h1, u):
-            nc.scalar.activation(out=th[u][:, span(h0, h1, u)].rearrange("p (h n) -> p h n", h=h1 - h0), in_=og_sb[:, h0:h1, Q0[u]:Q0[u] + QW[u]], func=ACT.Tanh, scale=0.5)
+        def gate_y(g):
+            nc.vector.scalar_tensor_tensor(out=gated_y[g][:], in0=tanh_og[g][:], scalar=1.0, in1=half_y[g],
+                                           op0=ALU.add, op1=ALU.mult)
 
-        def gate_v(h0, h1, u):
-            nc.vector.tensor_scalar(out=gate[u][:, span(h0, h1, u)], in0=th[u][:, span(h0, h1, u)], scalar1=1.0, scalar2=None, op0=ALU.add)
+        def scale_rows(g):
+            for m in range(2):
+                nc.scalar.activation(out=result[g][:, m], in_=gated_y[g][:, m], func=ACT.Copy,
+                                     scale=inverse[g][:, m:m + 1])
 
-        def gate_s(h0, h1, u):
-            nc.scalar.activation(out=gate[u][:, span(h0, h1, u)], in_=th[u][:, span(h0, h1, u)], func=ACT.Copy, bias=1.0)
+        def make_gate(g):
+            nc.scalar.activation(out=gate[g][:], in_=tanh_og[g][:], func=ACT.Copy, bias=1.0)
 
-        def denom(h0, h1, u):
-            nt = (h1 - h0) * QW[u] // P
-            c0 = Q0[u] // P
-            nc.vector.scalar_tensor_tensor(out=den[h0][u][:, 0:nt].rearrange("p (h c) -> p h c", h=h1 - h0),
-                                           in0=y_of(h0, h1, u).rearrange("p (h c e) -> p h c e", h=h1 - h0, e=E)[:, :, :, E - 1], scalar=2.0,
-                                           in1=sink_t[:, 0:8].rearrange("p (h c) -> p h c", h=H)[:, h0:h1, c0:c0 + QW[u] // P], op0=ALU.mult, op1=ALU.add)
+        def scale_and_gate(g, m):
+            nc.vector.scalar_tensor_tensor(out=result[g][:, m], in0=half_y[g][:, m], scalar=inverse[g][:, m:m + 1],
+                                           in1=gate[g][:, m], op0=ALU.mult, op1=ALU.mult)
 
-        def recip(h0, h1, u):
-            nt = (h1 - h0) * QW[u] // P
-            nc.vector.reciprocal(out=rec[h0][u][:, 0:nt], in_=den[h0][u][:, 0:nt])
+        nc.vector.memset(sink_rows[:], 0.0)
+        q_hbm = qT.rearrange("h (p j) n -> (h p) j n", j=PACK)
 
-        def gated(h0, h1, u):
-            nc.vector.scalar_tensor_tensor(out=gate[u][:, span(h0, h1, u)], in0=th[u][:, span(h0, h1, u)], scalar=1.0,
-                                           in1=y_of(h0, h1, u), op0=ALU.add, op1=ALU.mult)
+        def load_queries(u):
+            nc.sync.dma_start(out=q_raw[u][:], in_=q_hbm[:, :, P * PIECES[u][0]:P * (PIECES[u][-1] + 1)])
 
-        def fin_v(h0, h1, u, c):
-            g0 = h0 * QW[u] + E * c
-            nc.vector.scalar_tensor_tensor(out=res[u][:, g0:g0 + E], in0=y_of(h0, h1, u)[:, E * c:E * (c + 1)], scalar=rec[h0][u][:, c:c + 1],
-                                           in1=gate[u][:, g0:g0 + E], op0=ALU.mult, op1=ALU.mult)
+        nc.sync.dma_start(out=t_sb[:], in_=t.rearrange("(s r) o -> s (r o)", r=PACK))
+        nc.sync.dma_start(out=k_raw[:], in_=kT.rearrange("h (p j) n -> (h p) j n", j=PACK))
+        load_queries(0)
+        load_queries(1)
+        nc.sync.dma_start(out=v_raw[:].rearrange("s h r e -> s h (r e)"),
+                          in_=v.rearrange("h (s r) e -> s h (r e)", r=PACK))
+        load_queries(2)
+        for h in range(H):
+            nc.sync.dma_start(out=og_sb[:, h], in_=og[h].rearrange("(c p) e -> p c e", p=P))
+        sink_hbm = sink.rearrange("h (c a x) o -> a (h c) (x o)", a=P // QUAD, x=QUAD)
+        for a in range(P // QUAD):
+            nc.sync.dma_start(out=sink_rows[QUAD * a:QUAD * a + H * TILES, :], in_=sink_hbm[a])
 
-        def fin_s(h0, h1, u, c):
-            g0 = h0 * QW[u] + E * c
-            nc.scalar.activation(out=res[u][:, g0:g0 + E], in_=gate[u][:, g0:g0 + E], func=ACT.Copy, scale=rec[h0][u][:, c:c + 1])
+        t_bits = t_sb[:].bitcast(I32)
+        nc.vector.tensor_scalar(out=t_mantissa[:], in0=t_bits, scalar1=MANTISSA, scalar2=ONE,
+                                op0=ALU.bitwise_and, op1=ALU.bitwise_or)
+        nc.vector.tensor_scalar(out=t_exponent[:], in0=t_bits, scalar1=MANTISSA_BITS, scalar2=EXPONENT,
+                                op0=ALU.logical_shift_right, op1=ALU.bitwise_and)
+        nc.vector.tensor_scalar(out=half_sign[:], in0=t_bits, scalar1=SIGN, scalar2=HALF,
+                                op0=ALU.bitwise_and, op1=ALU.bitwise_or)
+        nc.scalar.activation(out=ln_mantissa[:], in_=t_mantissa[:].bitcast(F32), func=ACT.Ln)
+        nc.vector.tensor_scalar(out=ln_power[:], in0=t_exponent[:], scalar1=-float(EXPONENT_BIAS),
+                                scalar2=math.log(2.0), op0=ALU.add, op1=ALU.mult)
+        nc.vector.tensor_tensor(out=ln_t[:], in0=ln_power[:], in1=ln_mantissa[:], op=ALU.add)
 
-        def store(h0, h1, u, eng):
-            rows = slice(Q0[u], Q0[u] + QW[u])
-            if QW[u] == P:
-                eng.dma_start(out=out[h0:h1, rows, :].rearrange("h p e -> p h e"), in_=res[u][:, span(h0, h1, u)].rearrange("p (h e) -> p h e", e=E))
-            else:
-                for h in range(h0, h1):
-                    eng.dma_start(out=out[h, rows, :].rearrange("(c p) e -> p c e", p=P), in_=res[u][:, span(h, h + 1, u)].rearrange("p (c e) -> p c e", e=E))
+        deal_keys(nc.scalar.copy, N - K_SCALAR, N)
+        deal_keys(nc.vector.tensor_copy, 0, N - K_SCALAR)
+        interleave(q_words[0][:], q_raw[0][:])
+        quantise_keys(0)
+        quantise_queries(0)
+        quantise_keys(1)
+        quantise_keys(2)
+        interleave(q_words[1][:], q_raw[1][:])
+        quantise_keys(3)
+        quantise_queries(1)
 
-        nc.vector.memset(one[:], 1.0)
-        nc.vector.memset(sink_in[:], 0.0)
-        nc.scalar.dma_start(out=t_sb[:], in_=t.rearrange("(p r) o -> p (r o)", r=PACK))
-        ld_k(0)
-        ld_q(0)
-        ld_q(1)
-        nc.sync.dma_start(out=v_raw[:].rearrange("p h r e -> p h (r e)"), in_=v.rearrange("h (p r) e -> p h (r e)", r=PACK))
-        ld_q(2)
-        ld_og(0)
-        ld_og(1)
-        ld_sk(0)
-        ld_sk(1)
-        ld_sk(2)
-        ld_sk(3)
-        nc.scalar.activation(out=warm[:], in_=one[:], func=ACT.Ln)
-        nc.vector.tensor_scalar(out=mant[:], in0=t_bits, scalar1=0x007FFFFF, scalar2=0x3F800000, op0=ALU.bitwise_and, op1=ALU.bitwise_or)
-        nc.vector.tensor_scalar(out=expo[:], in0=t_bits, scalar1=23, scalar2=255, op0=ALU.logical_shift_right, op1=ALU.bitwise_and)
-        nc.vector.tensor_scalar(out=sgn[:], in0=t_bits, scalar1=-0x80000000, scalar2=0x3F000000, op0=ALU.bitwise_and, op1=ALU.bitwise_or)
-        nc.scalar.activation(out=ln_m[:], in_=mant[:].bitcast(F32), func=ACT.Ln)
-        nc.scalar.activation(out=warm2[:], in_=one[:], func=ACT.Exp)
-        nc.vector.tensor_scalar(out=ln_e[:], in0=expo[:], scalar1=-127.0, scalar2=math.log(2.0), op0=ALU.add, op1=ALU.mult)
-        nc.vector.tensor_tensor(out=ln_t[:], in0=ln_e[:], in1=ln_m[:], op=ALU.add)
-        k_copy(0, 384, 512, nc.scalar.copy)
-        k_copy(0, 0, 384, nc.vector.tensor_copy)
-        q_copy(0, nc.vector.tensor_copy)
-        k_quant(0, 1)
-        q_quant(0)
-        k_quant(1, 2)
-        k_quant(2, 3)
-        q_copy(1, nc.vector.tensor_copy)
-        k_quant(3, 4)
-        q_quant(1)
-        scores(0, 0, 0)
-        scores(1, 0, 0)
-        scores(0, 0, 1)
-        scores(1, 0, 1)
-        scores(0, 0, 2)
-        scores(1, 0, 2)
-        weights(0, 0, 0)
-        weights(1, 0, 0)
-        weights(0, 0, 1)
-        weights(0, 0, 2)
-        weights(1, 0, 1)
-        weights(1, 0, 2)
-        scores(0, 0, 3)
-        scores(1, 0, 3)
-        scores(1, 1, 0)
-        scores(1, 1, 1)
-        scores(1, 1, 2)
-        scores(1, 1, 3)
-        weights(0, 0, 3)
-        weights(1, 0, 3)
-        scores(0, 1, 0)
-        scores(0, 1, 1)
-        scores(0, 1, 2)
-        scores(0, 1, 3)
-        v_copy(0)
-        v_copy(1)
-        q_copy(2, nc.vector.tensor_copy)
-        w_copy(1, 0, 0, 256, nc.vector.tensor_copy)
-        q_quant(2)
-        v_quant(0, 1)
-        v_quant(1, 2)
-        w_quant(1, 0)
-        weights(1, 1, 0)
-        weights(1, 1, 1)
-        weights(1, 1, 2)
-        weights(1, 1, 3)
-        weights(0, 1, 0)
-        weights(0, 1, 1)
-        weights(0, 1, 2)
-        weights(0, 1, 3)
-        scores(0, 2, 0)
-        scores(0, 2, 1)
-        scores(0, 2, 2)
-        scores(0, 2, 3)
-        scores(1, 2, 0)
-        scores(1, 2, 1)
-        scores(1, 2, 2)
-        scores(1, 2, 3)
-        values(0, 0)
-        values(1, 0)
-        w_copy(1, 1, 0, 256, nc.vector.tensor_copy)
-        nc.vector.transpose(out=sink_t[:], in_=sink_in[:])
-        w_copy(0, 1, 0, 256, nc.vector.tensor_copy)
-        denom(0, 2, 0)
-        w_quant(1, 1)
-        values(1, 1)
-        w_quant(0, 1)
-        values(0, 1)
-        weights(0, 2, 0)
-        weights(0, 2, 1)
-        weights(0, 2, 2)
-        weights(0, 2, 3)
-        weights(1, 2, 0)
-        weights(1, 2, 1)
-        weights(1, 2, 2)
-        weights(1, 2, 3)
-        tanh(0, 2, 0)
-        tanh(0, 2, 2)
-        tanh(1, 2, 1)
-        tanh(0, 1, 1)
-        gate_s(1, 2, 1)
-        w_copy(1, 2, 0, 256, nc.vector.tensor_copy)
-        gated(0, 2, 0)
-        denom(1, 2, 1)
-        w_quant(1, 2)
-        values(0, 2)
-        values(1, 2)
-        recip(0, 2, 0)
-        denom(0, 1, 1)
-        recip(1, 2, 1)
-        gated(0, 1, 1)
-        recip(0, 1, 1)
-        fin_s(0, 2, 0, 0)
-        fin_s(0, 2, 0, 1)
-        store(0, 2, 0, nc.sync)
-        gate_s(0, 2, 2)
-        fin_v(1, 2, 1, 0)
-        denom(0, 2, 2)
-        fin_v(1, 2, 1, 1)
-        store(1, 2, 1, nc.sync)
-        recip(0, 2, 2)
-        fin_s(0, 1, 1, 0)
-        fin_s(0, 1, 1, 1)
-        store(0, 1, 1, nc.sync)
-        fin_v(0, 2, 2, 0)
-        fin_v(0, 2, 2, 1)
-        store(0, 2, 2, nc.sync)
+        for r in range(PACK - 1):
+            for h in range(H):
+                scores(h, 0, r)
+        for h, r in [(0, 0), (1, 0), (0, 1), (0, 2), (1, 1), (1, 2)]:
+            weights(h, 0, r)
+        for h in range(H):
+            scores(h, 0, PACK - 1)
+        for r in range(PACK):
+            scores(1, 1, r)
+        for h in range(H):
+            weights(h, 0, PACK - 1)
+        for r in range(PACK):
+            scores(0, 1, r)
+
+        for h in range(H):
+            sign_values(h)
+        interleave(q_words[2][:], q_raw[2][:])
+        interleave_weights(0)
+        quantise_queries(2)
+        for h in range(H):
+            quantise(v_codes[:, h], v_scales[:, h], v_words[:, h])
+
+        for h in (1, 0):
+            for r in range(PACK):
+                weights(h, 1, r)
+        for h in range(H):
+            for r in range(PACK):
+                scores(h, 2, r)
+        values(0)
+        interleave_weights(1)
+        nc.vector.transpose(out=sink_cols[:], in_=sink_rows[:])
+        interleave_weights(2)
+        add_sink(0)
+        values(1)
+        values(2)
+        for h in range(H):
+            for r in range(PACK):
+                weights(h, 2, r)
+
+        for g in (0, 3, 1, 2):
+            nc.scalar.activation(out=tanh_og[g][:], in_=of_group(og_sb[:], g), func=ACT.Tanh, scale=0.5)
+        make_gate(1)
+        interleave_weights(3)
+        gate_y(0)
+        add_sink(1)
+        values(3)
+        invert(0)
+        add_sink(2)
+        invert(1)
+        gate_y(2)
+        invert(2)
+        scale_rows(0)
+        store(0)
+        make_gate(3)
+        scale_and_gate(1, 0)
+        add_sink(3)
+        scale_and_gate(1, 1)
+        store(1)
+        invert(3)
+        scale_rows(2)
+        store(2)
+        for m in range(2):
+            scale_and_gate(3, m)
+        store(3)

@@ -19,13 +19,12 @@ P = 128
 ROWS = 64
 PACK = 4
 RUN = 4
-QUAD = 32
 TILES = NQ // P
 
 PIECES = [[0], [1, 2], [3]]
-GROUPS = [[(0, 0), (1, 0)], [(1, 1), (1, 2)], [(0, 1), (0, 2)], [(0, 3), (1, 3)]]
-WIDTH = 2 * P
-K_SCALAR = 144
+GROUPS = [[(0, 0), (1, 0)], [(1, 1), (1, 2)], [(0, 1), (0, 2)], [(0, 3)], [(1, 3)]]
+UNITS = [[(0, 0), (1, 0)], [(1, 1), (1, 2)], [(0, 1), (0, 2)], [(0, 3), (1, 3)]]
+SCORE_BANKS = 3
 
 MANTISSA, SIGN, ONE, HALF = 0x007FFFFF, -0x80000000, 0x3F800000, 0x3F000000
 MANTISSA_BITS, EXPONENT, EXPONENT_BIAS = 23, 0xFF, 127
@@ -33,14 +32,14 @@ MANTISSA_BITS, EXPONENT, EXPONENT_BIAS = 23, 0xFF, 127
 
 def score_place(piece, r):
     if piece == 0:
-        return [(0, 0), (1, 0), (1, P), (2, 0)][r]
+        return [(0, 0), (1, 0), (2, 0), (2, P)][r]
     if piece == 1:
-        return r // 2, WIDTH * (r % 2)
+        return r // 2, 2 * P * (r % 2)
     return 2, P * r
 
 
-def of_group(view, g):
-    (h0, c0), (h1, c1) = GROUPS[g]
+def of_unit(view, g):
+    (h0, c0), (h1, c1) = UNITS[g]
     return view[:, h0, c0:c1 + 1] if h0 == h1 else view[:, :, c0]
 
 
@@ -59,7 +58,10 @@ def tile_rows_sink_gate_kernel(tc, qT, kT, t, v, sink, og, out):
             return [sbuf("%s%d" % (name, u), shape(P * len(tiles)), dtype) for u, tiles in enumerate(PIECES)]
 
         def per_group(name, shape, dtype):
-            return [sbuf("%s%d" % (name, g), shape, dtype) for g in range(len(GROUPS))]
+            return [sbuf("%s%d" % (name, g), shape(P * len(pairs)), dtype) for g, pairs in enumerate(GROUPS)]
+
+        def per_unit(name, shape, dtype):
+            return [sbuf("%s%d" % (name, g), shape, dtype) for g in range(len(UNITS))]
 
         k_raw = sbuf("k_raw", [P, PACK, N], F32)
         k_words = sbuf("k_words", [P, PACK, P, PACK], BF16)
@@ -69,14 +71,14 @@ def tile_rows_sink_gate_kernel(tc, qT, kT, t, v, sink, og, out):
         q_words = per_piece("q_words", lambda n: [P, n, PACK], BF16)
         q_codes = per_piece("q_codes", lambda n: [P, n], U32)
         q_scales = per_piece("q_scales", lambda n: [P, n], U8)
-        v_raw = sbuf("v_raw", [P, H, PACK, E], F32)
+        v_raw = [sbuf("v_raw%d" % h, [P, PACK, E], F32) for h in range(H)]
         v_words = sbuf("v_words", [P, H, E, PACK], BF16)
         v_codes = sbuf("v_codes", [P, H, E], U32)
         v_scales = sbuf("v_scales", [P, H, E], U8)
-        w_rows = per_group("w_rows", [P, PACK, WIDTH], BF16)
-        w_words = per_group("w_words", [P, WIDTH, PACK], BF16)
-        w_codes = per_group("w_codes", [P, WIDTH], U32)
-        w_scales = per_group("w_scales", [P, WIDTH], U8)
+        w_rows = per_group("w_rows", lambda n: [P, PACK, n], BF16)
+        w_words = per_group("w_words", lambda n: [P, n, PACK], BF16)
+        w_codes = per_group("w_codes", lambda n: [P, n], U32)
+        w_scales = per_group("w_scales", lambda n: [P, n], U8)
 
         t_sb = sbuf("t_sb", [P, PACK], F32)
         t_mantissa = sbuf("t_mantissa", [P, PACK], I32)
@@ -85,19 +87,19 @@ def tile_rows_sink_gate_kernel(tc, qT, kT, t, v, sink, og, out):
         ln_mantissa = sbuf("ln_mantissa", [P, PACK], F32)
         ln_power = sbuf("ln_power", [P, PACK], F32)
         ln_t = sbuf("ln_t", [P, PACK], F32)
-        sink_rows = sbuf("sink_rows", [P, QUAD], F32)
-        sink_cols = sbuf("sink_cols", [P, QUAD], F32)
+        sinks = sbuf("sinks", [P, H, TILES], F32)
         og_sb = sbuf("og_sb", [P, H, TILES, E], F32)
-        tanh_og = per_group("tanh_og", [P, 2, E], F32)
-        gate = {g: sbuf("gate%d" % g, [P, 2, E], F32) for g in (1, 3)}
-        gated_y = {g: sbuf("gated_y%d" % g, [P, 2, E], F32) for g in (0, 2)}
-        denom = per_group("denom", [P, 2], F32)
-        inverse = per_group("inverse", [P, 2], F32)
-        result = per_group("result", [P, 2, E], F32)
+        tanh_og = per_unit("tanh_og", [P, 2, E], F32)
+        between = per_unit("between", [P, 2, E], F32)
+        denom = sbuf("denom", [P, H, TILES], F32)
+        inverse = sbuf("inverse", [P, H, TILES], F32)
+        result = per_unit("result", [P, 2, E], F32)
+        unread = sbuf("unread", [P, 1], F32)
 
-        score_banks = [[ps.tile([P, N], F32, name="score%d_%d" % (h, b)) for b in range(3)] for h in range(H)]
+        score_banks = [[ps.tile([P, N], F32, name="score%d_%d" % (h, b)) for b in range(SCORE_BANKS)]
+                       for h in range(H)]
         y_banks = [ps.tile([P, 2, 2, E], F32, name="y%d" % b) for b in range(2)]
-        half_y = [y_banks[g % 2][:, g // 2] for g in range(len(GROUPS))]
+        half_y = [y_banks[0][:, 0], y_banks[1][:, 1], y_banks[1][:, 0], y_banks[0][:, 1]]
 
         def quantise(codes, scales, words):
             nc.vector.quantize_mx(out=codes.bitcast(FP8X4), scales=scales, in_=words.rearrange("p n j -> p (n j)"))
@@ -106,29 +108,37 @@ def tile_rows_sink_gate_kernel(tc, qT, kT, t, v, sink, og, out):
             nc.vector.tensor_copy(out=words.rearrange("p (a b) j -> p a j b", b=RUN),
                                   in_=rows.rearrange("p j (a b) -> p a j b", b=RUN))
 
-        def deal_keys(copy, n0, n1):
-            copy(out=k_words[:, :, n0 // PACK:n1 // PACK, :].rearrange("p r s j -> p s j r"),
-                 in_=k_raw[:, :, n0:n1].rearrange("p j (s r) -> p s j r", r=PACK))
+        def deal_keys(copy, r0, r1):
+            copy(out=k_words[:, r0:r1].rearrange("p r s j -> p s j r"),
+                 in_=k_raw[:].rearrange("p j (s r) -> p s j r", r=PACK)[:, :, :, r0:r1])
 
         def quantise_keys(r):
             quantise(k_codes[:, P * r:P * (r + 1)], k_scales[:, P * r:P * (r + 1)], k_words[:, r])
 
-        def quantise_queries(u):
-            quantise(q_codes[u][:], q_scales[u][:], q_words[u][:])
+        def interleave_queries(u, m):
+            cols = slice(P * m, P * (m + 1))
+            interleave(q_words[u][:, cols], q_raw[u][:, :, cols])
+
+        def quantise_queries(u, m):
+            cols = slice(P * m, P * (m + 1))
+            quantise(q_codes[u][:, cols], q_scales[u][:, cols], q_words[u][:, cols])
+
+        def quantise_values():
+            quantise(v_codes[:].rearrange("p h e -> p (h e)"), v_scales[:].rearrange("p h e -> p (h e)"),
+                     v_words[:].rearrange("p h e r -> p (h e) r"))
 
         def sign_values(h):
             factor = half_sign[:].bitcast(F32).unsqueeze(1).unsqueeze(3).to_broadcast([P, E // RUN, PACK, RUN])
             nc.vector.tensor_tensor(out=v_words[:, h].rearrange("p (a b) r -> p a r b", b=RUN),
-                                    in0=v_raw[:, h].rearrange("p r (a b) -> p a r b", b=RUN), in1=factor, op=ALU.mult)
+                                    in0=v_raw[h][:].rearrange("p r (a b) -> p a r b", b=RUN), in1=factor, op=ALU.mult)
 
-        def scores(h, u, r):
-            rows, keys = slice(ROWS * h, ROWS * (h + 1)), slice(P * r, P * (r + 1))
+        def scores(h, u, r, m=0):
+            rows, keys, cols = slice(ROWS * h, ROWS * (h + 1)), slice(P * r, P * (r + 1)), slice(P * m, P * (m + 1))
             bank, first = score_place(u, r)
-            for n0 in range(0, P * len(PIECES[u]), P):
-                nc.tensor.matmul_mx(out=score_banks[h][bank][:, first + n0:first + n0 + P],
-                                    lhsT=k_codes[rows, keys].bitcast(FP8X4), lhsT_scale=k_scales[rows, keys],
-                                    rhs=q_codes[u][rows, n0:n0 + P].bitcast(FP8X4),
-                                    rhs_scale=q_scales[u][rows, n0:n0 + P], start=True, stop=True)
+            nc.tensor.matmul_mx(out=score_banks[h][bank][:, first + P * m:first + P * (m + 1)],
+                                lhsT=k_codes[rows, keys].bitcast(FP8X4), lhsT_scale=k_scales[rows, keys],
+                                rhs=q_codes[u][rows, cols].bitcast(FP8X4), rhs_scale=q_scales[u][rows, cols],
+                                start=True, stop=True)
 
         def weights(h, u, r):
             g = [(h, PIECES[u][0]) in members for members in GROUPS].index(True)
@@ -140,42 +150,51 @@ def tile_rows_sink_gate_kernel(tc, qT, kT, t, v, sink, og, out):
         def interleave_weights(g):
             interleave(w_words[g][:], w_rows[g][:])
 
-        def values(g):
+        def quantise_weights(g):
             quantise(w_codes[g][:], w_scales[g][:], w_words[g][:])
-            for m, h in enumerate(member[0] for member in GROUPS[g]):
+
+        def values(g):
+            for m, pair in enumerate(GROUPS[g]):
+                unit = [pair in members for members in UNITS].index(True)
                 cols = slice(P * m, P * (m + 1))
-                nc.tensor.matmul_mx(out=half_y[g][:, m], lhsT=w_codes[g][:, cols].bitcast(FP8X4),
-                                    lhsT_scale=w_scales[g][:, cols], rhs=v_codes[:, h].bitcast(FP8X4),
-                                    rhs_scale=v_scales[:, h], start=True, stop=True)
+                nc.tensor.matmul_mx(out=half_y[unit][:, UNITS[unit].index(pair)],
+                                    lhsT=w_codes[g][:, cols].bitcast(FP8X4), lhsT_scale=w_scales[g][:, cols],
+                                    rhs=v_codes[:, pair[0]].bitcast(FP8X4), rhs_scale=v_scales[:, pair[0]],
+                                    start=True, stop=True)
 
-        def add_sink(g):
-            sinks = sink_cols[:, 0:H * TILES].rearrange("p (h c) -> p h c", h=H)
-            nc.vector.scalar_tensor_tensor(out=denom[g][:], in0=half_y[g][:, :, E - 1], scalar=2.0,
-                                           in1=of_group(sinks, g), op0=ALU.mult, op1=ALU.add)
+        def add_sink(c0, c1, sums):
+            nc.vector.scalar_tensor_tensor(out=denom[:, :, c0:c1], in0=sums[:, :, :, E - 1], scalar=2.0,
+                                           in1=sinks[:, :, c0:c1], op0=ALU.mult, op1=ALU.add)
 
-        def invert(g):
-            nc.vector.reciprocal(out=inverse[g][:], in_=denom[g][:])
+        def invert(c0, c1):
+            nc.vector.reciprocal(out=inverse[:, :, c0:c1], in_=denom[:, :, c0:c1])
 
         def store(g):
-            nc.sync.dma_start(out=of_group(out.rearrange("h (c p) e -> p h c e", p=P), g), in_=result[g][:])
+            nc.sync.dma_start(out=of_unit(out.rearrange("h (c p) e -> p h c e", p=P), g), in_=result[g][:])
+
+        def tanh_gate(g):
+            nc.scalar.activation(out=tanh_og[g][:], in_=of_unit(og_sb[:], g), func=ACT.Tanh, scale=0.5)
 
         def gate_y(g):
-            nc.vector.scalar_tensor_tensor(out=gated_y[g][:], in0=tanh_og[g][:], scalar=1.0, in1=half_y[g],
+            nc.vector.scalar_tensor_tensor(out=between[g][:], in0=tanh_og[g][:], scalar=1.0, in1=half_y[g],
                                            op0=ALU.add, op1=ALU.mult)
 
-        def scale_rows(g):
+        def scale_on_scalar(g, m):
+            nc.scalar.activation(out=result[g][:, m], in_=between[g][:, m], func=ACT.Copy,
+                                 scale=of_unit(inverse[:], g)[:, m:m + 1])
+
+        def scale_on_vector(g, m):
+            nc.vector.tensor_scalar(out=result[g][:, m], in0=between[g][:, m], scalar1=of_unit(inverse[:], g)[:, m:m + 1],
+                                    scalar2=None, op0=ALU.mult)
+
+        def scale_gate(g):
             for m in range(2):
-                nc.scalar.activation(out=result[g][:, m], in_=gated_y[g][:, m], func=ACT.Copy,
-                                     scale=inverse[g][:, m:m + 1])
+                nc.scalar.activation(out=between[g][:, m], in_=tanh_og[g][:, m], func=ACT.Identity,
+                                     scale=of_unit(inverse[:], g)[:, m:m + 1], bias=of_unit(inverse[:], g)[:, m:m + 1])
 
-        def make_gate(g):
-            nc.scalar.activation(out=gate[g][:], in_=tanh_og[g][:], func=ACT.Copy, bias=1.0)
+        def times_y(g):
+            nc.vector.tensor_tensor(out=result[g][:], in0=half_y[g], in1=between[g][:], op=ALU.mult)
 
-        def scale_and_gate(g, m):
-            nc.vector.scalar_tensor_tensor(out=result[g][:, m], in0=half_y[g][:, m], scalar=inverse[g][:, m:m + 1],
-                                           in1=gate[g][:, m], op0=ALU.mult, op1=ALU.mult)
-
-        nc.vector.memset(sink_rows[:], 0.0)
         q_hbm = qT.rearrange("h (p j) n -> (h p) j n", j=PACK)
 
         def load_queries(u):
@@ -185,14 +204,13 @@ def tile_rows_sink_gate_kernel(tc, qT, kT, t, v, sink, og, out):
         nc.sync.dma_start(out=k_raw[:], in_=kT.rearrange("h (p j) n -> (h p) j n", j=PACK))
         load_queries(0)
         load_queries(1)
-        nc.sync.dma_start(out=v_raw[:].rearrange("s h r e -> s h (r e)"),
-                          in_=v.rearrange("h (s r) e -> s h (r e)", r=PACK))
+        for h in range(H):
+            nc.sync.dma_start(out=v_raw[h][:], in_=v[h].rearrange("(s r) e -> s r e", r=PACK))
         load_queries(2)
         for h in range(H):
             nc.sync.dma_start(out=og_sb[:, h], in_=og[h].rearrange("(c p) e -> p c e", p=P))
-        sink_hbm = sink.rearrange("h (c a x) o -> a (h c) (x o)", a=P // QUAD, x=QUAD)
-        for a in range(P // QUAD):
-            nc.sync.dma_start(out=sink_rows[QUAD * a:QUAD * a + H * TILES, :], in_=sink_hbm[a])
+        with nc.allow_non_contiguous_dma(reason="one sink a query, and a query tile has one query a partition"):
+            nc.sync.dma_start(out=sinks[:], in_=sink.rearrange("h (c p) o -> p h (c o)", p=P))
 
         t_bits = t_sb[:].bitcast(I32)
         nc.vector.tensor_scalar(out=t_mantissa[:], in0=t_bits, scalar1=MANTISSA, scalar2=ONE,
@@ -202,82 +220,86 @@ def tile_rows_sink_gate_kernel(tc, qT, kT, t, v, sink, og, out):
         nc.vector.tensor_scalar(out=half_sign[:], in0=t_bits, scalar1=SIGN, scalar2=HALF,
                                 op0=ALU.bitwise_and, op1=ALU.bitwise_or)
         nc.scalar.activation(out=ln_mantissa[:], in_=t_mantissa[:].bitcast(F32), func=ACT.Ln)
+        nc.scalar.activation(out=unread[:], in_=ln_mantissa[:, 0:1], func=ACT.Exp)
         nc.vector.tensor_scalar(out=ln_power[:], in0=t_exponent[:], scalar1=-float(EXPONENT_BIAS),
                                 scalar2=math.log(2.0), op0=ALU.add, op1=ALU.mult)
         nc.vector.tensor_tensor(out=ln_t[:], in0=ln_power[:], in1=ln_mantissa[:], op=ALU.add)
 
-        deal_keys(nc.scalar.copy, N - K_SCALAR, N)
-        deal_keys(nc.vector.tensor_copy, 0, N - K_SCALAR)
-        interleave(q_words[0][:], q_raw[0][:])
+        deal_keys(nc.vector.tensor_copy, 0, PACK // 2)
+        deal_keys(nc.scalar.copy, PACK // 2, PACK)
+        interleave_queries(0, 0)
         quantise_keys(0)
-        quantise_queries(0)
-        quantise_keys(1)
-        quantise_keys(2)
-        interleave(q_words[1][:], q_raw[1][:])
-        quantise_keys(3)
-        quantise_queries(1)
+        quantise_queries(0, 0)
+        for r in range(1, PACK):
+            quantise_keys(r)
+        for m in range(2):
+            interleave_queries(1, m)
+        for m in range(2):
+            quantise_queries(1, m)
 
-        for r in range(PACK - 1):
+        for r in range(PACK):
             for h in range(H):
                 scores(h, 0, r)
-        for h, r in [(0, 0), (1, 0), (0, 1), (0, 2), (1, 1), (1, 2)]:
-            weights(h, 0, r)
-        for h in range(H):
-            scores(h, 0, PACK - 1)
-        for r in range(PACK):
-            scores(1, 1, r)
-        for h in range(H):
-            weights(h, 0, PACK - 1)
-        for r in range(PACK):
-            scores(0, 1, r)
-
-        for h in range(H):
-            sign_values(h)
-        interleave(q_words[2][:], q_raw[2][:])
-        interleave_weights(0)
-        quantise_queries(2)
-        for h in range(H):
-            quantise(v_codes[:, h], v_scales[:, h], v_words[:, h])
-
+        for r in range(PACK // 2):
+            for h in range(H):
+                weights(h, 0, r)
         for h in (1, 0):
-            for r in range(PACK):
-                weights(h, 1, r)
+            for pair in range(2):
+                for m in range(2):
+                    for r in (2 * pair, 2 * pair + 1):
+                        scores(h, 1, r, m)
+        for r in range(PACK // 2, PACK):
+            for h in range(H):
+                weights(h, 0, r)
+
+        sign_values(0)
+        sign_values(1)
+        interleave_queries(2, 0)
+        interleave_weights(0)
+        quantise_queries(2, 0)
+        quantise_values()
         for h in range(H):
             for r in range(PACK):
                 scores(h, 2, r)
-        values(0)
+        for h in (1, 0):
+            for r in range(PACK):
+                weights(h, 1, r)
         interleave_weights(1)
-        nc.vector.transpose(out=sink_cols[:], in_=sink_rows[:])
-        interleave_weights(2)
-        add_sink(0)
+        quantise_weights(0)
+        values(0)
+        quantise_weights(1)
         values(1)
-        values(2)
+        interleave_weights(2)
+        add_sink(0, 1, half_y[0].unsqueeze(2))
         for h in range(H):
             for r in range(PACK):
                 weights(h, 2, r)
-
-        for g in (0, 3, 1, 2):
-            nc.scalar.activation(out=tanh_og[g][:], in_=of_group(og_sb[:], g), func=ACT.Tanh, scale=0.5)
-        make_gate(1)
+        for g in (1, 2, 0, 3):
+            tanh_gate(g)
+        quantise_weights(2)
+        values(2)
+        invert(0, 1)
         interleave_weights(3)
-        gate_y(0)
-        add_sink(1)
+        interleave_weights(4)
+        quantise_weights(3)
+        add_sink(1, 3, y_banks[1][:])
+        quantise_weights(4)
         values(3)
-        invert(0)
-        add_sink(2)
-        invert(1)
+        values(4)
+        gate_y(1)
+        invert(1, 3)
         gate_y(2)
-        invert(2)
-        scale_rows(0)
-        store(0)
-        make_gate(3)
-        scale_and_gate(1, 0)
-        add_sink(3)
-        scale_and_gate(1, 1)
+        add_sink(3, 4, half_y[3].unsqueeze(2))
+        gate_y(3)
+        invert(3, 4)
+        scale_gate(0)
+        for g in (1, 2):
+            for m in range(2):
+                scale_on_scalar(g, m)
         store(1)
-        invert(3)
-        scale_rows(2)
         store(2)
-        for m in range(2):
-            scale_and_gate(3, m)
+        times_y(0)
+        store(0)
+        scale_on_scalar(3, 0)
+        scale_on_vector(3, 1)
         store(3)

@@ -24,6 +24,7 @@ TILES = NQ // P
 PIECES = [[0], [1, 2], [3]]
 GROUPS = [[(0, 0), (1, 0)], [(1, 1), (1, 2)], [(0, 1), (0, 2)], [(0, 3)], [(1, 3)]]
 UNITS = [[(0, 0), (1, 0)], [(1, 1), (1, 2)], [(0, 1), (0, 2)], [(0, 3), (1, 3)]]
+Q_SCALAR = 48
 SCORE_BANKS = 3
 
 MANTISSA, SIGN, ONE, HALF = 0x007FFFFF, -0x80000000, 0x3F800000, 0x3F000000
@@ -104,9 +105,8 @@ def tile_rows_sink_gate_kernel(tc, qT, kT, t, v, sink, og, out):
         def quantise(codes, scales, words):
             nc.vector.quantize_mx(out=codes.bitcast(FP8X4), scales=scales, in_=words.rearrange("p n j -> p (n j)"))
 
-        def interleave(words, rows):
-            nc.vector.tensor_copy(out=words.rearrange("p (a b) j -> p a j b", b=RUN),
-                                  in_=rows.rearrange("p j (a b) -> p a j b", b=RUN))
+        def interleave(words, rows, copy=nc.vector.tensor_copy):
+            copy(out=words.rearrange("p (a b) j -> p a j b", b=RUN), in_=rows.rearrange("p j (a b) -> p a j b", b=RUN))
 
         def deal_keys(copy, r0, r1):
             copy(out=k_words[:, r0:r1].rearrange("p r s j -> p s j r"),
@@ -115,9 +115,8 @@ def tile_rows_sink_gate_kernel(tc, qT, kT, t, v, sink, og, out):
         def quantise_keys(r):
             quantise(k_codes[:, P * r:P * (r + 1)], k_scales[:, P * r:P * (r + 1)], k_words[:, r])
 
-        def interleave_queries(u, m):
-            cols = slice(P * m, P * (m + 1))
-            interleave(q_words[u][:, cols], q_raw[u][:, :, cols])
+        def interleave_queries(u, n0, n1, copy=nc.vector.tensor_copy):
+            interleave(q_words[u][:, n0:n1], q_raw[u][:, :, n0:n1], copy)
 
         def quantise_queries(u, m):
             cols = slice(P * m, P * (m + 1))
@@ -207,10 +206,10 @@ def tile_rows_sink_gate_kernel(tc, qT, kT, t, v, sink, og, out):
         for h in range(H):
             nc.sync.dma_start(out=v_raw[h][:], in_=v[h].rearrange("(s r) e -> s r e", r=PACK))
         load_queries(2)
-        for h in range(H):
-            nc.sync.dma_start(out=og_sb[:, h], in_=og[h].rearrange("(c p) e -> p c e", p=P))
         with nc.allow_non_contiguous_dma(reason="one sink a query, and a query tile has one query a partition"):
             nc.sync.dma_start(out=sinks[:], in_=sink.rearrange("h (c p) o -> p h (c o)", p=P))
+        for h in range(H):
+            nc.sync.dma_start(out=og_sb[:, h], in_=og[h].rearrange("(c p) e -> p c e", p=P))
 
         t_bits = t_sb[:].bitcast(I32)
         nc.vector.tensor_scalar(out=t_mantissa[:], in0=t_bits, scalar1=MANTISSA, scalar2=ONE,
@@ -227,13 +226,14 @@ def tile_rows_sink_gate_kernel(tc, qT, kT, t, v, sink, og, out):
 
         deal_keys(nc.vector.tensor_copy, 0, PACK // 2)
         deal_keys(nc.scalar.copy, PACK // 2, PACK)
-        interleave_queries(0, 0)
+        interleave_queries(0, 0, P)
         quantise_keys(0)
         quantise_queries(0, 0)
         for r in range(1, PACK):
             quantise_keys(r)
-        for m in range(2):
-            interleave_queries(1, m)
+        interleave_queries(1, 0, P)
+        interleave_queries(1, P, 2 * P - Q_SCALAR)
+        interleave_queries(1, 2 * P - Q_SCALAR, 2 * P, nc.scalar.copy)
         for m in range(2):
             quantise_queries(1, m)
 
@@ -254,7 +254,7 @@ def tile_rows_sink_gate_kernel(tc, qT, kT, t, v, sink, og, out):
 
         sign_values(0)
         sign_values(1)
-        interleave_queries(2, 0)
+        interleave_queries(2, 0, P)
         interleave_weights(0)
         quantise_queries(2, 0)
         quantise_values()
@@ -270,7 +270,6 @@ def tile_rows_sink_gate_kernel(tc, qT, kT, t, v, sink, og, out):
         quantise_weights(1)
         values(1)
         interleave_weights(2)
-        add_sink(0, 1, half_y[0].unsqueeze(2))
         for h in range(H):
             for r in range(PACK):
                 weights(h, 2, r)
@@ -278,8 +277,9 @@ def tile_rows_sink_gate_kernel(tc, qT, kT, t, v, sink, og, out):
             tanh_gate(g)
         quantise_weights(2)
         values(2)
-        invert(0, 1)
+        add_sink(0, 1, half_y[0].unsqueeze(2))
         interleave_weights(3)
+        invert(0, 1)
         interleave_weights(4)
         quantise_weights(3)
         add_sink(1, 3, y_banks[1][:])

@@ -92,15 +92,15 @@ def tile_rows_sink_gate_kernel(tc, qT, kT, t, v, sink, og, out):
         og_sb = sbuf("og_sb", [P, H, TILES, E], F32)
         tanh_og = per_unit("tanh_og", [P, 2, E], F32)
         between = per_unit("between", [P, 2, E], F32)
-        denom = sbuf("denom", [P, H, TILES], F32)
-        inverse = sbuf("inverse", [P, H, TILES], F32)
+        denom = sbuf("denom", [P, len(UNITS), 2], F32)
+        inverse = sbuf("inverse", [P, len(UNITS), 2], F32)
         result = per_unit("result", [P, 2, E], F32)
         unread = sbuf("unread", [P, 1], F32)
 
         score_banks = [[ps.tile([P, N], F32, name="score%d_%d" % (h, b)) for b in range(SCORE_BANKS)]
                        for h in range(H)]
         y_banks = [ps.tile([P, 2, 2, E], F32, name="y%d" % b) for b in range(2)]
-        half_y = [y_banks[0][:, 0], y_banks[1][:, 1], y_banks[1][:, 0], y_banks[0][:, 1]]
+        half_y = [y_banks[g % 2][:, g // 2] for g in range(len(UNITS))]
 
         def quantise(codes, scales, words):
             nc.vector.quantize_mx(out=codes.bitcast(FP8X4), scales=scales, in_=words.rearrange("p n j -> p (n j)"))
@@ -161,12 +161,12 @@ def tile_rows_sink_gate_kernel(tc, qT, kT, t, v, sink, og, out):
                                     rhs=v_codes[:, pair[0]].bitcast(FP8X4), rhs_scale=v_scales[:, pair[0]],
                                     start=True, stop=True)
 
-        def add_sink(c0, c1, sums):
-            nc.vector.scalar_tensor_tensor(out=denom[:, :, c0:c1], in0=sums[:, :, :, E - 1], scalar=2.0,
-                                           in1=sinks[:, :, c0:c1], op0=ALU.mult, op1=ALU.add)
+        def add_sink(g):
+            nc.vector.scalar_tensor_tensor(out=denom[:, g], in0=half_y[g][:, :, E - 1], scalar=2.0,
+                                           in1=of_unit(sinks[:], g), op0=ALU.mult, op1=ALU.add)
 
-        def invert(c0, c1):
-            nc.vector.reciprocal(out=inverse[:, :, c0:c1], in_=denom[:, :, c0:c1])
+        def invert(g0, g1):
+            nc.vector.reciprocal(out=inverse[:, g0:g1], in_=denom[:, g0:g1])
 
         def store(g):
             nc.sync.dma_start(out=of_unit(out.rearrange("h (c p) e -> p h c e", p=P), g), in_=result[g][:])
@@ -180,19 +180,11 @@ def tile_rows_sink_gate_kernel(tc, qT, kT, t, v, sink, og, out):
 
         def scale_on_scalar(g, m):
             nc.scalar.activation(out=result[g][:, m], in_=between[g][:, m], func=ACT.Copy,
-                                 scale=of_unit(inverse[:], g)[:, m:m + 1])
+                                 scale=inverse[:, g, m:m + 1])
 
         def scale_on_vector(g, m):
-            nc.vector.tensor_scalar(out=result[g][:, m], in0=between[g][:, m], scalar1=of_unit(inverse[:], g)[:, m:m + 1],
+            nc.vector.tensor_scalar(out=result[g][:, m], in0=between[g][:, m], scalar1=inverse[:, g, m:m + 1],
                                     scalar2=None, op0=ALU.mult)
-
-        def scale_gate(g):
-            for m in range(2):
-                nc.scalar.activation(out=between[g][:, m], in_=tanh_og[g][:, m], func=ACT.Identity,
-                                     scale=of_unit(inverse[:], g)[:, m:m + 1], bias=of_unit(inverse[:], g)[:, m:m + 1])
-
-        def times_y(g):
-            nc.vector.tensor_tensor(out=result[g][:], in0=half_y[g], in1=between[g][:], op=ALU.mult)
 
         q_hbm = qT.rearrange("h (p j) n -> (h p) j n", j=PACK)
 
@@ -208,7 +200,7 @@ def tile_rows_sink_gate_kernel(tc, qT, kT, t, v, sink, og, out):
         load_queries(2)
         with nc.allow_non_contiguous_dma(reason="one sink a query, and a query tile has one query a partition"):
             nc.sync.dma_start(out=sinks[:], in_=sink.rearrange("h (c p) o -> p h (c o)", p=P))
-        for h in range(H):
+        for h in (1, 0):
             nc.sync.dma_start(out=og_sb[:, h], in_=og[h].rearrange("(c p) e -> p c e", p=P))
 
         t_bits = t_sb[:].bitcast(I32)
@@ -270,36 +262,34 @@ def tile_rows_sink_gate_kernel(tc, qT, kT, t, v, sink, og, out):
         quantise_weights(1)
         values(1)
         interleave_weights(2)
+        add_sink(0)
         for h in range(H):
             for r in range(PACK):
                 weights(h, 2, r)
-        for g in (1, 2, 0, 3):
+        for g in (1, 0, 2, 3):
             tanh_gate(g)
+        interleave_weights(3)
+        add_sink(1)
         quantise_weights(2)
         values(2)
-        add_sink(0, 1, half_y[0].unsqueeze(2))
-        interleave_weights(3)
-        invert(0, 1)
-        interleave_weights(4)
         quantise_weights(3)
-        add_sink(1, 3, y_banks[1][:])
+        interleave_weights(4)
+        invert(0, 2)
+        gate_y(1)
         quantise_weights(4)
         values(3)
         values(4)
-        gate_y(1)
-        invert(1, 3)
+        add_sink(2)
+        gate_y(0)
+        invert(2, 3)
         gate_y(2)
-        add_sink(3, 4, half_y[3].unsqueeze(2))
+        add_sink(3)
         gate_y(3)
         invert(3, 4)
-        scale_gate(0)
-        for g in (1, 2):
+        for g in (1, 0, 2):
             for m in range(2):
                 scale_on_scalar(g, m)
-        store(1)
-        store(2)
-        times_y(0)
-        store(0)
+            store(g)
         scale_on_scalar(3, 0)
         scale_on_vector(3, 1)
         store(3)

@@ -19,12 +19,14 @@ P = 128
 ROWS = 64
 PACK = 4
 RUN = 4
+QUAD = 32
 TILES = NQ // P
 
 PIECES = [[0], [1, 2], [3]]
 GROUPS = [[(0, 0), (1, 0)], [(1, 1), (1, 2)], [(0, 1), (0, 2)], [(0, 3)], [(1, 3)]]
 UNITS = [[(0, 0), (1, 0)], [(1, 1), (1, 2)], [(0, 1), (0, 2)], [(0, 3), (1, 3)]]
 Q_SCALAR = 48
+SINK_STEP = QUAD // (H * TILES)
 SCORE_BANKS = 3
 
 MANTISSA, SIGN, ONE, HALF = 0x007FFFFF, -0x80000000, 0x3F800000, 0x3F000000
@@ -88,7 +90,9 @@ def tile_rows_sink_gate_kernel(tc, qT, kT, t, v, sink, og, out):
         ln_mantissa = sbuf("ln_mantissa", [P, PACK], F32)
         ln_power = sbuf("ln_power", [P, PACK], F32)
         ln_t = sbuf("ln_t", [P, PACK], F32)
-        sinks = sbuf("sinks", [P, H, TILES], F32)
+        sink_rows = sbuf("sink_rows", [P, QUAD], F32)
+        sink_cols = sbuf("sink_cols", [P, QUAD], F32)
+        sinks = sink_cols[:, 0:QUAD:SINK_STEP].rearrange("p (h c) -> p h c", h=H)
         og_sb = sbuf("og_sb", [P, H, TILES, E], F32)
         tanh_og = per_unit("tanh_og", [P, 2, E], F32)
         between = per_unit("between", [P, 2, E], F32)
@@ -163,7 +167,7 @@ def tile_rows_sink_gate_kernel(tc, qT, kT, t, v, sink, og, out):
 
         def add_sink(g):
             nc.vector.scalar_tensor_tensor(out=denom[:, g], in0=half_y[g][:, :, E - 1], scalar=2.0,
-                                           in1=of_unit(sinks[:], g), op0=ALU.mult, op1=ALU.add)
+                                           in1=of_unit(sinks, g), op0=ALU.mult, op1=ALU.add)
 
         def invert(g0, g1):
             nc.vector.reciprocal(out=inverse[:, g0:g1], in_=denom[:, g0:g1])
@@ -186,6 +190,7 @@ def tile_rows_sink_gate_kernel(tc, qT, kT, t, v, sink, og, out):
             nc.vector.tensor_scalar(out=result[g][:, m], in0=between[g][:, m], scalar1=inverse[:, g, m:m + 1],
                                     scalar2=None, op0=ALU.mult)
 
+        nc.vector.memset(sink_rows[:], 0.0)
         q_hbm = qT.rearrange("h (p j) n -> (h p) j n", j=PACK)
 
         def load_queries(u):
@@ -195,11 +200,11 @@ def tile_rows_sink_gate_kernel(tc, qT, kT, t, v, sink, og, out):
         nc.sync.dma_start(out=k_raw[:], in_=kT.rearrange("h (p j) n -> (h p) j n", j=PACK))
         load_queries(0)
         load_queries(1)
+        nc.sync.dma_start(out=sink_rows[0:P:SINK_STEP, :],
+                          in_=sink.rearrange("h (c a x) o -> a (h c) (x o)", a=P // QUAD, x=QUAD))
         for h in range(H):
             nc.sync.dma_start(out=v_raw[h][:], in_=v[h].rearrange("(s r) e -> s r e", r=PACK))
         load_queries(2)
-        with nc.allow_non_contiguous_dma(reason="one sink a query, and a query tile has one query a partition"):
-            nc.sync.dma_start(out=sinks[:], in_=sink.rearrange("h (c p) o -> p h (c o)", p=P))
         for h in (1, 0):
             nc.sync.dma_start(out=og_sb[:, h], in_=og[h].rearrange("(c p) e -> p c e", p=P))
 
@@ -244,6 +249,7 @@ def tile_rows_sink_gate_kernel(tc, qT, kT, t, v, sink, og, out):
             for h in range(H):
                 weights(h, 0, r)
 
+        nc.vector.transpose(out=sink_cols[:], in_=sink_rows[:])
         sign_values(0)
         sign_values(1)
         interleave_queries(2, 0, P)
@@ -290,6 +296,6 @@ def tile_rows_sink_gate_kernel(tc, qT, kT, t, v, sink, og, out):
             for m in range(2):
                 scale_on_scalar(g, m)
             store(g)
-        scale_on_scalar(3, 0)
-        scale_on_vector(3, 1)
+        for m in range(2):
+            scale_on_vector(3, m)
         store(3)

@@ -25,7 +25,7 @@ TILES = NQ // P
 PIECES = [[0], [1, 2], [3]]
 GROUPS = [[(0, 0), (1, 0)], [(1, 1), (1, 2)], [(0, 1), (0, 2)], [(0, 3)], [(1, 3)]]
 UNITS = [[(0, 0), (1, 0)], [(1, 1), (1, 2)], [(0, 1), (0, 2)], [(0, 3), (1, 3)]]
-Q_SCALAR = 48
+Q_SCALAR = 64
 SINK_STEP = QUAD // (H * TILES)
 SCORE_BANKS = 3
 
@@ -95,7 +95,7 @@ def tile_rows_sink_gate_kernel(tc, qT, kT, t, v, sink, og, out):
         sinks = sink_cols[:, 0:QUAD:SINK_STEP].rearrange("p (h c) -> p h c", h=H)
         og_sb = sbuf("og_sb", [P, H, TILES, E], F32)
         tanh_og = per_unit("tanh_og", [P, 2, E], F32)
-        between = per_unit("between", [P, 2, E], F32)
+        gated_y = per_unit("gated_y", [P, 2, E], F32)
         denom = sbuf("denom", [P, len(UNITS), 2], F32)
         inverse = sbuf("inverse", [P, len(UNITS), 2], F32)
         result = per_unit("result", [P, 2, E], F32)
@@ -116,8 +116,9 @@ def tile_rows_sink_gate_kernel(tc, qT, kT, t, v, sink, og, out):
             copy(out=k_words[:, r0:r1].rearrange("p r s j -> p s j r"),
                  in_=k_raw[:].rearrange("p j (s r) -> p s j r", r=PACK)[:, :, :, r0:r1])
 
-        def quantise_keys(r):
-            quantise(k_codes[:, P * r:P * (r + 1)], k_scales[:, P * r:P * (r + 1)], k_words[:, r])
+        def quantise_keys(r0, r1):
+            quantise(k_codes[:, P * r0:P * r1], k_scales[:, P * r0:P * r1],
+                     k_words[:, r0:r1].rearrange("p r s j -> p (r s) j"))
 
         def interleave_queries(u, n0, n1, copy=nc.vector.tensor_copy):
             interleave(q_words[u][:, n0:n1], q_raw[u][:, :, n0:n1], copy)
@@ -179,16 +180,13 @@ def tile_rows_sink_gate_kernel(tc, qT, kT, t, v, sink, og, out):
             nc.scalar.activation(out=tanh_og[g][:], in_=of_unit(og_sb[:], g), func=ACT.Tanh, scale=0.5)
 
         def gate_y(g):
-            nc.vector.scalar_tensor_tensor(out=between[g][:], in0=tanh_og[g][:], scalar=1.0, in1=half_y[g],
+            nc.vector.scalar_tensor_tensor(out=gated_y[g][:], in0=tanh_og[g][:], scalar=1.0, in1=half_y[g],
                                            op0=ALU.add, op1=ALU.mult)
 
-        def scale_on_scalar(g, m):
-            nc.scalar.activation(out=result[g][:, m], in_=between[g][:, m], func=ACT.Copy,
-                                 scale=inverse[:, g, m:m + 1])
-
-        def scale_on_vector(g, m):
-            nc.vector.tensor_scalar(out=result[g][:, m], in0=between[g][:, m], scalar1=inverse[:, g, m:m + 1],
-                                    scalar2=None, op0=ALU.mult)
+        def scale_on_scalar(g):
+            for m in range(2):
+                nc.scalar.activation(out=result[g][:, m], in_=gated_y[g][:, m], func=ACT.Copy,
+                                     scale=inverse[:, g, m:m + 1])
 
         nc.vector.memset(sink_rows[:], 0.0)
         q_hbm = qT.rearrange("h (p j) n -> (h p) j n", j=PACK)
@@ -224,15 +222,16 @@ def tile_rows_sink_gate_kernel(tc, qT, kT, t, v, sink, og, out):
         deal_keys(nc.vector.tensor_copy, 0, PACK // 2)
         deal_keys(nc.scalar.copy, PACK // 2, PACK)
         interleave_queries(0, 0, P)
-        quantise_keys(0)
+        quantise_keys(0, 1)
         quantise_queries(0, 0)
-        for r in range(1, PACK):
-            quantise_keys(r)
+        quantise_keys(1, 2)
+        quantise_keys(2, PACK)
         interleave_queries(1, 0, P)
         interleave_queries(1, P, 2 * P - Q_SCALAR)
         interleave_queries(1, 2 * P - Q_SCALAR, 2 * P, nc.scalar.copy)
-        for m in range(2):
-            quantise_queries(1, m)
+        quantise_queries(1, 0)
+        nc.vector.transpose(out=sink_cols[:], in_=sink_rows[:])
+        quantise_queries(1, 1)
 
         for r in range(PACK):
             for h in range(H):
@@ -249,7 +248,6 @@ def tile_rows_sink_gate_kernel(tc, qT, kT, t, v, sink, og, out):
             for h in range(H):
                 weights(h, 0, r)
 
-        nc.vector.transpose(out=sink_cols[:], in_=sink_rows[:])
         sign_values(0)
         sign_values(1)
         interleave_queries(2, 0, P)
@@ -272,6 +270,7 @@ def tile_rows_sink_gate_kernel(tc, qT, kT, t, v, sink, og, out):
         for h in range(H):
             for r in range(PACK):
                 weights(h, 2, r)
+
         for g in (1, 0, 2, 3):
             tanh_gate(g)
         interleave_weights(3)
@@ -293,9 +292,10 @@ def tile_rows_sink_gate_kernel(tc, qT, kT, t, v, sink, og, out):
         gate_y(3)
         invert(3, 4)
         for g in (1, 0, 2):
-            for m in range(2):
-                scale_on_scalar(g, m)
+            scale_on_scalar(g)
             store(g)
+        out_tiles = of_unit(out.rearrange("h (c p) e -> p h c e", p=P), 3)
         for m in range(2):
-            scale_on_vector(3, m)
-        store(3)
+            nc.vector.tensor_scalar(out=result[3][:, m], in0=gated_y[3][:, m], scalar1=inverse[:, 3, m:m + 1],
+                                    scalar2=None, op0=ALU.mult)
+            nc.sync.dma_start(out=out_tiles[:, m], in_=result[3][:, m])

@@ -25,7 +25,6 @@ TILES = NQ // P
 PIECES = [[0], [1, 2], [3]]
 GROUPS = [[(0, 0), (1, 0)], [(1, 1), (1, 2)], [(0, 1), (0, 2)], [(0, 3)], [(1, 3)]]
 UNITS = [[(0, 0), (1, 0)], [(1, 1), (1, 2)], [(0, 1), (0, 2)], [(0, 3), (1, 3)]]
-Q_SCALAR = 64
 SINK_STEP = QUAD // (H * TILES)
 SCORE_BANKS = 3
 
@@ -57,8 +56,8 @@ def tile_rows_sink_gate_kernel(tc, qT, kT, t, v, sink, og, out):
         def sbuf(name, shape, dtype):
             return sb.tile(shape, dtype, name=name, align_bytes=64)
 
-        def per_piece(name, shape, dtype):
-            return [sbuf("%s%d" % (name, u), shape(P * len(tiles)), dtype) for u, tiles in enumerate(PIECES)]
+        def per_tile(name, shape, dtype):
+            return [sbuf("%s%d" % (name, c), shape, dtype) for c in range(TILES)]
 
         def per_group(name, shape, dtype):
             return [sbuf("%s%d" % (name, g), shape(P * len(pairs)), dtype) for g, pairs in enumerate(GROUPS)]
@@ -70,10 +69,10 @@ def tile_rows_sink_gate_kernel(tc, qT, kT, t, v, sink, og, out):
         k_words = sbuf("k_words", [P, PACK, P, PACK], BF16)
         k_codes = sbuf("k_codes", [P, N], U32)
         k_scales = sbuf("k_scales", [P, N], U8)
-        q_raw = per_piece("q_raw", lambda n: [P, PACK, n], F32)
-        q_words = per_piece("q_words", lambda n: [P, n, PACK], BF16)
-        q_codes = per_piece("q_codes", lambda n: [P, n], U32)
-        q_scales = per_piece("q_scales", lambda n: [P, n], U8)
+        q_raw = per_tile("q_raw", [P, PACK, P], F32)
+        q_words = per_tile("q_words", [P, P, PACK], BF16)
+        q_codes = per_tile("q_codes", [P, P], U32)
+        q_scales = per_tile("q_scales", [P, P], U8)
         v_raw = [sbuf("v_raw%d" % h, [P, PACK, E], F32) for h in range(H)]
         v_words = sbuf("v_words", [P, H, E, PACK], BF16)
         v_codes = sbuf("v_codes", [P, H, E], U32)
@@ -120,12 +119,11 @@ def tile_rows_sink_gate_kernel(tc, qT, kT, t, v, sink, og, out):
             quantise(k_codes[:, P * r0:P * r1], k_scales[:, P * r0:P * r1],
                      k_words[:, r0:r1].rearrange("p r s j -> p (r s) j"))
 
-        def interleave_queries(u, n0, n1, copy=nc.vector.tensor_copy):
-            interleave(q_words[u][:, n0:n1], q_raw[u][:, :, n0:n1], copy)
+        def interleave_queries(c, copy=nc.vector.tensor_copy):
+            interleave(q_words[c][:], q_raw[c][:], copy)
 
-        def quantise_queries(u, m):
-            cols = slice(P * m, P * (m + 1))
-            quantise(q_codes[u][:, cols], q_scales[u][:, cols], q_words[u][:, cols])
+        def quantise_queries(c):
+            quantise(q_codes[c][:], q_scales[c][:], q_words[c][:])
 
         def quantise_values():
             quantise(v_codes[:].rearrange("p h e -> p (h e)"), v_scales[:].rearrange("p h e -> p (h e)"),
@@ -137,11 +135,11 @@ def tile_rows_sink_gate_kernel(tc, qT, kT, t, v, sink, og, out):
                                     in0=v_raw[h][:].rearrange("p r (a b) -> p a r b", b=RUN), in1=factor, op=ALU.mult)
 
         def scores(h, u, r, m=0):
-            rows, keys, cols = slice(ROWS * h, ROWS * (h + 1)), slice(P * r, P * (r + 1)), slice(P * m, P * (m + 1))
+            rows, keys, c = slice(ROWS * h, ROWS * (h + 1)), slice(P * r, P * (r + 1)), PIECES[u][m]
             bank, first = score_place(u, r)
             nc.tensor.matmul_mx(out=score_banks[h][bank][:, first + P * m:first + P * (m + 1)],
                                 lhsT=k_codes[rows, keys].bitcast(FP8X4), lhsT_scale=k_scales[rows, keys],
-                                rhs=q_codes[u][rows, cols].bitcast(FP8X4), rhs_scale=q_scales[u][rows, cols],
+                                rhs=q_codes[c][rows].bitcast(FP8X4), rhs_scale=q_scales[c][rows],
                                 start=True, stop=True)
 
         def weights(h, u, r):
@@ -191,18 +189,19 @@ def tile_rows_sink_gate_kernel(tc, qT, kT, t, v, sink, og, out):
         nc.vector.memset(sink_rows[:], 0.0)
         q_hbm = qT.rearrange("h (p j) n -> (h p) j n", j=PACK)
 
-        def load_queries(u):
-            nc.sync.dma_start(out=q_raw[u][:], in_=q_hbm[:, :, P * PIECES[u][0]:P * (PIECES[u][-1] + 1)])
+        def load_queries(c):
+            nc.sync.dma_start(out=q_raw[c][:], in_=q_hbm[:, :, P * c:P * (c + 1)])
 
         nc.sync.dma_start(out=t_sb[:], in_=t.rearrange("(s r) o -> s (r o)", r=PACK))
         nc.sync.dma_start(out=k_raw[:], in_=kT.rearrange("h (p j) n -> (h p) j n", j=PACK))
         load_queries(0)
         load_queries(1)
+        load_queries(2)
         nc.sync.dma_start(out=sink_rows[0:P:SINK_STEP, :],
                           in_=sink.rearrange("h (c a x) o -> a (h c) (x o)", a=P // QUAD, x=QUAD))
         for h in range(H):
             nc.sync.dma_start(out=v_raw[h][:], in_=v[h].rearrange("(s r) e -> s r e", r=PACK))
-        load_queries(2)
+        load_queries(3)
         for h in (1, 0):
             nc.sync.dma_start(out=og_sb[:, h], in_=og[h].rearrange("(c p) e -> p c e", p=P))
 
@@ -221,17 +220,16 @@ def tile_rows_sink_gate_kernel(tc, qT, kT, t, v, sink, og, out):
 
         deal_keys(nc.vector.tensor_copy, 0, PACK // 2)
         deal_keys(nc.scalar.copy, PACK // 2, PACK)
-        interleave_queries(0, 0, P)
+        interleave_queries(0)
         quantise_keys(0, 1)
-        quantise_queries(0, 0)
+        quantise_queries(0)
         quantise_keys(1, 2)
         quantise_keys(2, PACK)
-        interleave_queries(1, 0, P)
-        interleave_queries(1, P, 2 * P - Q_SCALAR)
-        interleave_queries(1, 2 * P - Q_SCALAR, 2 * P, nc.scalar.copy)
-        quantise_queries(1, 0)
+        interleave_queries(1, copy=nc.scalar.copy)
+        interleave_queries(2)
+        quantise_queries(1)
         nc.vector.transpose(out=sink_cols[:], in_=sink_rows[:])
-        quantise_queries(1, 1)
+        quantise_queries(2)
 
         for r in range(PACK):
             for h in range(H):
@@ -250,9 +248,9 @@ def tile_rows_sink_gate_kernel(tc, qT, kT, t, v, sink, og, out):
 
         sign_values(0)
         sign_values(1)
-        interleave_queries(2, 0, P)
+        interleave_queries(3)
         interleave_weights(0)
-        quantise_queries(2, 0)
+        quantise_queries(3)
         quantise_values()
         for h in range(H):
             for r in range(PACK):

@@ -292,8 +292,7 @@ def tile_rows_sink_gate_kernel(tc, qT, kT, t, v, sink, og, out):
         for g in (1, 0, 2):
             scale_on_scalar(g)
             store(g)
-        out_tiles = of_unit(out.rearrange("h (c p) e -> p h c e", p=P), 3)
         for m in range(2):
             nc.vector.tensor_scalar(out=result[3][:, m], in0=gated_y[3][:, m], scalar1=inverse[:, 3, m:m + 1],
                                     scalar2=None, op0=ALU.mult)
-            nc.sync.dma_start(out=out_tiles[:, m], in_=result[3][:, m])
+        store(3)

@@ -30,6 +30,10 @@ SCORE_BANKS = 3
 
 MANTISSA, SIGN, ONE, HALF = 0x007FFFFF, -0x80000000, 0x3F800000, 0x3F000000
 MANTISSA_BITS, EXPONENT, EXPONENT_BIAS = 23, 0xFF, 127
+ODD = [11, 9, 7, 5, 3, 1]
+COMMON = 3465
+STEPS = 8
+SQRT2 = math.sqrt(2.0)
 
 
 def score_place(piece, r):
@@ -86,9 +90,13 @@ def tile_rows_sink_gate_kernel(tc, qT, kT, t, v, sink, og, out):
         t_mantissa = sbuf("t_mantissa", [P, PACK], I32)
         t_exponent = sbuf("t_exponent", [P, PACK], I32)
         half_sign = sbuf("half_sign", [P, PACK], I32)
-        ln_mantissa = sbuf("ln_mantissa", [P, PACK], F32)
-        ln_power = sbuf("ln_power", [P, PACK], F32)
-        ln_t = sbuf("ln_t", [P, PACK], F32)
+        shifted = sbuf("shifted", [P, PACK], F32)
+        inv_shifted = sbuf("inv_shifted", [P, PACK], F32)
+        z = sbuf("z", [P, PACK], F32)
+        factors = sbuf("factors", [P, PACK, STEPS], F32)
+        terms = sbuf("terms", [P, PACK, STEPS], F32)
+        sums = sbuf("sums", [P, PACK, STEPS], F32)
+        ln_t = sums[:, :, STEPS - 1]
         sink_rows = sbuf("sink_rows", [P, QUAD], F32)
         sink_cols = sbuf("sink_cols", [P, QUAD], F32)
         sinks = sink_cols[:, 0:QUAD:SINK_STEP].rearrange("p (h c) -> p h c", h=H)
@@ -98,7 +106,6 @@ def tile_rows_sink_gate_kernel(tc, qT, kT, t, v, sink, og, out):
         denom = sbuf("denom", [P, len(UNITS), 2], F32)
         inverse = sbuf("inverse", [P, len(UNITS), 2], F32)
         result = per_unit("result", [P, 2, E], F32)
-        unread = sbuf("unread", [P, 1], F32)
 
         score_banks = [[ps.tile([P, N], F32, name="score%d_%d" % (h, b)) for b in range(SCORE_BANKS)]
                        for h in range(H)]
@@ -110,6 +117,9 @@ def tile_rows_sink_gate_kernel(tc, qT, kT, t, v, sink, og, out):
 
         def interleave(words, rows, copy=nc.vector.tensor_copy):
             copy(out=words.rearrange("p (a b) j -> p a j b", b=RUN), in_=rows.rearrange("p j (a b) -> p a j b", b=RUN))
+
+        def scalar_copy(out, in_):
+            nc.scalar.activation(out=out, in_=in_, func=ACT.Copy)
 
         def deal_keys(copy, r0, r1):
             copy(out=k_words[:, r0:r1].rearrange("p r s j -> p s j r"),
@@ -168,6 +178,11 @@ def tile_rows_sink_gate_kernel(tc, qT, kT, t, v, sink, og, out):
             nc.vector.scalar_tensor_tensor(out=denom[:, g], in0=half_y[g][:, :, E - 1], scalar=2.0,
                                            in1=of_unit(sinks, g), op0=ALU.mult, op1=ALU.add)
 
+        def add_sink_on_scalar(g):
+            for m in range(2):
+                nc.scalar.activation(out=denom[:, g, m:m + 1], in_=half_y[g][:, m, E - 1:E], func=ACT.Identity,
+                                     scale=2.0, bias=of_unit(sinks, g)[:, m:m + 1])
+
         def invert(g0, g1):
             nc.vector.reciprocal(out=inverse[:, g0:g1], in_=denom[:, g0:g1])
 
@@ -187,6 +202,10 @@ def tile_rows_sink_gate_kernel(tc, qT, kT, t, v, sink, og, out):
                                      scale=inverse[:, g, m:m + 1])
 
         nc.vector.memset(sink_rows[:], 0.0)
+        nc.vector.memset(factors[:, :, 0:2], 0.0)
+        nc.vector.memset(terms[:, :, 0:1], 0.0)
+        for step, odd in enumerate(ODD):
+            nc.vector.memset(terms[:, :, step + 1:step + 2], float(COMMON // odd))
         q_hbm = qT.rearrange("h (p j) n -> (h p) j n", j=PACK)
 
         def load_queries(c):
@@ -212,14 +231,24 @@ def tile_rows_sink_gate_kernel(tc, qT, kT, t, v, sink, og, out):
                                 op0=ALU.logical_shift_right, op1=ALU.bitwise_and)
         nc.vector.tensor_scalar(out=half_sign[:], in0=t_bits, scalar1=SIGN, scalar2=HALF,
                                 op0=ALU.bitwise_and, op1=ALU.bitwise_or)
-        nc.scalar.activation(out=ln_mantissa[:], in_=t_mantissa[:].bitcast(F32), func=ACT.Ln)
-        nc.scalar.activation(out=unread[:], in_=ln_mantissa[:, 0:1], func=ACT.Exp)
-        nc.vector.tensor_scalar(out=ln_power[:], in0=t_exponent[:], scalar1=-float(EXPONENT_BIAS),
+        nc.vector.tensor_scalar(out=shifted[:], in0=t_mantissa[:].bitcast(F32), scalar1=SQRT2, scalar2=None,
+                                op0=ALU.add)
+        nc.vector.tensor_scalar(out=terms[:, :, STEPS - 1], in0=t_exponent[:], scalar1=0.5 - EXPONENT_BIAS,
                                 scalar2=math.log(2.0), op0=ALU.add, op1=ALU.mult)
-        nc.vector.tensor_tensor(out=ln_t[:], in0=ln_power[:], in1=ln_mantissa[:], op=ALU.add)
+        nc.vector.reciprocal(out=inv_shifted[:], in_=shifted[:])
+        nc.vector.tensor_scalar(out=z[:], in0=inv_shifted[:], scalar1=-2.0 * SQRT2, scalar2=1.0,
+                                op0=ALU.mult, op1=ALU.add)
+        nc.vector.tensor_scalar(out=factors[:, :, STEPS - 1], in0=inv_shifted[:], scalar1=-4.0 * SQRT2 / COMMON,
+                                scalar2=2.0 / COMMON, op0=ALU.mult, op1=ALU.add)
+        z_wide = z[:].unsqueeze(2).to_broadcast([P, PACK, len(ODD) - 1])
+        nc.vector.tensor_tensor(out=factors[:, :, 2:STEPS - 1], in0=z_wide, in1=z_wide, op=ALU.mult)
+        nc.vector.tensor_tensor_scan(out=sums[:].rearrange("p r k -> p (r k)"),
+                                     data0=factors[:].rearrange("p r k -> p (r k)"),
+                                     data1=terms[:].rearrange("p r k -> p (r k)"),
+                                     initial=0.0, op0=ALU.mult, op1=ALU.add)
 
         deal_keys(nc.vector.tensor_copy, 0, PACK // 2)
-        deal_keys(nc.scalar.copy, PACK // 2, PACK)
+        deal_keys(scalar_copy, PACK // 2, PACK)
         interleave_queries(0)
         quantise_keys(0, 1)
         quantise_queries(0)
@@ -249,9 +278,9 @@ def tile_rows_sink_gate_kernel(tc, qT, kT, t, v, sink, og, out):
         sign_values(0)
         sign_values(1)
         interleave_queries(3)
-        interleave_weights(0)
-        quantise_queries(3)
         quantise_values()
+        quantise_queries(3)
+        interleave_weights(0)
         for h in range(H):
             for r in range(PACK):
                 scores(h, 2, r)
@@ -264,15 +293,15 @@ def tile_rows_sink_gate_kernel(tc, qT, kT, t, v, sink, og, out):
         quantise_weights(1)
         values(1)
         interleave_weights(2)
-        add_sink(0)
         for h in range(H):
             for r in range(PACK):
                 weights(h, 2, r)
 
+        add_sink_on_scalar(0)
+        add_sink_on_scalar(1)
         for g in (1, 0, 2, 3):
             tanh_gate(g)
         interleave_weights(3)
-        add_sink(1)
         quantise_weights(2)
         values(2)
         quantise_weights(3)

@@ -32,16 +32,16 @@ MANTISSA, SIGN, ONE, HALF = 0x007FFFFF, -0x80000000, 0x3F800000, 0x3F000000
 MANTISSA_BITS, EXPONENT, EXPONENT_BIAS = 23, 0xFF, 127
 ODD = [11, 9, 7, 5, 3, 1]
 COMMON = 3465
-STEPS = 8
+STEPS = len(ODD) + 1
 SQRT2 = math.sqrt(2.0)
 
 
-def score_place(piece, r):
+def score_place(h, piece, r):
     if piece == 0:
-        return [(0, 0), (1, 0), (2, 0), (2, P)][r]
+        return (r // 2, P * (r % 2)) if h else (min(r, 2), P * (r // 3))
     if piece == 1:
-        return r // 2, 2 * P * (r % 2)
-    return 2, P * r
+        return (2 * (1 - r // 2) if h else r // 2), 2 * P * (r % 2)
+    return 2 - h, P * r
 
 
 def of_unit(view, g):
@@ -146,7 +146,7 @@ def tile_rows_sink_gate_kernel(tc, qT, kT, t, v, sink, og, out):
 
         def scores(h, u, r, m=0):
             rows, keys, c = slice(ROWS * h, ROWS * (h + 1)), slice(P * r, P * (r + 1)), PIECES[u][m]
-            bank, first = score_place(u, r)
+            bank, first = score_place(h, u, r)
             nc.tensor.matmul_mx(out=score_banks[h][bank][:, first + P * m:first + P * (m + 1)],
                                 lhsT=k_codes[rows, keys].bitcast(FP8X4), lhsT_scale=k_scales[rows, keys],
                                 rhs=q_codes[c][rows].bitcast(FP8X4), rhs_scale=q_scales[c][rows],
@@ -155,7 +155,7 @@ def tile_rows_sink_gate_kernel(tc, qT, kT, t, v, sink, og, out):
         def weights(h, u, r):
             g = [(h, PIECES[u][0]) in members for members in GROUPS].index(True)
             n0, n = P * GROUPS[g].index((h, PIECES[u][0])), P * len(PIECES[u])
-            bank, first = score_place(u, r)
+            bank, first = score_place(h, u, r)
             nc.scalar.activation(out=w_rows[g][:, r, n0:n0 + n], in_=score_banks[h][bank][:, first:first + n],
                                  func=ACT.Exp, bias=ln_t[:, r:r + 1])
 
@@ -196,16 +196,18 @@ def tile_rows_sink_gate_kernel(tc, qT, kT, t, v, sink, og, out):
             nc.vector.scalar_tensor_tensor(out=gated_y[g][:], in0=tanh_og[g][:], scalar=1.0, in1=half_y[g],
                                            op0=ALU.add, op1=ALU.mult)
 
-        def scale_on_scalar(g):
-            for m in range(2):
-                nc.scalar.activation(out=result[g][:, m], in_=gated_y[g][:, m], func=ACT.Copy,
-                                     scale=inverse[:, g, m:m + 1])
+        def scale_on_scalar(g, m):
+            nc.scalar.activation(out=result[g][:, m], in_=gated_y[g][:, m], func=ACT.Copy,
+                                 scale=inverse[:, g, m:m + 1])
+
+        def scale_on_vector(g, m):
+            nc.vector.tensor_scalar(out=result[g][:, m], in0=gated_y[g][:, m], scalar1=inverse[:, g, m:m + 1],
+                                    scalar2=None, op0=ALU.mult)
 
         nc.vector.memset(sink_rows[:], 0.0)
-        nc.vector.memset(factors[:, :, 0:2], 0.0)
-        nc.vector.memset(terms[:, :, 0:1], 0.0)
+        nc.vector.memset(factors[:, :, 0:1], 0.0)
         for step, odd in enumerate(ODD):
-            nc.vector.memset(terms[:, :, step + 1:step + 2], float(COMMON // odd))
+            nc.vector.memset(terms[:, :, step:step + 1], float(COMMON // odd))
         q_hbm = qT.rearrange("h (p j) n -> (h p) j n", j=PACK)
 
         def load_queries(c):
@@ -241,7 +243,7 @@ def tile_rows_sink_gate_kernel(tc, qT, kT, t, v, sink, og, out):
         nc.vector.tensor_scalar(out=factors[:, :, STEPS - 1], in0=inv_shifted[:], scalar1=-4.0 * SQRT2 / COMMON,
                                 scalar2=2.0 / COMMON, op0=ALU.mult, op1=ALU.add)
         z_wide = z[:].unsqueeze(2).to_broadcast([P, PACK, len(ODD) - 1])
-        nc.vector.tensor_tensor(out=factors[:, :, 2:STEPS - 1], in0=z_wide, in1=z_wide, op=ALU.mult)
+        nc.vector.tensor_tensor(out=factors[:, :, 1:STEPS - 1], in0=z_wide, in1=z_wide, op=ALU.mult)
         nc.vector.tensor_tensor_scan(out=sums[:].rearrange("p r k -> p (r k)"),
                                      data0=factors[:].rearrange("p r k -> p (r k)"),
                                      data1=terms[:].rearrange("p r k -> p (r k)"),
@@ -263,8 +265,8 @@ def tile_rows_sink_gate_kernel(tc, qT, kT, t, v, sink, og, out):
         for r in range(PACK):
             for h in range(H):
                 scores(h, 0, r)
-        for r in range(PACK // 2):
-            for h in range(H):
+        for h in range(H):
+            for r in range(PACK // 2):
                 weights(h, 0, r)
         for h in (1, 0):
             for pair in range(2):
@@ -319,9 +321,9 @@ def tile_rows_sink_gate_kernel(tc, qT, kT, t, v, sink, og, out):
         gate_y(3)
         invert(3, 4)
         for g in (1, 0, 2):
-            scale_on_scalar(g)
+            for m in range(2):
+                scale_on_scalar(g, m)
             store(g)
         for m in range(2):
-            nc.vector.tensor_scalar(out=result[3][:, m], in0=gated_y[3][:, m], scalar1=inverse[:, 3, m:m + 1],
-                                    scalar2=None, op0=ALU.mult)
+            scale_on_vector(3, m)
         store(3)

@@ -23,8 +23,8 @@ QUAD = 32
 TILES = NQ // P
 
 PIECES = [[0], [1, 2], [3]]
-GROUPS = [[(0, 0), (1, 0)], [(1, 1), (1, 2)], [(0, 1), (0, 2)], [(0, 3)], [(1, 3)]]
-UNITS = [[(0, 0), (1, 0)], [(1, 1), (1, 2)], [(0, 1), (0, 2)], [(0, 3), (1, 3)]]
+GROUPS = [[(0, 0), (1, 0)], [(0, 1), (0, 2)], [(1, 1), (1, 2)], [(0, 3)], [(1, 3)]]
+UNITS = [[(0, 0), (1, 0)], [(0, 1), (0, 2)], [(1, 1), (1, 2)], [(0, 3), (1, 3)]]
 SINK_STEP = QUAD // (H * TILES)
 SCORE_BANKS = 3
 
@@ -37,11 +37,12 @@ SQRT2 = math.sqrt(2.0)
 
 
 def score_place(h, piece, r):
-    if piece == 0:
-        return (r // 2, P * (r % 2)) if h else (min(r, 2), P * (r // 3))
+    width = P * len(PIECES[piece])
+    if piece == 0 or (piece, h) == (1, 0):
+        return min(r, 2), width * (r // 3)
     if piece == 1:
-        return (2 * (1 - r // 2) if h else r // 2), 2 * P * (r % 2)
-    return 2 - h, P * r
+        return r // 2, width * (r % 2)
+    return 2 * h, width * r
 
 
 def of_unit(view, g):
@@ -159,8 +160,9 @@ def tile_rows_sink_gate_kernel(tc, qT, kT, t, v, sink, og, out):
             nc.scalar.activation(out=w_rows[g][:, r, n0:n0 + n], in_=score_banks[h][bank][:, first:first + n],
                                  func=ACT.Exp, bias=ln_t[:, r:r + 1])
 
-        def interleave_weights(g):
-            interleave(w_words[g][:], w_rows[g][:])
+        def interleave_weights(g, m0=0, m1=None):
+            cols = slice(P * m0, P * (len(GROUPS[g]) if m1 is None else m1))
+            interleave(w_words[g][:, cols], w_rows[g][:, :, cols])
 
         def quantise_weights(g):
             quantise(w_codes[g][:], w_scales[g][:], w_words[g][:])
@@ -223,7 +225,7 @@ def tile_rows_sink_gate_kernel(tc, qT, kT, t, v, sink, og, out):
         for h in range(H):
             nc.sync.dma_start(out=v_raw[h][:], in_=v[h].rearrange("(s r) e -> s r e", r=PACK))
         load_queries(3)
-        for h in (1, 0):
+        for h in range(H):
             nc.sync.dma_start(out=og_sb[:, h], in_=og[h].rearrange("(c p) e -> p c e", p=P))
 
         t_bits = t_sb[:].bitcast(I32)
@@ -262,32 +264,34 @@ def tile_rows_sink_gate_kernel(tc, qT, kT, t, v, sink, og, out):
         nc.vector.transpose(out=sink_cols[:], in_=sink_rows[:])
         quantise_queries(2)
 
-        for r in range(PACK):
-            for h in range(H):
-                scores(h, 0, r)
+        first_piece = [(0, 0), (1, 0), (0, 1), (1, 1), (0, 2), (0, 3), (1, 2), (1, 3)]
+        for h, r in first_piece:
+            scores(h, 0, r)
+        for h, r in first_piece[:6]:
+            weights(h, 0, r)
+        for m in range(2):
+            for r in range(2):
+                scores(0, 1, r, m)
         for h in range(H):
-            for r in range(PACK // 2):
-                weights(h, 0, r)
-        for h in (1, 0):
-            for pair in range(2):
+            for r in range(2 - 2 * h, PACK):
                 for m in range(2):
-                    for r in (2 * pair, 2 * pair + 1):
-                        scores(h, 1, r, m)
-        for r in range(PACK // 2, PACK):
-            for h in range(H):
-                weights(h, 0, r)
+                    scores(h, 1, r, m)
+        for h, r in first_piece[6:]:
+            weights(h, 0, r)
 
         sign_values(0)
         sign_values(1)
+        interleave_weights(0, 0, 1)
         interleave_queries(3)
         quantise_values()
         quantise_queries(3)
-        interleave_weights(0)
+        interleave_weights(0, 1, 2)
+        weights(0, 1, 0)
         for h in range(H):
             for r in range(PACK):
                 scores(h, 2, r)
-        for h in (1, 0):
-            for r in range(PACK):
+        for h in range(H):
+            for r in range(1 - h, PACK):
                 weights(h, 1, r)
         interleave_weights(1)
         quantise_weights(0)

@@ -26,6 +26,7 @@ PIECES = [[0], [1, 2], [3]]
 GROUPS = [[(0, 0), (1, 0)], [(0, 1), (0, 2)], [(1, 1), (1, 2)], [(0, 3)], [(1, 3)]]
 UNITS = [[(0, 0), (1, 0)], [(0, 1), (0, 2)], [(1, 1), (1, 2)], [(0, 3), (1, 3)]]
 SINK_STEP = QUAD // (H * TILES)
+SCALAR_SHARE = 64
 SCORE_BANKS = 3
 
 MANTISSA, SIGN, ONE, HALF = 0x007FFFFF, -0x80000000, 0x3F800000, 0x3F000000
@@ -160,9 +161,8 @@ def tile_rows_sink_gate_kernel(tc, qT, kT, t, v, sink, og, out):
             nc.scalar.activation(out=w_rows[g][:, r, n0:n0 + n], in_=score_banks[h][bank][:, first:first + n],
                                  func=ACT.Exp, bias=ln_t[:, r:r + 1])
 
-        def interleave_weights(g, m0=0, m1=None):
-            cols = slice(P * m0, P * (len(GROUPS[g]) if m1 is None else m1))
-            interleave(w_words[g][:, cols], w_rows[g][:, :, cols])
+        def interleave_weights(g, n0=0, n1=None, copy=nc.vector.tensor_copy):
+            interleave(w_words[g][:, n0:n1], w_rows[g][:, :, n0:n1], copy)
 
         def quantise_weights(g):
             quantise(w_codes[g][:], w_scales[g][:], w_words[g][:])
@@ -215,6 +215,9 @@ def tile_rows_sink_gate_kernel(tc, qT, kT, t, v, sink, og, out):
         def load_queries(c):
             nc.sync.dma_start(out=q_raw[c][:], in_=q_hbm[:, :, P * c:P * (c + 1)])
 
+        def load_values(h):
+            nc.sync.dma_start(out=v_raw[h][:], in_=v[h].rearrange("(s r) e -> s r e", r=PACK))
+
         nc.sync.dma_start(out=t_sb[:], in_=t.rearrange("(s r) o -> s (r o)", r=PACK))
         nc.sync.dma_start(out=k_raw[:], in_=kT.rearrange("h (p j) n -> (h p) j n", j=PACK))
         load_queries(0)
@@ -222,9 +225,9 @@ def tile_rows_sink_gate_kernel(tc, qT, kT, t, v, sink, og, out):
         load_queries(2)
         nc.sync.dma_start(out=sink_rows[0:P:SINK_STEP, :],
                           in_=sink.rearrange("h (c a x) o -> a (h c) (x o)", a=P // QUAD, x=QUAD))
-        for h in range(H):
-            nc.sync.dma_start(out=v_raw[h][:], in_=v[h].rearrange("(s r) e -> s r e", r=PACK))
+        load_values(0)
         load_queries(3)
+        load_values(1)
         for h in range(H):
             nc.sync.dma_start(out=og_sb[:, h], in_=og[h].rearrange("(c p) e -> p c e", p=P))
 
@@ -278,14 +281,15 @@ def tile_rows_sink_gate_kernel(tc, qT, kT, t, v, sink, og, out):
                     scores(h, 1, r, m)
         for h, r in first_piece[6:]:
             weights(h, 0, r)
+        interleave_weights(0, 0, SCALAR_SHARE, nc.scalar.copy)
 
         sign_values(0)
-        sign_values(1)
-        interleave_weights(0, 0, 1)
+        interleave_weights(0, SCALAR_SHARE, P)
         interleave_queries(3)
-        quantise_values()
+        interleave_weights(0, P)
         quantise_queries(3)
-        interleave_weights(0, 1, 2)
+        sign_values(1)
+        quantise_weights(0)
         weights(0, 1, 0)
         for h in range(H):
             for r in range(PACK):
@@ -294,7 +298,7 @@ def tile_rows_sink_gate_kernel(tc, qT, kT, t, v, sink, og, out):
             for r in range(1 - h, PACK):
                 weights(h, 1, r)
         interleave_weights(1)
-        quantise_weights(0)
+        quantise_values()
         values(0)
         quantise_weights(1)
         values(1)
@@ -303,7 +307,7 @@ def tile_rows_sink_gate_kernel(tc, qT, kT, t, v, sink, og, out):
             for r in range(PACK):
                 weights(h, 2, r)
 
-        add_sink_on_scalar(0)
+        add_sink(0)
         add_sink_on_scalar(1)
         for g in (1, 0, 2, 3):
             tanh_gate(g)

@@ -22,11 +22,15 @@ RUN = 4
 QUAD = 32
 TILES = NQ // P
 
-PIECES = [[0], [1, 2], [3]]
-GROUPS = [[(0, 0), (1, 0)], [(0, 1), (0, 2)], [(1, 1), (1, 2)], [(0, 3)], [(1, 3)]]
+PIECES = [(0, [0], [(0, 0), (1, 0), (2, 0), (2, P)]),
+          (1, [0], [(0, 0), (0, P), (1, 0), (1, P)]),
+          (1, [1, 2], [(2, 0), (0, 0), (1, 0), (2, 2 * P)]),
+          (0, [1, 2], [(0, 0), (1, 0), (2, 0), (0, 2 * P)]),
+          (1, [3], [(0, 0), (0, P), (1, 0), (1, P)]),
+          (0, [3], [(1, P * r) for r in range(PACK)])]
+GROUPS = [[(0, 0), (1, 0)], [(1, 1), (1, 2)], [(0, 1), (0, 2)], [(1, 3)], [(0, 3)]]
 UNITS = [[(0, 0), (1, 0)], [(0, 1), (0, 2)], [(1, 1), (1, 2)], [(0, 3), (1, 3)]]
 SINK_STEP = QUAD // (H * TILES)
-SCALAR_SHARE = 64
 SCORE_BANKS = 3
 
 MANTISSA, SIGN, ONE, HALF = 0x007FFFFF, -0x80000000, 0x3F800000, 0x3F000000
@@ -35,15 +39,6 @@ ODD = [11, 9, 7, 5, 3, 1]
 COMMON = 3465
 STEPS = len(ODD) + 1
 SQRT2 = math.sqrt(2.0)
-
-
-def score_place(h, piece, r):
-    width = P * len(PIECES[piece])
-    if piece == 0 or (piece, h) == (1, 0):
-        return min(r, 2), width * (r // 3)
-    if piece == 1:
-        return r // 2, width * (r % 2)
-    return 2 * h, width * r
 
 
 def of_unit(view, g):
@@ -112,7 +107,7 @@ def tile_rows_sink_gate_kernel(tc, qT, kT, t, v, sink, og, out):
         score_banks = [[ps.tile([P, N], F32, name="score%d_%d" % (h, b)) for b in range(SCORE_BANKS)]
                        for h in range(H)]
         y_banks = [ps.tile([P, 2, 2, E], F32, name="y%d" % b) for b in range(2)]
-        half_y = [y_banks[g % 2][:, g // 2] for g in range(len(UNITS))]
+        half_y = [y_banks[0][:, 0], y_banks[1][:, 0], y_banks[1][:, 1], y_banks[0][:, 1]]
 
         def quantise(codes, scales, words):
             nc.vector.quantize_mx(out=codes.bitcast(FP8X4), scales=scales, in_=words.rearrange("p n j -> p (n j)"))
@@ -146,23 +141,26 @@ def tile_rows_sink_gate_kernel(tc, qT, kT, t, v, sink, og, out):
             nc.vector.tensor_tensor(out=v_words[:, h].rearrange("p (a b) r -> p a r b", b=RUN),
                                     in0=v_raw[h][:].rearrange("p r (a b) -> p a r b", b=RUN), in1=factor, op=ALU.mult)
 
-        def scores(h, u, r, m=0):
-            rows, keys, c = slice(ROWS * h, ROWS * (h + 1)), slice(P * r, P * (r + 1)), PIECES[u][m]
-            bank, first = score_place(h, u, r)
+        def scores(u, r, m=0):
+            h, tiles, places = PIECES[u]
+            rows, keys, c = slice(ROWS * h, ROWS * (h + 1)), slice(P * r, P * (r + 1)), tiles[m]
+            bank, first = places[r]
             nc.tensor.matmul_mx(out=score_banks[h][bank][:, first + P * m:first + P * (m + 1)],
                                 lhsT=k_codes[rows, keys].bitcast(FP8X4), lhsT_scale=k_scales[rows, keys],
                                 rhs=q_codes[c][rows].bitcast(FP8X4), rhs_scale=q_scales[c][rows],
                                 start=True, stop=True)
 
-        def weights(h, u, r):
-            g = [(h, PIECES[u][0]) in members for members in GROUPS].index(True)
-            n0, n = P * GROUPS[g].index((h, PIECES[u][0])), P * len(PIECES[u])
-            bank, first = score_place(h, u, r)
+        def weights(u, r):
+            h, tiles, places = PIECES[u]
+            g = [(h, tiles[0]) in members for members in GROUPS].index(True)
+            n0, n = P * GROUPS[g].index((h, tiles[0])), P * len(tiles)
+            bank, first = places[r]
             nc.scalar.activation(out=w_rows[g][:, r, n0:n0 + n], in_=score_banks[h][bank][:, first:first + n],
                                  func=ACT.Exp, bias=ln_t[:, r:r + 1])
 
-        def interleave_weights(g, n0=0, n1=None, copy=nc.vector.tensor_copy):
-            interleave(w_words[g][:, n0:n1], w_rows[g][:, :, n0:n1], copy)
+        def interleave_weights(g, m0=0, m1=None):
+            cols = slice(P * m0, P * (len(GROUPS[g]) if m1 is None else m1))
+            interleave(w_words[g][:, cols], w_rows[g][:, :, cols])
 
         def quantise_weights(g):
             quantise(w_codes[g][:], w_scales[g][:], w_words[g][:])
@@ -179,6 +177,10 @@ def tile_rows_sink_gate_kernel(tc, qT, kT, t, v, sink, og, out):
         def add_sink(g):
             nc.vector.scalar_tensor_tensor(out=denom[:, g], in0=half_y[g][:, :, E - 1], scalar=2.0,
                                            in1=of_unit(sinks, g), op0=ALU.mult, op1=ALU.add)
+
+        def add_middle_sinks():
+            nc.vector.scalar_tensor_tensor(out=denom[:, 1:3], in0=y_banks[1][:, :, :, E - 1], scalar=2.0,
+                                           in1=sinks[:, :, 1:3], op0=ALU.mult, op1=ALU.add)
 
         def add_sink_on_scalar(g):
             for m in range(2):
@@ -218,18 +220,24 @@ def tile_rows_sink_gate_kernel(tc, qT, kT, t, v, sink, og, out):
         def load_values(h):
             nc.sync.dma_start(out=v_raw[h][:], in_=v[h].rearrange("(s r) e -> s r e", r=PACK))
 
+        def load_gates(h):
+            nc.sync.dma_start(out=og_sb[:, h], in_=og[h].rearrange("(c p) e -> p c e", p=P))
+
+        def load_sinks():
+            nc.sync.dma_start(out=sink_rows[0:P:SINK_STEP, :],
+                              in_=sink.rearrange("h (c a x) o -> a (h c) (x o)", a=P // QUAD, x=QUAD))
+
         nc.sync.dma_start(out=t_sb[:], in_=t.rearrange("(s r) o -> s (r o)", r=PACK))
         nc.sync.dma_start(out=k_raw[:], in_=kT.rearrange("h (p j) n -> (h p) j n", j=PACK))
         load_queries(0)
         load_queries(1)
         load_queries(2)
-        nc.sync.dma_start(out=sink_rows[0:P:SINK_STEP, :],
-                          in_=sink.rearrange("h (c a x) o -> a (h c) (x o)", a=P // QUAD, x=QUAD))
+        load_sinks()
         load_values(0)
         load_queries(3)
         load_values(1)
-        for h in range(H):
-            nc.sync.dma_start(out=og_sb[:, h], in_=og[h].rearrange("(c p) e -> p c e", p=P))
+        load_gates(1)
+        load_gates(0)
 
         t_bits = t_sb[:].bitcast(I32)
         nc.vector.tensor_scalar(out=t_mantissa[:], in0=t_bits, scalar1=MANTISSA, scalar2=ONE,
@@ -267,68 +275,76 @@ def tile_rows_sink_gate_kernel(tc, qT, kT, t, v, sink, og, out):
         nc.vector.transpose(out=sink_cols[:], in_=sink_rows[:])
         quantise_queries(2)
 
-        first_piece = [(0, 0), (1, 0), (0, 1), (1, 1), (0, 2), (0, 3), (1, 2), (1, 3)]
-        for h, r in first_piece:
-            scores(h, 0, r)
-        for h, r in first_piece[:6]:
-            weights(h, 0, r)
-        for m in range(2):
-            for r in range(2):
-                scores(0, 1, r, m)
-        for h in range(H):
-            for r in range(2 - 2 * h, PACK):
-                for m in range(2):
-                    scores(h, 1, r, m)
-        for h, r in first_piece[6:]:
-            weights(h, 0, r)
-        interleave_weights(0, 0, SCALAR_SHARE, nc.scalar.copy)
+        def second_scores(r):
+            for m in range(2):
+                for u in (2, 3):
+                    scores(u, r, m)
 
+        for r in range(PACK):
+            for u in (0, 1):
+                scores(u, r)
+        for u in (0, 1):
+            for r in (0, 1):
+                weights(u, r)
+        second_scores(0)
+        second_scores(1)
+        for u in (0, 1):
+            for r in (2, 3):
+                weights(u, r)
+        second_scores(2)
+        for u in (2, 3):
+            weights(u, 0)
+        second_scores(3)
+        for u in (2, 3):
+            weights(u, 1)
         sign_values(0)
-        interleave_weights(0, SCALAR_SHARE, P)
+        interleave_weights(0, 0, 1)
         interleave_queries(3)
-        interleave_weights(0, P)
+        interleave_weights(0, 1, 2)
         quantise_queries(3)
         sign_values(1)
         quantise_weights(0)
-        weights(0, 1, 0)
-        for h in range(H):
-            for r in range(PACK):
-                scores(h, 2, r)
-        for h in range(H):
-            for r in range(1 - h, PACK):
-                weights(h, 1, r)
-        interleave_weights(1)
+        for r in (0, 1):
+            for u in (4, 5):
+                scores(u, r)
+        weights(2, 2)
+        for r in (2, 3):
+            for u in (5, 4):
+                scores(u, r)
+        weights(2, 3)
+        for r in (2, 3):
+            weights(3, r)
         quantise_values()
         values(0)
+        interleave_weights(1)
+        interleave_weights(2)
         quantise_weights(1)
         values(1)
-        interleave_weights(2)
-        for h in range(H):
+        for u in (4, 5):
             for r in range(PACK):
-                weights(h, 2, r)
+                weights(u, r)
 
-        add_sink(0)
-        add_sink_on_scalar(1)
-        for g in (1, 0, 2, 3):
+        add_sink_on_scalar(0)
+        for g in (0, 2, 1, 3):
             tanh_gate(g)
         interleave_weights(3)
         quantise_weights(2)
         values(2)
         quantise_weights(3)
         interleave_weights(4)
-        invert(0, 2)
-        gate_y(1)
+        invert(0, 1)
+        gate_y(0)
         quantise_weights(4)
         values(3)
         values(4)
-        add_sink(2)
-        gate_y(0)
-        invert(2, 3)
+        add_middle_sinks()
         gate_y(2)
+        invert(1, 3)
+        gate_y(1)
         add_sink(3)
         gate_y(3)
         invert(3, 4)
-        for g in (1, 0, 2):
+        for g in (0, 2, 1):
             for m in range(2):
                 scale_on_scalar(g, m)
             store(g)

@@ -21,17 +21,7 @@ PACK = 4
 RUN = 4
 QUAD = 32
 TILES = NQ // P
-
-PIECES = [(0, [0], [(0, 0), (1, 0), (2, 0), (2, P)]),
-          (1, [0], [(0, 0), (0, P), (1, 0), (1, P)]),
-          (1, [1, 2], [(2, 0), (0, 0), (1, 0), (2, 2 * P)]),
-          (0, [1, 2], [(0, 0), (1, 0), (2, 0), (0, 2 * P)]),
-          (1, [3], [(0, 0), (0, P), (1, 0), (1, P)]),
-          (0, [3], [(1, P * r) for r in range(PACK)])]
-GROUPS = [[(0, 0), (1, 0)], [(1, 1), (1, 2)], [(0, 1), (0, 2)], [(1, 3)], [(0, 3)]]
-UNITS = [[(0, 0), (1, 0)], [(0, 1), (0, 2)], [(1, 1), (1, 2)], [(0, 3), (1, 3)]]
 SINK_STEP = QUAD // (H * TILES)
-SCORE_BANKS = 3
 
 MANTISSA, SIGN, ONE, HALF = 0x007FFFFF, -0x80000000, 0x3F800000, 0x3F000000
 MANTISSA_BITS, EXPONENT, EXPONENT_BIAS = 23, 0xFF, 127
@@ -40,10 +30,18 @@ COMMON = 3465
 STEPS = len(ODD) + 1
 SQRT2 = math.sqrt(2.0)
 
-
-def of_unit(view, g):
-    (h0, c0), (h1, c1) = UNITS[g]
-    return view[:, h0, c0:c1 + 1] if h0 == h1 else view[:, :, c0]
+Q_LOADS = [[0], [1], [2], [3]]
+TURNS = [(0, 0), (1, 0), (0, 1), (0, 2), (1, 1), (1, 2), (0, 3), (1, 3)]
+SCORE_BANKS = [3, 3]
+Y_BANKS = [[0, 1, 6, 7], [2, 3, 4, 5]]
+PLACES = [[(0, 0), (0, P), (1, 0), (1, P)],
+          [(0, 0), (1, 0), (2, 0), (2, P)],
+          [(2, 0), (0, 0), (1, 0), (2, 2 * P)],
+          [(2, P), (0, P), (1, P), (2, 3 * P)],
+          [(0, 0), (1, 0), (2, 0), (0, 2 * P)],
+          [(0, P), (1, P), (2, P), (0, 3 * P)],
+          [(0, 0), (0, P), (1, 0), (1, P)],
+          [(1, P * r) for r in range(PACK)]]
 
 
 def tile_rows_sink_gate_kernel(tc, qT, kT, t, v, sink, og, out):
@@ -60,28 +58,22 @@ def tile_rows_sink_gate_kernel(tc, qT, kT, t, v, sink, og, out):
         def per_tile(name, shape, dtype):
             return [sbuf("%s%d" % (name, c), shape, dtype) for c in range(TILES)]
 
-        def per_group(name, shape, dtype):
-            return [sbuf("%s%d" % (name, g), shape(P * len(pairs)), dtype) for g, pairs in enumerate(GROUPS)]
-
-        def per_unit(name, shape, dtype):
-            return [sbuf("%s%d" % (name, g), shape, dtype) for g in range(len(UNITS))]
-
         k_raw = sbuf("k_raw", [P, PACK, N], F32)
         k_words = sbuf("k_words", [P, PACK, P, PACK], BF16)
         k_codes = sbuf("k_codes", [P, N], U32)
         k_scales = sbuf("k_scales", [P, N], U8)
-        q_raw = per_tile("q_raw", [P, PACK, P], F32)
-        q_words = per_tile("q_words", [P, P, PACK], BF16)
-        q_codes = per_tile("q_codes", [P, P], U32)
-        q_scales = per_tile("q_scales", [P, P], U8)
+        q_raw = [sbuf("q_raw%d" % n, [P, PACK, P * len(tiles)], F32) for n, tiles in enumerate(Q_LOADS)]
+        q_words = sbuf("q_words", [P, NQ, PACK], BF16)
+        q_codes = sbuf("q_codes", [P, NQ], U32)
+        q_scales = sbuf("q_scales", [P, NQ], U8)
         v_raw = [sbuf("v_raw%d" % h, [P, PACK, E], F32) for h in range(H)]
         v_words = sbuf("v_words", [P, H, E, PACK], BF16)
         v_codes = sbuf("v_codes", [P, H, E], U32)
         v_scales = sbuf("v_scales", [P, H, E], U8)
-        w_rows = per_group("w_rows", lambda n: [P, PACK, n], BF16)
-        w_words = per_group("w_words", lambda n: [P, n, PACK], BF16)
-        w_codes = per_group("w_codes", lambda n: [P, n], U32)
-        w_scales = per_group("w_scales", lambda n: [P, n], U8)
+        w_rows = sbuf("w_rows", [P, PACK, H * NQ], BF16)
+        w_words = sbuf("w_words", [P, H * NQ, PACK], BF16)
+        w_codes = sbuf("w_codes", [P, H * NQ], U32)
+        w_scales = sbuf("w_scales", [P, H * NQ], U8)
 
         t_sb = sbuf("t_sb", [P, PACK], F32)
         t_mantissa = sbuf("t_mantissa", [P, PACK], I32)
@@ -96,117 +88,147 @@ def tile_rows_sink_gate_kernel(tc, qT, kT, t, v, sink, og, out):
         ln_t = sums[:, :, STEPS - 1]
         sink_rows = sbuf("sink_rows", [P, QUAD], F32)
         sink_cols = sbuf("sink_cols", [P, QUAD], F32)
-        sinks = sink_cols[:, 0:QUAD:SINK_STEP].rearrange("p (h c) -> p h c", h=H)
-        og_sb = sbuf("og_sb", [P, H, TILES, E], F32)
-        tanh_og = per_unit("tanh_og", [P, 2, E], F32)
-        gated_y = per_unit("gated_y", [P, 2, E], F32)
-        denom = sbuf("denom", [P, len(UNITS), 2], F32)
-        inverse = sbuf("inverse", [P, len(UNITS), 2], F32)
-        result = per_unit("result", [P, 2, E], F32)
+        sinks = sink_cols[:, 0:QUAD:SINK_STEP]
+        og_sb = sbuf("og_sb", [P, H * TILES, E], F32)
+        tanh_og = sbuf("tanh_og", [P, H * TILES, E], F32)
+        gate = sbuf("gate", [P, H * TILES, E], F32)
+        denom = sbuf("denom", [P, H * TILES], F32)
+        inverse = sbuf("inverse", [P, H * TILES], F32)
+        result = sbuf("result", [P, H * TILES, E], F32)
 
-        score_banks = [[ps.tile([P, N], F32, name="score%d_%d" % (h, b)) for b in range(SCORE_BANKS)]
+        score_banks = [[ps.tile([P, N], F32, name="score%d_%d" % (h, b)) for b in range(SCORE_BANKS[h])]
                        for h in range(H)]
-        y_banks = [ps.tile([P, 2, 2, E], F32, name="y%d" % b) for b in range(2)]
-        half_y = [y_banks[0][:, 0], y_banks[1][:, 0], y_banks[1][:, 1], y_banks[0][:, 1]]
+        y_banks = [ps.tile([P, len(turns), E], F32, name="y%d" % b) for b, turns in enumerate(Y_BANKS)]
+
+        def half_y(n0, n1):
+            b = [n0 in turns for turns in Y_BANKS].index(True)
+            m = Y_BANKS[b].index(n0)
+            return y_banks[b][:, m:m + n1 - n0]
+
+        def of_turns(view, n0, n1):
+            at = [TILES * h + c for h, c in TURNS[n0:n1]]
+            return view[:, at[0]:at[-1] + 1:(at[1] - at[0] if len(at) > 1 else 1)]
 
         def quantise(codes, scales, words):
             nc.vector.quantize_mx(out=codes.bitcast(FP8X4), scales=scales, in_=words.rearrange("p n j -> p (n j)"))
 
-        def interleave(words, rows, copy=nc.vector.tensor_copy):
+        def interleave(words, rows, copy):
             copy(out=words.rearrange("p (a b) j -> p a j b", b=RUN), in_=rows.rearrange("p j (a b) -> p a j b", b=RUN))
 
         def scalar_copy(out, in_):
             nc.scalar.activation(out=out, in_=in_, func=ACT.Copy)
 
-        def deal_keys(copy, r0, r1):
-            copy(out=k_words[:, r0:r1].rearrange("p r s j -> p s j r"),
-                 in_=k_raw[:].rearrange("p j (s r) -> p s j r", r=PACK)[:, :, :, r0:r1])
+        def deal_keys(copy, r0, r1, s0=0, s1=P):
+            copy(out=k_words[:, r0:r1, s0:s1].rearrange("p r s j -> p s j r"),
+                 in_=k_raw[:].rearrange("p j (s r) -> p s j r", r=PACK)[:, s0:s1, :, r0:r1])
 
         def quantise_keys(r0, r1):
             quantise(k_codes[:, P * r0:P * r1], k_scales[:, P * r0:P * r1],
                      k_words[:, r0:r1].rearrange("p r s j -> p (r s) j"))
 
-        def interleave_queries(c, copy=nc.vector.tensor_copy):
-            interleave(q_words[c][:], q_raw[c][:], copy)
+        def interleave_queries(n0, n1, copy=nc.vector.tensor_copy):
+            n = [n0 // P in tiles for tiles in Q_LOADS].index(True)
+            first = P * Q_LOADS[n][0]
+            interleave(q_words[:, n0:n1], q_raw[n][:, :, n0 - first:n1 - first], copy)
 
-        def quantise_queries(c):
-            quantise(q_codes[c][:], q_scales[c][:], q_words[c][:])
+        def quantise_queries(c0, c1):
+            quantise(q_codes[:, P * c0:P * c1], q_scales[:, P * c0:P * c1], q_words[:, P * c0:P * c1])
 
-        def quantise_values():
-            quantise(v_codes[:].rearrange("p h e -> p (h e)"), v_scales[:].rearrange("p h e -> p (h e)"),
-                     v_words[:].rearrange("p h e r -> p (h e) r"))
+        def quantise_values(h0, h1):
+            quantise(v_codes[:, h0:h1].rearrange("p h e -> p (h e)"), v_scales[:, h0:h1].rearrange("p h e -> p (h e)"),
+                     v_words[:, h0:h1].rearrange("p h e r -> p (h e) r"))
 
-        def sign_values(h):
-            factor = half_sign[:].bitcast(F32).unsqueeze(1).unsqueeze(3).to_broadcast([P, E // RUN, PACK, RUN])
-            nc.vector.tensor_tensor(out=v_words[:, h].rearrange("p (a b) r -> p a r b", b=RUN),
-                                    in0=v_raw[h][:].rearrange("p r (a b) -> p a r b", b=RUN), in1=factor, op=ALU.mult)
+        def sign_values(h, e0=0, e1=E):
+            factor = half_sign[:].bitcast(F32).unsqueeze(1).unsqueeze(3).to_broadcast([P, (e1 - e0) // RUN, PACK, RUN])
+            nc.vector.tensor_tensor(out=v_words[:, h, e0:e1].rearrange("p (a b) r -> p a r b", b=RUN),
+                                    in0=v_raw[h][:, :, e0:e1].rearrange("p r (a b) -> p a r b", b=RUN), in1=factor,
+                                    op=ALU.mult)
 
-        def scores(u, r, m=0):
-            h, tiles, places = PIECES[u]
-            rows, keys, c = slice(ROWS * h, ROWS * (h + 1)), slice(P * r, P * (r + 1)), tiles[m]
-            bank, first = places[r]
-            nc.tensor.matmul_mx(out=score_banks[h][bank][:, first + P * m:first + P * (m + 1)],
+        def score(n, r):
+            h, c = TURNS[n]
+            rows, keys, queries = slice(ROWS * h, ROWS * (h + 1)), slice(P * r, P * (r + 1)), slice(P * c, P * (c + 1))
+            bank, first = PLACES[n][r]
+            nc.tensor.matmul_mx(out=score_banks[h][bank][:, first:first + P],
                                 lhsT=k_codes[rows, keys].bitcast(FP8X4), lhsT_scale=k_scales[rows, keys],
-                                rhs=q_codes[c][rows].bitcast(FP8X4), rhs_scale=q_scales[c][rows],
+                                rhs=q_codes[rows, queries].bitcast(FP8X4), rhs_scale=q_scales[rows, queries],
                                 start=True, stop=True)
 
-        def weights(u, r):
-            h, tiles, places = PIECES[u]
-            g = [(h, tiles[0]) in members for members in GROUPS].index(True)
-            n0, n = P * GROUPS[g].index((h, tiles[0])), P * len(tiles)
-            bank, first = places[r]
-            nc.scalar.activation(out=w_rows[g][:, r, n0:n0 + n], in_=score_banks[h][bank][:, first:first + n],
+        def scores(n):
+            for r in range(PACK):
+                score(n, r)
+
+        def weight(n, r, turns=1):
+            bank, first = PLACES[n][r]
+            nc.scalar.activation(out=w_rows[:, r, P * n:P * (n + turns)],
+                                 in_=score_banks[TURNS[n][0]][bank][:, first:first + P * turns],
                                  func=ACT.Exp, bias=ln_t[:, r:r + 1])
 
-        def interleave_weights(g, m0=0, m1=None):
-            cols = slice(P * m0, P * (len(GROUPS[g]) if m1 is None else m1))
-            interleave(w_words[g][:, cols], w_rows[g][:, :, cols])
+        def weights(n, turns=1):
+            for r in range(PACK):
+                weight(n, r, turns)
 
-        def quantise_weights(g):
-            quantise(w_codes[g][:], w_scales[g][:], w_words[g][:])
+        def interleave_weights(n0, n1, copy=nc.vector.tensor_copy):
+            interleave(w_words[:, n0:n1], w_rows[:, :, n0:n1], copy)
 
-        def values(g):
-            for m, pair in enumerate(GROUPS[g]):
-                unit = [pair in members for members in UNITS].index(True)
-                cols = slice(P * m, P * (m + 1))
-                nc.tensor.matmul_mx(out=half_y[unit][:, UNITS[unit].index(pair)],
-                                    lhsT=w_codes[g][:, cols].bitcast(FP8X4), lhsT_scale=w_scales[g][:, cols],
-                                    rhs=v_codes[:, pair[0]].bitcast(FP8X4), rhs_scale=v_scales[:, pair[0]],
+        def quantise_weights(n0, n1):
+            quantise(w_codes[:, P * n0:P * n1], w_scales[:, P * n0:P * n1], w_words[:, P * n0:P * n1])
+
+        def values(n0, n1):
+            for n in range(n0, n1):
+                h, cols = TURNS[n][0], slice(P * n, P * (n + 1))
+                nc.tensor.matmul_mx(out=half_y(n, n + 1)[:, 0],
+                                    lhsT=w_codes[:, cols].bitcast(FP8X4), lhsT_scale=w_scales[:, cols],
+                                    rhs=v_codes[:, h].bitcast(FP8X4), rhs_scale=v_scales[:, h],
                                     start=True, stop=True)
 
-        def add_sink(g):
-            nc.vector.scalar_tensor_tensor(out=denom[:, g], in0=half_y[g][:, :, E - 1], scalar=2.0,
-                                           in1=of_unit(sinks, g), op0=ALU.mult, op1=ALU.add)
+        def add_sinks(n0, n1):
+            nc.vector.scalar_tensor_tensor(out=denom[:, n0:n1], in0=half_y(n0, n1)[:, :, E - 1], scalar=2.0,
+                                           in1=of_turns(sinks, n0, n1), op0=ALU.mult, op1=ALU.add)
 
         def add_middle_sinks():
-            nc.vector.scalar_tensor_tensor(out=denom[:, 1:3], in0=y_banks[1][:, :, :, E - 1], scalar=2.0,
-                                           in1=sinks[:, :, 1:3], op0=ALU.mult, op1=ALU.add)
+            nc.vector.scalar_tensor_tensor(out=denom[:, 2:6].rearrange("p (h c) -> p h c", h=H),
+                                           in0=half_y(2, 6)[:, :, E - 1].rearrange("p (h c) -> p h c", h=H),
+                                           scalar=2.0, in1=sinks.rearrange("p (h c) -> p h c", h=H)[:, :, 1:3],
+                                           op0=ALU.mult, op1=ALU.add)
 
-        def add_sink_on_scalar(g):
-            for m in range(2):
-                nc.scalar.activation(out=denom[:, g, m:m + 1], in_=half_y[g][:, m, E - 1:E], func=ACT.Identity,
-                                     scale=2.0, bias=of_unit(sinks, g)[:, m:m + 1])
+        def add_sink_on_scalar(n):
+            nc.scalar.activation(out=denom[:, n:n + 1], in_=half_y(n, n + 1)[:, 0, E - 1:E], func=ACT.Identity,
+                                 scale=2.0, bias=of_turns(sinks, n, n + 1))
 
-        def invert(g0, g1):
-            nc.vector.reciprocal(out=inverse[:, g0:g1], in_=denom[:, g0:g1])
+        def invert(n0, n1):
+            nc.vector.reciprocal(out=inverse[:, n0:n1], in_=denom[:, n0:n1])
 
-        def store(g):
-            nc.sync.dma_start(out=of_unit(out.rearrange("h (c p) e -> p h c e", p=P), g), in_=result[g][:])
+        def tanh_gate(n0, n1):
+            nc.scalar.activation(out=tanh_og[:, n0:n1], in_=of_turns(og_sb, n0, n1), func=ACT.Tanh, scale=0.5)
 
-        def tanh_gate(g):
-            nc.scalar.activation(out=tanh_og[g][:], in_=of_unit(og_sb[:], g), func=ACT.Tanh, scale=0.5)
+        def one_plus_on_scalar(n0, n1):
+            nc.scalar.activation(out=gate[:, n0:n1], in_=tanh_og[:, n0:n1], func=ACT.Copy, bias=1.0)
 
-        def gate_y(g):
-            nc.vector.scalar_tensor_tensor(out=gated_y[g][:], in0=tanh_og[g][:], scalar=1.0, in1=half_y[g],
+        def one_plus_on_vector(n0, n1):
+            nc.vector.tensor_scalar(out=gate[:, n0:n1], in0=tanh_og[:, n0:n1], scalar1=1.0, scalar2=None, op0=ALU.add)
+
+        def one_plus_on_gpsimd(n0, n1):
+            nc.gpsimd.tensor_scalar(out=gate[:, n0:n1], in0=tanh_og[:, n0:n1], scalar1=1.0, scalar2=1.0,
+                                    op0=ALU.mult, op1=ALU.add)
+
+        def finish(n):
+            nc.vector.scalar_tensor_tensor(out=result[:, n], in0=half_y(n, n + 1)[:, 0], scalar=inverse[:, n:n + 1],
+                                           in1=gate[:, n], op0=ALU.mult, op1=ALU.mult)
+
+        def gate_y(n0, n1):
+            nc.vector.scalar_tensor_tensor(out=gate[:, n0:n1], in0=tanh_og[:, n0:n1], scalar=1.0, in1=half_y(n0, n1),
                                            op0=ALU.add, op1=ALU.mult)
 
-        def scale_on_scalar(g, m):
-            nc.scalar.activation(out=result[g][:, m], in_=gated_y[g][:, m], func=ACT.Copy,
-                                 scale=inverse[:, g, m:m + 1])
+        def scale_on_scalar(n):
+            nc.scalar.activation(out=result[:, n], in_=gate[:, n], func=ACT.Copy, scale=inverse[:, n:n + 1])
 
-        def scale_on_vector(g, m):
-            nc.vector.tensor_scalar(out=result[g][:, m], in0=gated_y[g][:, m], scalar1=inverse[:, g, m:m + 1],
+        def scale_on_vector(n):
+            nc.vector.tensor_scalar(out=result[:, n], in0=gate[:, n], scalar1=inverse[:, n:n + 1],
                                     scalar2=None, op0=ALU.mult)
+
+        def store(n0, n1):
+            nc.sync.dma_start(out=of_turns(out.rearrange("h (c p) e -> p (h c) e", p=P), n0, n1),
+                              in_=result[:, n0:n1])
 
         nc.vector.memset(sink_rows[:], 0.0)
         nc.vector.memset(factors[:, :, 0:1], 0.0)
@@ -214,18 +236,22 @@ def tile_rows_sink_gate_kernel(tc, qT, kT, t, v, sink, og, out):
             nc.vector.memset(terms[:, :, step:step + 1], float(COMMON // odd))
         q_hbm = qT.rearrange("h (p j) n -> (h p) j n", j=PACK)
 
-        def load_queries(c):
-            nc.sync.dma_start(out=q_raw[c][:], in_=q_hbm[:, :, P * c:P * (c + 1)])
+        def load_queries(n):
+            tiles = Q_LOADS[n]
+            nc.sync.dma_start(out=q_raw[n][:], in_=q_hbm[:, :, P * tiles[0]:P * (tiles[-1] + 1)])
 
         def load_values(h):
             nc.sync.dma_start(out=v_raw[h][:], in_=v[h].rearrange("(s r) e -> s r e", r=PACK))
 
         def load_gates(h):
-            nc.sync.dma_start(out=og_sb[:, h], in_=og[h].rearrange("(c p) e -> p c e", p=P))
+            nc.sync.dma_start(out=og_sb[:, TILES * h:TILES * (h + 1)], in_=og[h].rearrange("(c p) e -> p c e", p=P))
 
         def load_sinks():
             nc.sync.dma_start(out=sink_rows[0:P:SINK_STEP, :],
                               in_=sink.rearrange("h (c a x) o -> a (h c) (x o)", a=P // QUAD, x=QUAD))
+
+        def turn_sinks():
+            nc.vector.transpose(out=sink_cols[:], in_=sink_rows[:])
 
         nc.sync.dma_start(out=t_sb[:], in_=t.rearrange("(s r) o -> s (r o)", r=PACK))
         nc.sync.dma_start(out=k_raw[:], in_=kT.rearrange("h (p j) n -> (h p) j n", j=PACK))
@@ -236,8 +262,8 @@ def tile_rows_sink_gate_kernel(tc, qT, kT, t, v, sink, og, out):
         load_values(0)
         load_queries(3)
         load_values(1)
-        load_gates(1)
         load_gates(0)
+        load_gates(1)
 
         t_bits = t_sb[:].bitcast(I32)
         nc.vector.tensor_scalar(out=t_mantissa[:], in0=t_bits, scalar1=MANTISSA, scalar2=ONE,
@@ -262,92 +288,88 @@ def tile_rows_sink_gate_kernel(tc, qT, kT, t, v, sink, og, out):
                                      data1=terms[:].rearrange("p r k -> p (r k)"),
                                      initial=0.0, op0=ALU.mult, op1=ALU.add)
 
-        deal_keys(nc.vector.tensor_copy, 0, PACK // 2)
-        deal_keys(scalar_copy, PACK // 2, PACK)
-        interleave_queries(0)
-        quantise_keys(0, 1)
-        quantise_queries(0)
-        quantise_keys(1, 2)
-        quantise_keys(2, PACK)
-        interleave_queries(1, copy=nc.scalar.copy)
-        interleave_queries(2)
-        quantise_queries(1)
-        nc.vector.transpose(out=sink_cols[:], in_=sink_rows[:])
-        quantise_queries(2)
 
         def second_scores(r):
-            for m in range(2):
-                for u in (2, 3):
-                    scores(u, r, m)
+            for n in (2, 4, 3, 5):
+                score(n, r)
 
+        deal_keys(nc.vector.tensor_copy, 0, 2)
+        deal_keys(scalar_copy, 2, 4)
+        interleave_queries(0, P)
+        quantise_keys(0, 1)
+        quantise_queries(0, 1)
+        quantise_keys(1, 2)
+        quantise_keys(2, 4)
+        interleave_queries(P, 2 * P, copy=nc.scalar.copy)
+        interleave_queries(2 * P, 3 * P)
+        quantise_queries(1, 2)
+        turn_sinks()
+        quantise_queries(2, 3)
         for r in range(PACK):
-            for u in (0, 1):
-                scores(u, r)
-        for u in (0, 1):
+            score(1, r)
+            score(0, r)
+        for n in (1, 0):
             for r in (0, 1):
-                weights(u, r)
+                weight(n, r)
         second_scores(0)
         second_scores(1)
-        for u in (0, 1):
+        for n in (1, 0):
             for r in (2, 3):
-                weights(u, r)
+                weight(n, r)
         second_scores(2)
-        for u in (2, 3):
-            weights(u, 0)
+        for n in (2, 4):
+            weight(n, 0, 2)
         second_scores(3)
-        for u in (2, 3):
-            weights(u, 1)
+        for n in (2, 4):
+            weight(n, 1, 2)
         sign_values(0)
-        interleave_weights(0, 0, 1)
-        interleave_queries(3)
-        interleave_weights(0, 1, 2)
-        quantise_queries(3)
+        interleave_weights(P, 2 * P)
+        interleave_queries(3 * P, 4 * P)
+        interleave_weights(0, P)
+        quantise_queries(3, 4)
         sign_values(1)
-        quantise_weights(0)
+        quantise_weights(0, 2)
         for r in (0, 1):
-            for u in (4, 5):
-                scores(u, r)
-        weights(2, 2)
+            for n in (6, 7):
+                score(n, r)
+        weight(2, 2, 2)
         for r in (2, 3):
-            for u in (5, 4):
-                scores(u, r)
-        weights(2, 3)
+            for n in (7, 6):
+                score(n, r)
+        weight(2, 3, 2)
         for r in (2, 3):
-            weights(3, r)
-        quantise_values()
-        values(0)
-        interleave_weights(1)
-        interleave_weights(2)
-        quantise_weights(1)
-        values(1)
-        for u in (4, 5):
-            for r in range(PACK):
-                weights(u, r)
-
-        add_sink_on_scalar(0)
-        for g in (0, 2, 1, 3):
-            tanh_gate(g)
-        interleave_weights(3)
-        quantise_weights(2)
-        values(2)
-        quantise_weights(3)
-        interleave_weights(4)
-        invert(0, 1)
-        gate_y(0)
-        quantise_weights(4)
-        values(3)
-        values(4)
+            weight(4, r, 2)
+        quantise_values(0, 2)
+        values(0, 2)
+        interleave_weights(2 * P, 4 * P)
+        interleave_weights(4 * P, 6 * P)
+        quantise_weights(2, 4)
+        values(2, 4)
+        weights(6)
+        weights(7)
+        tanh_gate(0, 2)
+        interleave_weights(7 * P, 8 * P, copy=nc.scalar.copy)
+        for n in range(2, 8, 2):
+            tanh_gate(n, n + 2)
+        interleave_weights(6 * P, 7 * P)
+        quantise_weights(4, 6)
+        values(4, 6)
+        add_sinks(0, 2)
+        gate_y(0, 2)
+        invert(0, 2)
+        quantise_weights(6, 8)
+        values(6, 8)
         add_middle_sinks()
-        gate_y(2)
-        invert(1, 3)
-        gate_y(1)
-        add_sink(3)
-        gate_y(3)
-        invert(3, 4)
-        for g in (0, 2, 1):
-            for m in range(2):
-                scale_on_scalar(g, m)
-            store(g)
-        for m in range(2):
-            scale_on_vector(3, m)
-        store(3)
+        gate_y(2, 4)
+        invert(2, 6)
+        gate_y(4, 6)
+        add_sinks(6, 8)
+        gate_y(6, 8)
+        invert(6, 8)
+        for n in range(0, 6, 2):
+            scale_on_scalar(n)
+            scale_on_scalar(n + 1)
+            store(n, n + 2)
+        scale_on_vector(6)
+        scale_on_vector(7)
+        store(6, 8)

@@ -355,9 +355,10 @@ def tile_rows_sink_gate_kernel(tc, qT, kT, t, v, sink, og, out):
         quantise_weights(4, 6)
         values(4, 6)
         add_sinks(0, 2)
+        quantise_weights(6, 7)
         gate_y(0, 2)
         invert(0, 2)
-        quantise_weights(6, 8)
+        quantise_weights(7, 8)
         values(6, 8)
         add_middle_sinks()
         gate_y(2, 4)

@@ -19,6 +19,7 @@ P = 128
 ROWS = 64
 PACK = 4
 RUN = 4
+LONG_RUN = 8
 QUAD = 32
 TILES = NQ // P
 SINK_STEP = QUAD // (H * TILES)
@@ -112,8 +113,8 @@ def tile_rows_sink_gate_kernel(tc, qT, kT, t, v, sink, og, out):
         def quantise(codes, scales, words):
             nc.vector.quantize_mx(out=codes.bitcast(FP8X4), scales=scales, in_=words.rearrange("p n j -> p (n j)"))
 
-        def interleave(words, rows, copy):
-            copy(out=words.rearrange("p (a b) j -> p a j b", b=RUN), in_=rows.rearrange("p j (a b) -> p a j b", b=RUN))
+        def interleave(words, rows, copy, run=RUN):
+            copy(out=words.rearrange("p (a b) j -> p a j b", b=run), in_=rows.rearrange("p j (a b) -> p a j b", b=run))
 
         def scalar_copy(out, in_):
             nc.scalar.activation(out=out, in_=in_, func=ACT.Copy)
@@ -129,7 +130,7 @@ def tile_rows_sink_gate_kernel(tc, qT, kT, t, v, sink, og, out):
         def interleave_queries(n0, n1, copy=nc.vector.tensor_copy):
             n = [n0 // P in tiles for tiles in Q_LOADS].index(True)
             first = P * Q_LOADS[n][0]
-            interleave(q_words[:, n0:n1], q_raw[n][:, :, n0 - first:n1 - first], copy)
+            interleave(q_words[:, n0:n1], q_raw[n][:, :, n0 - first:n1 - first], copy, LONG_RUN)
 
         def quantise_queries(c0, c1):
             quantise(q_codes[:, P * c0:P * c1], q_scales[:, P * c0:P * c1], q_words[:, P * c0:P * c1])
@@ -139,9 +140,9 @@ def tile_rows_sink_gate_kernel(tc, qT, kT, t, v, sink, og, out):
                      v_words[:, h0:h1].rearrange("p h e r -> p (h e) r"))
 
         def sign_values(h, e0=0, e1=E):
-            factor = half_sign[:].bitcast(F32).unsqueeze(1).unsqueeze(3).to_broadcast([P, (e1 - e0) // RUN, PACK, RUN])
-            nc.vector.tensor_tensor(out=v_words[:, h, e0:e1].rearrange("p (a b) r -> p a r b", b=RUN),
-                                    in0=v_raw[h][:, :, e0:e1].rearrange("p r (a b) -> p a r b", b=RUN), in1=factor,
+            factor = half_sign[:].bitcast(F32).unsqueeze(1).unsqueeze(3).to_broadcast([P, (e1 - e0) // LONG_RUN, PACK, LONG_RUN])
+            nc.vector.tensor_tensor(out=v_words[:, h, e0:e1].rearrange("p (a b) r -> p a r b", b=LONG_RUN),
+                                    in0=v_raw[h][:, :, e0:e1].rearrange("p r (a b) -> p a r b", b=LONG_RUN), in1=factor,
                                     op=ALU.mult)
 
         def score(n, r):

import math
from contextlib import ExitStack

import concourse.mybir as mybir

F32 = mybir.dt.float32
BF16 = mybir.dt.bfloat16
I32 = mybir.dt.int32
U32 = mybir.dt.uint32
U8 = mybir.dt.uint8
FP8X4 = mybir.dt.float8_e4m3fn_x4
ALU = mybir.AluOpType
ACT = mybir.ActivationFunctionType

H, D, NQ, N, E = 2, 256, 512, 512, 128
FLOPS = 2 * H * N * NQ * (D + E)

P = 128
ROWS = 64
PACK = 4
RUN = 4
LONG_RUN = 8
QUAD = 32
TILES = NQ // P
SINK_STEP = QUAD // (H * TILES)

MANTISSA, SIGN, ONE, HALF = 0x007FFFFF, -0x80000000, 0x3F800000, 0x3F000000
MANTISSA_BITS, EXPONENT, EXPONENT_BIAS = 23, 0xFF, 127
ODD = [11, 9, 7, 5, 3, 1]
COMMON = 3465
STEPS = len(ODD) + 1
SQRT2 = math.sqrt(2.0)

Q_LOADS = [[0], [1], [2], [3]]
TURNS = [(0, 0), (1, 0), (0, 1), (0, 2), (1, 1), (1, 2), (0, 3), (1, 3)]
SCORE_BANKS = [3, 3]
Y_BANKS = [[0, 1, 6, 7], [2, 3, 4, 5]]
PLACES = [[(0, 0), (0, P), (1, 0), (1, P)],
          [(0, 0), (1, 0), (2, 0), (2, P)],
          [(2, 0), (0, 0), (1, 0), (2, 2 * P)],
          [(2, P), (0, P), (1, P), (2, 3 * P)],
          [(0, 0), (1, 0), (2, 0), (0, 2 * P)],
          [(0, P), (1, P), (2, P), (0, 3 * P)],
          [(0, 0), (0, P), (1, 0), (1, P)],
          [(1, P * r) for r in range(PACK)]]


def tile_rows_sink_gate_kernel(tc, qT, kT, t, v, sink, og, out):
    nc = tc.nc

    with ExitStack() as ctx:
        sb = ctx.enter_context(tc.tile_pool(name="sb", bufs=1))
        ps = ctx.enter_context(tc.psum_pool(name="ps", bufs=1))
        ctx.enter_context(tc.manual_schedule())

        def sbuf(name, shape, dtype):
            return sb.tile(shape, dtype, name=name, align_bytes=64)

        def per_tile(name, shape, dtype):
            return [sbuf("%s%d" % (name, c), shape, dtype) for c in range(TILES)]

        k_raw = sbuf("k_raw", [P, PACK, N], F32)
        k_words = sbuf("k_words", [P, PACK, P, PACK], BF16)
        k_codes = sbuf("k_codes", [P, N], U32)
        k_scales = sbuf("k_scales", [P, N], U8)
        q_raw = [sbuf("q_raw%d" % n, [P, PACK, P * len(tiles)], F32) for n, tiles in enumerate(Q_LOADS)]
        q_words = sbuf("q_words", [P, NQ, PACK], BF16)
        q_codes = sbuf("q_codes", [P, NQ], U32)
        q_scales = sbuf("q_scales", [P, NQ], U8)
        v_raw = [sbuf("v_raw%d" % h, [P, PACK, E], F32) for h in range(H)]
        v_words = sbuf("v_words", [P, H, E, PACK], BF16)
        v_codes = sbuf("v_codes", [P, H, E], U32)
        v_scales = sbuf("v_scales", [P, H, E], U8)
        w_rows = sbuf("w_rows", [P, PACK, H * NQ], BF16)
        w_words = sbuf("w_words", [P, H * NQ, PACK], BF16)
        w_codes = sbuf("w_codes", [P, H * NQ], U32)
        w_scales = sbuf("w_scales", [P, H * NQ], U8)

        t_sb = sbuf("t_sb", [P, PACK], F32)
        t_mantissa = sbuf("t_mantissa", [P, PACK], I32)
        t_exponent = sbuf("t_exponent", [P, PACK], I32)
        half_sign = sbuf("half_sign", [P, PACK], I32)
        shifted = sbuf("shifted", [P, PACK], F32)
        inv_shifted = sbuf("inv_shifted", [P, PACK], F32)
        z = sbuf("z", [P, PACK], F32)
        factors = sbuf("factors", [P, PACK, STEPS], F32)
        terms = sbuf("terms", [P, PACK, STEPS], F32)
        sums = sbuf("sums", [P, PACK, STEPS], F32)
        ln_t = sums[:, :, STEPS - 1]
        sink_rows = sbuf("sink_rows", [P, QUAD], F32)
        sink_cols = sbuf("sink_cols", [P, QUAD], F32)
        sinks = sink_cols[:, 0:QUAD:SINK_STEP]
        og_sb = sbuf("og_sb", [P, H * TILES, E], F32)
        tanh_og = sbuf("tanh_og", [P, H * TILES, E], F32)
        gate = sbuf("gate", [P, H * TILES, E], F32)
        denom = sbuf("denom", [P, H * TILES], F32)
        inverse = sbuf("inverse", [P, H * TILES], F32)
        result = sbuf("result", [P, H * TILES, E], F32)

        score_banks = [[ps.tile([P, N], F32, name="score%d_%d" % (h, b)) for b in range(SCORE_BANKS[h])]
                       for h in range(H)]
        y_banks = [ps.tile([P, len(turns), E], F32, name="y%d" % b) for b, turns in enumerate(Y_BANKS)]

        def half_y(n0, n1):
            b = [n0 in turns for turns in Y_BANKS].index(True)
            m = Y_BANKS[b].index(n0)
            return y_banks[b][:, m:m + n1 - n0]

        def of_turns(view, n0, n1):
            at = [TILES * h + c for h, c in TURNS[n0:n1]]
            return view[:, at[0]:at[-1] + 1:(at[1] - at[0] if len(at) > 1 else 1)]

        def quantise(codes, scales, words):
            nc.vector.quantize_mx(out=codes.bitcast(FP8X4), scales=scales, in_=words.rearrange("p n j -> p (n j)"))

        def interleave(words, rows, copy, run=RUN):
            copy(out=words.rearrange("p (a b) j -> p a j b", b=run), in_=rows.rearrange("p j (a b) -> p a j b", b=run))

        def scalar_copy(out, in_):
            nc.scalar.activation(out=out, in_=in_, func=ACT.Copy)

        def deal_keys(copy, r0, r1, s0=0, s1=P):
            copy(out=k_words[:, r0:r1, s0:s1].rearrange("p r s j -> p s j r"),
                 in_=k_raw[:].rearrange("p j (s r) -> p s j r", r=PACK)[:, s0:s1, :, r0:r1])

        def quantise_keys(r0, r1):
            quantise(k_codes[:, P * r0:P * r1], k_scales[:, P * r0:P * r1],
                     k_words[:, r0:r1].rearrange("p r s j -> p (r s) j"))

        def interleave_queries(n0, n1, copy=nc.vector.tensor_copy):
            n = [n0 // P in tiles for tiles in Q_LOADS].index(True)
            first = P * Q_LOADS[n][0]
            interleave(q_words[:, n0:n1], q_raw[n][:, :, n0 - first:n1 - first], copy, LONG_RUN)

        def quantise_queries(c0, c1):
            quantise(q_codes[:, P * c0:P * c1], q_scales[:, P * c0:P * c1], q_words[:, P * c0:P * c1])

        def quantise_values(h0, h1):
            quantise(v_codes[:, h0:h1].rearrange("p h e -> p (h e)"), v_scales[:, h0:h1].rearrange("p h e -> p (h e)"),
                     v_words[:, h0:h1].rearrange("p h e r -> p (h e) r"))

        def sign_values(h, e0=0, e1=E):
            factor = half_sign[:].bitcast(F32).unsqueeze(1).unsqueeze(3).to_broadcast([P, (e1 - e0) // LONG_RUN, PACK, LONG_RUN])
            nc.vector.tensor_tensor(out=v_words[:, h, e0:e1].rearrange("p (a b) r -> p a r b", b=LONG_RUN),
                                    in0=v_raw[h][:, :, e0:e1].rearrange("p r (a b) -> p a r b", b=LONG_RUN), in1=factor,
                                    op=ALU.mult)

        def score(n, r):
            h, c = TURNS[n]
            rows, keys, queries = slice(ROWS * h, ROWS * (h + 1)), slice(P * r, P * (r + 1)), slice(P * c, P * (c + 1))
            bank, first = PLACES[n][r]
            nc.tensor.matmul_mx(out=score_banks[h][bank][:, first:first + P],
                                lhsT=k_codes[rows, keys].bitcast(FP8X4), lhsT_scale=k_scales[rows, keys],
                                rhs=q_codes[rows, queries].bitcast(FP8X4), rhs_scale=q_scales[rows, queries],
                                start=True, stop=True)

        def scores(n):
            for r in range(PACK):
                score(n, r)

        def weight(n, r, turns=1):
            bank, first = PLACES[n][r]
            nc.scalar.activation(out=w_rows[:, r, P * n:P * (n + turns)],
                                 in_=score_banks[TURNS[n][0]][bank][:, first:first + P * turns],
                                 func=ACT.Exp, bias=ln_t[:, r:r + 1])

        def weights(n, turns=1):
            for r in range(PACK):
                weight(n, r, turns)

        def interleave_weights(n0, n1, copy=nc.vector.tensor_copy):
            interleave(w_words[:, n0:n1], w_rows[:, :, n0:n1], copy)

        def quantise_weights(n0, n1):
            quantise(w_codes[:, P * n0:P * n1], w_scales[:, P * n0:P * n1], w_words[:, P * n0:P * n1])

        def values(n0, n1):
            for n in range(n0, n1):
                h, cols = TURNS[n][0], slice(P * n, P * (n + 1))
                nc.tensor.matmul_mx(out=half_y(n, n + 1)[:, 0],
                                    lhsT=w_codes[:, cols].bitcast(FP8X4), lhsT_scale=w_scales[:, cols],
                                    rhs=v_codes[:, h].bitcast(FP8X4), rhs_scale=v_scales[:, h],
                                    start=True, stop=True)

        def add_sinks(n0, n1):
            nc.vector.scalar_tensor_tensor(out=denom[:, n0:n1], in0=half_y(n0, n1)[:, :, E - 1], scalar=2.0,
                                           in1=of_turns(sinks, n0, n1), op0=ALU.mult, op1=ALU.add)

        def add_middle_sinks():
            nc.vector.scalar_tensor_tensor(out=denom[:, 2:6].rearrange("p (h c) -> p h c", h=H),
                                           in0=half_y(2, 6)[:, :, E - 1].rearrange("p (h c) -> p h c", h=H),
                                           scalar=2.0, in1=sinks.rearrange("p (h c) -> p h c", h=H)[:, :, 1:3],
                                           op0=ALU.mult, op1=ALU.add)

        def add_sink_on_scalar(n):
            nc.scalar.activation(out=denom[:, n:n + 1], in_=half_y(n, n + 1)[:, 0, E - 1:E], func=ACT.Identity,
                                 scale=2.0, bias=of_turns(sinks, n, n + 1))

        def invert(n0, n1):
            nc.vector.reciprocal(out=inverse[:, n0:n1], in_=denom[:, n0:n1])

        def tanh_gate(n0, n1):
            nc.scalar.activation(out=tanh_og[:, n0:n1], in_=of_turns(og_sb, n0, n1), func=ACT.Tanh, scale=0.5)

        def one_plus_on_scalar(n0, n1):
            nc.scalar.activation(out=gate[:, n0:n1], in_=tanh_og[:, n0:n1], func=ACT.Copy, bias=1.0)

        def one_plus_on_vector(n0, n1):
            nc.vector.tensor_scalar(out=gate[:, n0:n1], in0=tanh_og[:, n0:n1], scalar1=1.0, scalar2=None, op0=ALU.add)

        def one_plus_on_gpsimd(n0, n1):
            nc.gpsimd.tensor_scalar(out=gate[:, n0:n1], in0=tanh_og[:, n0:n1], scalar1=1.0, scalar2=1.0,
                                    op0=ALU.mult, op1=ALU.add)

        def finish(n):
            nc.vector.scalar_tensor_tensor(out=result[:, n], in0=half_y(n, n + 1)[:, 0], scalar=inverse[:, n:n + 1],
                                           in1=gate[:, n], op0=ALU.mult, op1=ALU.mult)

        def gate_y(n0, n1):
            nc.vector.scalar_tensor_tensor(out=gate[:, n0:n1], in0=tanh_og[:, n0:n1], scalar=1.0, in1=half_y(n0, n1),
                                           op0=ALU.add, op1=ALU.mult)

        def scale_on_scalar(n):
            nc.scalar.activation(out=result[:, n], in_=gate[:, n], func=ACT.Copy, scale=inverse[:, n:n + 1])

        def scale_on_vector(n):
            nc.vector.tensor_scalar(out=result[:, n], in0=gate[:, n], scalar1=inverse[:, n:n + 1],
                                    scalar2=None, op0=ALU.mult)

        def store(n0, n1):
            nc.sync.dma_start(out=of_turns(out.rearrange("h (c p) e -> p (h c) e", p=P), n0, n1),
                              in_=result[:, n0:n1])

        nc.vector.memset(sink_rows[:], 0.0)
        nc.vector.memset(factors[:, :, 0:1], 0.0)
        for step, odd in enumerate(ODD):
            nc.vector.memset(terms[:, :, step:step + 1], float(COMMON // odd))
        q_hbm = qT.rearrange("h (p j) n -> (h p) j n", j=PACK)

        def load_queries(n):
            tiles = Q_LOADS[n]
            nc.sync.dma_start(out=q_raw[n][:], in_=q_hbm[:, :, P * tiles[0]:P * (tiles[-1] + 1)])

        def load_values(h):
            nc.sync.dma_start(out=v_raw[h][:], in_=v[h].rearrange("(s r) e -> s r e", r=PACK))

        def load_gates(h):
            nc.sync.dma_start(out=og_sb[:, TILES * h:TILES * (h + 1)], in_=og[h].rearrange("(c p) e -> p c e", p=P))

        def load_sinks():
            nc.sync.dma_start(out=sink_rows[0:P:SINK_STEP, :],
                              in_=sink.rearrange("h (c a x) o -> a (h c) (x o)", a=P // QUAD, x=QUAD))

        def turn_sinks():
            nc.vector.transpose(out=sink_cols[:], in_=sink_rows[:])

        nc.sync.dma_start(out=t_sb[:], in_=t.rearrange("(s r) o -> s (r o)", r=PACK))
        nc.sync.dma_start(out=k_raw[:], in_=kT.rearrange("h (p j) n -> (h p) j n", j=PACK))
        load_queries(0)
        load_queries(1)
        load_queries(2)
        load_sinks()
        load_values(0)
        load_queries(3)
        load_values(1)
        load_gates(0)
        load_gates(1)

        t_bits = t_sb[:].bitcast(I32)
        nc.vector.tensor_scalar(out=t_mantissa[:], in0=t_bits, scalar1=MANTISSA, scalar2=ONE,
                                op0=ALU.bitwise_and, op1=ALU.bitwise_or)
        nc.vector.tensor_scalar(out=t_exponent[:], in0=t_bits, scalar1=MANTISSA_BITS, scalar2=EXPONENT,
                                op0=ALU.logical_shift_right, op1=ALU.bitwise_and)
        nc.vector.tensor_scalar(out=half_sign[:], in0=t_bits, scalar1=SIGN, scalar2=HALF,
                                op0=ALU.bitwise_and, op1=ALU.bitwise_or)
        nc.vector.tensor_scalar(out=shifted[:], in0=t_mantissa[:].bitcast(F32), scalar1=SQRT2, scalar2=None,
                                op0=ALU.add)
        nc.vector.tensor_scalar(out=terms[:, :, STEPS - 1], in0=t_exponent[:], scalar1=0.5 - EXPONENT_BIAS,
                                scalar2=math.log(2.0), op0=ALU.add, op1=ALU.mult)
        nc.vector.reciprocal(out=inv_shifted[:], in_=shifted[:])
        nc.vector.tensor_scalar(out=z[:], in0=inv_shifted[:], scalar1=-2.0 * SQRT2, scalar2=1.0,
                                op0=ALU.mult, op1=ALU.add)
        nc.vector.tensor_scalar(out=factors[:, :, STEPS - 1], in0=inv_shifted[:], scalar1=-4.0 * SQRT2 / COMMON,
                                scalar2=2.0 / COMMON, op0=ALU.mult, op1=ALU.add)
        z_wide = z[:].unsqueeze(2).to_broadcast([P, PACK, len(ODD) - 1])
        nc.vector.tensor_tensor(out=factors[:, :, 1:STEPS - 1], in0=z_wide, in1=z_wide, op=ALU.mult)
        nc.vector.tensor_tensor_scan(out=sums[:].rearrange("p r k -> p (r k)"),
                                     data0=factors[:].rearrange("p r k -> p (r k)"),
                                     data1=terms[:].rearrange("p r k -> p (r k)"),
                                     initial=0.0, op0=ALU.mult, op1=ALU.add)


        def second_scores(r):
            for n in (2, 4, 3, 5):
                score(n, r)

        deal_keys(nc.vector.tensor_copy, 0, 2)
        deal_keys(scalar_copy, 2, 4)
        interleave_queries(0, P)
        quantise_keys(0, 1)
        quantise_queries(0, 1)
        quantise_keys(1, 2)
        quantise_keys(2, 4)
        interleave_queries(P, 2 * P, copy=nc.scalar.copy)
        interleave_queries(2 * P, 3 * P)
        quantise_queries(1, 2)
        turn_sinks()
        quantise_queries(2, 3)
        for r in range(PACK):
            score(1, r)
            score(0, r)
        for n in (1, 0):
            for r in (0, 1):
                weight(n, r)
        second_scores(0)
        second_scores(1)
        for n in (1, 0):
            for r in (2, 3):
                weight(n, r)
        second_scores(2)
        for n in (2, 4):
            weight(n, 0, 2)
        second_scores(3)
        for n in (2, 4):
            weight(n, 1, 2)
        sign_values(0)
        interleave_weights(P, 2 * P)
        interleave_queries(3 * P, 4 * P)
        interleave_weights(0, P)
        quantise_queries(3, 4)
        sign_values(1)
        quantise_weights(0, 2)
        for r in (0, 1):
            for n in (6, 7):
                score(n, r)
        weight(2, 2, 2)
        for r in (2, 3):
            for n in (7, 6):
                score(n, r)
        weight(2, 3, 2)
        for r in (2, 3):
            weight(4, r, 2)
        quantise_values(0, 2)
        values(0, 2)
        interleave_weights(2 * P, 4 * P)
        interleave_weights(4 * P, 6 * P)
        quantise_weights(2, 4)
        values(2, 4)
        weights(6)
        weights(7)
        tanh_gate(0, 2)
        interleave_weights(7 * P, 8 * P, copy=nc.scalar.copy)
        for n in range(2, 8, 2):
            tanh_gate(n, n + 2)
        interleave_weights(6 * P, 7 * P)
        quantise_weights(4, 6)
        values(4, 6)
        add_sinks(0, 2)
        quantise_weights(6, 7)
        gate_y(0, 2)
        invert(0, 2)
        quantise_weights(7, 8)
        values(6, 8)
        add_middle_sinks()
        gate_y(2, 4)
        invert(2, 6)
        gate_y(4, 6)
        add_sinks(6, 8)
        gate_y(6, 8)
        invert(6, 8)
        for n in range(0, 6, 2):
            scale_on_scalar(n)
            scale_on_scalar(n + 1)
            store(n, n + 2)
        scale_on_vector(6)
        scale_on_vector(7)
        store(6, 8)
